import numpy as np
import ml_dtypes


def mxq(x, axis, fmt="e4m3"):
    dtype, down = {"e4m3": (ml_dtypes.float8_e4m3fn, 7), "e5m2": (ml_dtypes.float8_e5m2, 14)}[fmt]
    v = np.moveaxis(np.asarray(x, np.float32).astype(ml_dtypes.bfloat16).astype(np.float64), axis, -1)
    blocks = v.reshape(v.shape[:-1] + (-1, 32))
    amax = np.abs(blocks).max(-1, keepdims=True)
    byte = np.maximum(np.where(amax > 0, np.frexp(amax)[1] - 1 + 127, 0) - down, 1)
    scale = np.exp2(byte - 127.0)
    codes = (blocks / scale).astype(np.float32).astype(dtype).astype(np.float64)
    return np.moveaxis((codes * scale).reshape(v.shape), -1, axis)


WIDE = False


def mx_kscale(k):
    if not WIDE:
        return np.ones(k)
    levels = np.array([18, -18])
    if k % 512:
        return np.exp2(np.random.permutation(np.resize(levels, k // 32))).repeat(32)
    a = np.empty((k // 512, 16))
    for p in range(k // 512):
        a[p, :8] = np.random.permutation(np.resize(levels, 8))
        for g in range(8):
            far = levels[np.abs(levels - a[p, g]) >= 10]
            a[p, g + 8] = far[np.random.randint(len(far))]
    return np.exp2(a.ravel()).repeat(32)


def f64(x):
    return np.asarray(x).astype(np.float64)


def striped(idx):
    return np.tile(np.asarray(idx).reshape(-1, 16).T, (8, 1)).astype(np.uint16)


def unstriped(offs):
    return offs[:16].T.reshape(-1).astype(np.int64)


def setup_inputs():
    n = np.random.standard_normal
    uni = np.random.uniform
    idx = np.random.permutation(2048)[:512]
    pos = np.random.randint(0, 1024, 512)
    ang = np.arange(1024)[None, :] * np.power(10000.0, -np.arange(512) / 512.0)[:, None]
    f_r = mx_kscale(512)
    return {
        "q1": (n((512, 512)) * f_r[None, :]).astype(np.float32),
        "q2": (n((512, 512)) * f_r[None, :]).astype(np.float32),
        "G": (n((512, 512)) / np.sqrt(512) / f_r[:, None]).astype(np.float32),
        "cs": (np.cos(ang)).astype(np.float32),
        "sn": (np.sin(ang)).astype(np.float32),
        "offs": striped(idx),
        "poffs": striped(pos),
    }


def reference(q1, q2, G, cs, sn, offs, poffs):
    idx = unstriped(offs)
    pos = unstriped(poffs)
    c = f64(cs)[:, pos]
    s = f64(sn)[:, pos]
    q_G = mxq(f64(G), 0, "e5m2")
    a = mxq(f64(q1), 1, "e4m3") @ q_G
    b = mxq(f64(q2), 1, "e4m3") @ q_G
    d1 = c * a + s * b
    d2 = c * b - s * a
    out_0 = np.zeros((512, 2048))
    out_0[:, idx] = d1
    out_1 = np.zeros((512, 2048))
    out_1[:, idx] = d2
    return out_0, out_1

@@ -1,0 +1,140 @@
+from contextlib import ExitStack
+
+import concourse.mybir as mybir
+from concourse.masks import make_identity
+
+F32 = mybir.dt.float32
+BF16 = mybir.dt.bfloat16
+U32 = mybir.dt.uint32
+I32 = mybir.dt.int32
+U16 = mybir.dt.uint16
+U8 = mybir.dt.uint8
+E4M3 = mybir.dt.float8_e4m3fn_x4
+E5M2 = mybir.dt.float8_e5m2_x4
+MULT = mybir.AluOpType.mult
+ADD = mybir.AluOpType.add
+SUBTRACT = mybir.AluOpType.subtract
+
+P = 128
+PACK = 4
+FEATURES = 512
+QUERIES = 512
+SLOTS = 512
+POSITIONS = 1024
+TOKENS = 2048
+BLOCKS = FEATURES // P
+G_PARTS = 2
+G_COLS = SLOTS // G_PARTS
+WINDOWS = 3
+
+FLOPS = 2 * 2 * FEATURES * QUERIES * SLOTS
+
+
+def tile_attend_grope_kernel(tc, q1, q2, G, cs, sn, offs, poffs, out_0, out_1):
+    nc = tc.nc
+    with ExitStack() as ctx:
+        keep = ctx.enter_context(tc.tile_pool(name="keep", bufs=1))
+        work = ctx.enter_context(tc.tile_pool(name="work", bufs=2))
+        psum = ctx.enter_context(tc.psum_pool(name="psum", bufs=1))
+
+        token_list = keep.tile([P, SLOTS // 16], U16, name="token_list")
+        position_list = keep.tile([P, SLOTS // 16], U16, name="position_list")
+        q_raw = [[keep.tile([P, QUERIES], F32, name="q_raw%d_%d" % (h, b)) for h in range(2)] for b in range(BLOCKS)]
+        g_raw = [keep.tile([P, PACK, G_COLS], F32, name="g_raw%d" % u) for u in range(G_PARTS)]
+        cos_table = [keep.tile([P, POSITIONS], F32, name="cos_table%d" % b) for b in range(BLOCKS)]
+        sin_table = [keep.tile([P, POSITIONS], F32, name="sin_table%d" % b) for b in range(BLOCKS)]
+        windows = [keep.tile([P, TOKENS], F32, name="window%d" % w) for w in range(WINDOWS)]
+        identity = keep.tile([P, P], F32, name="identity")
+        g_codes = keep.tile([P, SLOTS], U32, name="g_codes", align_bytes=64)
+        g_scales = keep.tile([P, SLOTS], U8, name="g_scales", align_bytes=64)
+
+        def load_q(b):
+            rows = slice(b * P, (b + 1) * P)
+            nc.sync.dma_start(q_raw[b][0][:], q1[rows, :])
+            nc.sync.dma_start(q_raw[b][1][:], q2[rows, :])
+
+        def load_tables(b):
+            rows = slice(b * P, (b + 1) * P)
+            nc.sync.dma_start(cos_table[b][:], cs[rows, :])
+            nc.sync.dma_start(sin_table[b][:], sn[rows, :])
+
+        load_q(0)
+        g_rows = G.rearrange("(p t) i -> p t i", t=PACK)
+        for u in range(G_PARTS):
+            nc.sync.dma_start(g_raw[u][:], g_rows[:, :, u * G_COLS : (u + 1) * G_COLS])
+        nc.sync.dma_start(position_list[:], poffs)
+        load_tables(0)
+        nc.sync.dma_start(token_list[:], offs)
+        for b in range(1, BLOCKS):
+            load_tables(b)
+            load_q(b)
+
+        make_identity(nc, identity[:])
+        for window in windows:
+            nc.vector.memset(window[:].bitcast(I32), 0)
+
+        g_grouped = [keep.tile([P, G_COLS, PACK], BF16, name="g_grouped%d" % u, align_bytes=64) for u in range(G_PARTS)]
+        for u in range(G_PARTS):
+            nc.vector.tensor_copy(
+                g_grouped[u][:].rearrange("p (c i) t -> p c t i", i=4),
+                g_raw[u][:].rearrange("p t (c i) -> p c t i", i=4),
+            )
+        for u in range(G_PARTS):
+            cols = slice(u * G_COLS, (u + 1) * G_COLS)
+            nc.vector.quantize_mx(
+                out=g_codes[:, cols].bitcast(E5M2),
+                scales=g_scales[:, cols],
+                in_=g_grouped[u][:].rearrange("p c t -> p (c t)"),
+            )
+
+        for b in range(BLOCKS):
+            rows = slice(b * P, (b + 1) * P)
+            q_codes = keep.tile([P, 2 * P], U32, name="q_codes", tag="look2" if b == 0 else "q_codes", align_bytes=64)
+            q_scales = keep.tile([P, 2 * P], U8, name="q_scales", tag="look3" if b == 0 else "q_scales", align_bytes=64)
+            for h in range(2):
+                cols = slice(h * P, (h + 1) * P)
+                turned = psum.tile([P, PACK, P], F32, name="turned%d" % h, tag="bank%d" % h)
+                for t in range(PACK):
+                    nc.tensor.transpose(turned[:, t, :], q_raw[b][h][:, t::PACK], identity[:])
+                q_grouped = keep.tile(
+                    [P, P, PACK], BF16, name="q_grouped", tag=("look%d" if b == 0 else "q_grouped%d") % h, align_bytes=64
+                )
+                nc.scalar.copy(q_grouped[:], turned[:].rearrange("p t f -> p f t"))
+                nc.vector.quantize_mx(
+                    out=q_codes[:, cols].bitcast(E4M3),
+                    scales=q_scales[:, cols],
+                    in_=q_grouped[:].rearrange("p f t -> p (f t)"),
+                )
+            sums = []
+            for h in range(2):
+                cols = slice(h * P, (h + 1) * P)
+                acc = psum.tile([P, SLOTS], F32, name="acc%d" % h, tag="bank%d" % h)
+                nc.tensor.matmul_mx(
+                    out=acc[:],
+                    lhsT=q_codes[:, cols].bitcast(E4M3),
+                    lhsT_scale=q_scales[:, cols],
+                    rhs=g_codes[:].bitcast(E5M2),
+                    rhs_scale=g_scales[:],
+                    start=True,
+                    stop=True,
+                )
+                held = work.tile([P, SLOTS], F32, name="held%d" % h)
+                nc.scalar.copy(held[:], acc[:])
+                sums.append(held)
+            a, bb = sums
+
+            c = keep.tile([P, SLOTS], F32, name="c", tag="look%d" % (2 * (b % 2)), align_bytes=64)
+            s = keep.tile([P, SLOTS], F32, name="s", tag="look%d" % (2 * (b % 2) + 1), align_bytes=64)
+            nc.vector.tensor_copy(c[:], cos_table[b][:].indirect(position_list[:]))
+            nc.vector.tensor_copy(s[:], sin_table[b][:].indirect(position_list[:]))
+
+            for h, (x, y, op, out) in enumerate(((a, bb, ADD, out_0), (bb, a, SUBTRACT, out_1))):
+                cos_term = work.tile([P, SLOTS], F32, name="cos_term")
+                sin_term = work.tile([P, SLOTS], F32, name="sin_term")
+                gradient = work.tile([P, SLOTS], F32, name="gradient", bufs=3)
+                nc.gpsimd.tensor_tensor(cos_term[:], x[:], c[:], MULT)
+                nc.gpsimd.tensor_tensor(sin_term[:], y[:], s[:], MULT)
+                nc.gpsimd.tensor_tensor(gradient[:], cos_term[:], sin_term[:], op)
+                window = windows[(2 * b + h) % WINDOWS]
+                nc.vector.tensor_copy(window[:].indirect(token_list[:]), gradient[:])
+                nc.sync.dma_start(out[rows, :], window[:])

@@ -23,8 +23,6 @@ SLOTS = 512
 POSITIONS = 1024
 TOKENS = 2048
 BLOCKS = FEATURES // P
-G_PARTS = 2
-G_COLS = SLOTS // G_PARTS
 WINDOWS = 3
 
 FLOPS = 2 * 2 * FEATURES * QUERIES * SLOTS
@@ -34,15 +32,14 @@ def tile_attend_grope_kernel(tc, q1, q2, G, cs, sn, offs, poffs, out_0, out_1):
     nc = tc.nc
     with ExitStack() as ctx:
         keep = ctx.enter_context(tc.tile_pool(name="keep", bufs=1))
-        work = ctx.enter_context(tc.tile_pool(name="work", bufs=2))
         psum = ctx.enter_context(tc.psum_pool(name="psum", bufs=1))
 
         token_list = keep.tile([P, SLOTS // 16], U16, name="token_list")
         position_list = keep.tile([P, SLOTS // 16], U16, name="position_list")
         q_raw = [[keep.tile([P, QUERIES], F32, name="q_raw%d_%d" % (h, b)) for h in range(2)] for b in range(BLOCKS)]
-        g_raw = [keep.tile([P, PACK, G_COLS], F32, name="g_raw%d" % u) for u in range(G_PARTS)]
+        g_raw = keep.tile([P, PACK, SLOTS], F32, name="g_raw")
         cos_table = [keep.tile([P, POSITIONS], F32, name="cos_table%d" % b) for b in range(BLOCKS)]
-        sin_table = [keep.tile([P, POSITIONS], F32, name="sin_table%d" % b) for b in range(BLOCKS)]
+        sin_table = [keep.tile([P, POSITIONS], F32, name="sin_table%d" % b, align_bytes=64) for b in range(BLOCKS)]
         windows = [keep.tile([P, TOKENS], F32, name="window%d" % w) for w in range(WINDOWS)]
         identity = keep.tile([P, P], F32, name="identity")
         g_codes = keep.tile([P, SLOTS], U32, name="g_codes", align_bytes=64)
@@ -58,83 +55,113 @@ def tile_attend_grope_kernel(tc, q1, q2, G, cs, sn, offs, poffs, out_0, out_1):
             nc.sync.dma_start(cos_table[b][:], cs[rows, :])
             nc.sync.dma_start(sin_table[b][:], sn[rows, :])
 
+        nc.sync.dma_start(g_raw[:], G.rearrange("(p t) i -> p t i", t=PACK))
         load_q(0)
-        g_rows = G.rearrange("(p t) i -> p t i", t=PACK)
-        for u in range(G_PARTS):
-            nc.sync.dma_start(g_raw[u][:], g_rows[:, :, u * G_COLS : (u + 1) * G_COLS])
         nc.sync.dma_start(position_list[:], poffs)
         load_tables(0)
         nc.sync.dma_start(token_list[:], offs)
+        load_tables(1)
         for b in range(1, BLOCKS):
-            load_tables(b)
             load_q(b)
+        for b in range(2, BLOCKS):
+            load_tables(b)
 
         make_identity(nc, identity[:])
         for window in windows:
             nc.vector.memset(window[:].bitcast(I32), 0)
 
-        g_grouped = [keep.tile([P, G_COLS, PACK], BF16, name="g_grouped%d" % u, align_bytes=64) for u in range(G_PARTS)]
-        for u in range(G_PARTS):
-            nc.vector.tensor_copy(
-                g_grouped[u][:].rearrange("p (c i) t -> p c t i", i=4),
-                g_raw[u][:].rearrange("p t (c i) -> p c t i", i=4),
-            )
-        for u in range(G_PARTS):
-            cols = slice(u * G_COLS, (u + 1) * G_COLS)
-            nc.vector.quantize_mx(
-                out=g_codes[:, cols].bitcast(E5M2),
-                scales=g_scales[:, cols],
-                in_=g_grouped[u][:].rearrange("p c t -> p (c t)"),
-            )
-
-        for b in range(BLOCKS):
-            rows = slice(b * P, (b + 1) * P)
-            q_codes = keep.tile([P, 2 * P], U32, name="q_codes", tag="look2" if b == 0 else "q_codes", align_bytes=64)
-            q_scales = keep.tile([P, 2 * P], U8, name="q_scales", tag="look3" if b == 0 else "q_scales", align_bytes=64)
+        def turn_q(b, grouped, rounded_tag):
+            rounded = keep.tile([P, 2, QUERIES], BF16, name="q_rounded", tag=rounded_tag, align_bytes=64)
             for h in range(2):
-                cols = slice(h * P, (h + 1) * P)
-                turned = psum.tile([P, PACK, P], F32, name="turned%d" % h, tag="bank%d" % h)
-                for t in range(PACK):
-                    nc.tensor.transpose(turned[:, t, :], q_raw[b][h][:, t::PACK], identity[:])
-                q_grouped = keep.tile(
-                    [P, P, PACK], BF16, name="q_grouped", tag=("look%d" if b == 0 else "q_grouped%d") % h, align_bytes=64
+                nc.scalar.copy(
+                    rounded[:, h, :].rearrange("f (u p e) -> f u p e", u=2, e=2),
+                    q_raw[b][h][:].rearrange("f (p u e) -> f u p e", u=2, e=2),
                 )
-                nc.scalar.copy(q_grouped[:], turned[:].rearrange("p t f -> p f t"))
-                nc.vector.quantize_mx(
-                    out=q_codes[:, cols].bitcast(E4M3),
-                    scales=q_scales[:, cols],
-                    in_=q_grouped[:].rearrange("p f t -> p (f t)"),
+                words = rounded[:, h, :].bitcast(F32)
+                turned = psum.tile([P, 2, P], F32, name="turned", tag="bank%d" % h)
+                for u in range(2):
+                    nc.tensor.transpose(turned[:, u, :], words[:, u * P : (u + 1) * P], identity[:])
+                nc.scalar.copy(
+                    grouped[:, h * QUERIES : (h + 1) * QUERIES].bitcast(F32).rearrange("p (f u) -> p f u", u=2),
+                    turned[:].rearrange("p u f -> p f u"),
                 )
+
+        def quantise_q(calls, codes_tag, rounded_tags):
+            blocks = [b for call in calls for b in call]
+            codes = keep.tile([P, 2 * P * len(blocks)], U32, name="q_codes", tag=codes_tag, align_bytes=64)
+            scales = keep.tile([P, 2 * P * len(blocks)], U8, name="q_scales", tag="q_scales%d" % blocks[0], align_bytes=64)
+            for call in calls:
+                width = 2 * QUERIES
+                grouped = keep.tile(
+                    [P, width * len(call)], BF16, name="q_grouped", tag="grouped%d" % call[0], align_bytes=64
+                )
+                for j, b in enumerate(call):
+                    turn_q(b, grouped[:, j * width : (j + 1) * width], rounded_tags[b % len(rounded_tags)])
+                first = 2 * P * blocks.index(call[0])
+                cols = slice(first, first + 2 * P * len(call))
+                nc.vector.quantize_mx(out=codes[:, cols].bitcast(E4M3), scales=scales[:, cols], in_=grouped[:])
+            return {b: (codes, scales, 2 * j * P) for j, b in enumerate(blocks)}
+
+        def multiply(b):
+            codes, scales, first = quantised[b]
             sums = []
             for h in range(2):
-                cols = slice(h * P, (h + 1) * P)
-                acc = psum.tile([P, SLOTS], F32, name="acc%d" % h, tag="bank%d" % h)
+                cols = slice(first + h * P, first + (h + 1) * P)
+                acc = psum.tile([P, SLOTS], F32, name="acc", tag="bank%d" % h)
                 nc.tensor.matmul_mx(
                     out=acc[:],
-                    lhsT=q_codes[:, cols].bitcast(E4M3),
-                    lhsT_scale=q_scales[:, cols],
+                    lhsT=codes[:, cols].bitcast(E4M3),
+                    lhsT_scale=scales[:, cols],
                     rhs=g_codes[:].bitcast(E5M2),
                     rhs_scale=g_scales[:],
                     start=True,
                     stop=True,
                 )
-                held = work.tile([P, SLOTS], F32, name="held%d" % h)
+                held = keep.tile([P, SLOTS], F32, name="held%d_%d" % (b, h))
                 nc.scalar.copy(held[:], acc[:])
                 sums.append(held)
-            a, bb = sums
+            return sums
 
-            c = keep.tile([P, SLOTS], F32, name="c", tag="look%d" % (2 * (b % 2)), align_bytes=64)
-            s = keep.tile([P, SLOTS], F32, name="s", tag="look%d" % (2 * (b % 2) + 1), align_bytes=64)
-            nc.vector.tensor_copy(c[:], cos_table[b][:].indirect(position_list[:]))
-            nc.vector.tensor_copy(s[:], sin_table[b][:].indirect(position_list[:]))
+        def look_up(b, pair):
+            nc.vector.tensor_copy(pair[:, 0, :], cos_table[b][:].indirect(position_list[:]))
+            nc.vector.tensor_copy(pair[:, 1, :], sin_table[b][:].indirect(position_list[:]))
+            return pair[:, 0, :], pair[:, 1, :]
 
-            for h, (x, y, op, out) in enumerate(((a, bb, ADD, out_0), (bb, a, SUBTRACT, out_1))):
-                cos_term = work.tile([P, SLOTS], F32, name="cos_term")
-                sin_term = work.tile([P, SLOTS], F32, name="sin_term")
-                gradient = work.tile([P, SLOTS], F32, name="gradient", bufs=3)
-                nc.gpsimd.tensor_tensor(cos_term[:], x[:], c[:], MULT)
-                nc.gpsimd.tensor_tensor(sin_term[:], y[:], s[:], MULT)
-                nc.gpsimd.tensor_tensor(gradient[:], cos_term[:], sin_term[:], op)
-                window = windows[(2 * b + h) % WINDOWS]
-                nc.vector.tensor_copy(window[:].indirect(token_list[:]), gradient[:])
-                nc.sync.dma_start(out[rows, :], window[:])
+        def columns(n, tag):
+            return keep.tile([P, n, SLOTS], F32, name="columns", tag=tag, align_bytes=64)
+
+        def rotate(b, h, gradient):
+            c, s = angles[b]
+            x, y = sums[b][h], sums[b][1 - h]
+            cos_term = keep.tile([P, SLOTS], F32, name="cos_term", tag="cos_term%d" % (h if b else 1))
+            sin_term = keep.tile([P, SLOTS], F32, name="sin_term", tag="sin_term%d" % (h if b else 1))
+            nc.gpsimd.tensor_tensor(cos_term[:], x[:], c, MULT)
+            nc.gpsimd.tensor_tensor(sin_term[:], y[:], s, MULT)
+            nc.gpsimd.tensor_tensor(gradient, cos_term[:], sin_term[:], (ADD, SUBTRACT)[h])
+            window = windows[(2 * b + h) % WINDOWS]
+            nc.vector.tensor_copy(window[:].indirect(token_list[:]), gradient)
+            nc.sync.dma_start((out_0, out_1)[h][b * P : (b + 1) * P, :], window[:])
+
+        g_grouped = keep.tile([P, SLOTS, PACK], BF16, name="g_grouped", align_bytes=64)
+        nc.vector.tensor_copy(
+            g_grouped[:].rearrange("p (c i) t -> p c t i", i=4), g_raw[:].rearrange("p t (c i) -> p c t i", i=4)
+        )
+        nc.vector.quantize_mx(
+            out=g_codes[:].bitcast(E5M2), scales=g_scales[:], in_=g_grouped[:].rearrange("p c t -> p (c t)")
+        )
+        quantised = quantise_q([[0]], "q_codes0", ["q_rounded0"])
+
+        sums = {0: multiply(0)}
+        angles = {0: look_up(0, columns(2, "grouped0"))}
+        rotate(0, 0, columns(1, "gradient0")[:, 0, :])
+        angles[1] = look_up(1, columns(2, "sin_table0"))
+        quantised.update(quantise_q([[1], [2, 3]], "gradient0", ["q_scales0", "q_codes0"]))
+        angles[2] = look_up(2, columns(2, "grouped2"))
+        rotate(0, 1, columns(1, "gradient0_1")[:, 0, :])
+        for b in range(1, BLOCKS):
+            sums[b] = multiply(b)
+        for b in range(1, BLOCKS):
+            for h in range(2):
+                rotate(b, h, columns(1, "gradient%d_%d" % (b, h))[:, 0, :])
+            if b == 1:
+                angles[3] = look_up(3, columns(2, "sin_table0"))

@@ -13,7 +13,7 @@ E4M3 = mybir.dt.float8_e4m3fn_x4
 E5M2 = mybir.dt.float8_e5m2_x4
 MULT = mybir.AluOpType.mult
 ADD = mybir.AluOpType.add
-SUBTRACT = mybir.AluOpType.subtract
+COPY = mybir.ActivationFunctionType.Copy
 
 P = 128
 PACK = 4
@@ -32,6 +32,7 @@ def tile_attend_grope_kernel(tc, q1, q2, G, cs, sn, offs, poffs, out_0, out_1):
     nc = tc.nc
     with ExitStack() as ctx:
         keep = ctx.enter_context(tc.tile_pool(name="keep", bufs=1))
+        shared = ctx.enter_context(tc.tile_pool(name="shared", bufs=1))
         psum = ctx.enter_context(tc.psum_pool(name="psum", bufs=1))
 
         token_list = keep.tile([P, SLOTS // 16], U16, name="token_list")
@@ -39,7 +40,7 @@ def tile_attend_grope_kernel(tc, q1, q2, G, cs, sn, offs, poffs, out_0, out_1):
         q_raw = [[keep.tile([P, QUERIES], F32, name="q_raw%d_%d" % (h, b)) for h in range(2)] for b in range(BLOCKS)]
         g_raw = keep.tile([P, PACK, SLOTS], F32, name="g_raw")
         cos_table = [keep.tile([P, POSITIONS], F32, name="cos_table%d" % b) for b in range(BLOCKS)]
-        sin_table = [keep.tile([P, POSITIONS], F32, name="sin_table%d" % b, align_bytes=64) for b in range(BLOCKS)]
+        sin_table = [keep.tile([P, POSITIONS], F32, name="sin_table%d" % b) for b in range(BLOCKS)]
         windows = [keep.tile([P, TOKENS], F32, name="window%d" % w) for w in range(WINDOWS)]
         identity = keep.tile([P, P], F32, name="identity")
         g_codes = keep.tile([P, SLOTS], U32, name="g_codes", align_bytes=64)
@@ -61,17 +62,17 @@ def tile_attend_grope_kernel(tc, q1, q2, G, cs, sn, offs, poffs, out_0, out_1):
         load_tables(0)
         nc.sync.dma_start(token_list[:], offs)
         load_tables(1)
-        for b in range(1, BLOCKS):
-            load_q(b)
-        for b in range(2, BLOCKS):
-            load_tables(b)
+        load_q(1)
+        load_q(2)
+        load_q(3)
+        load_tables(2)
+        load_tables(3)
 
         make_identity(nc, identity[:])
         for window in windows:
             nc.vector.memset(window[:].bitcast(I32), 0)
 
-        def turn_q(b, grouped, rounded_tag):
-            rounded = keep.tile([P, 2, QUERIES], BF16, name="q_rounded", tag=rounded_tag, align_bytes=64)
+        def turn_q(b, grouped, rounded):
             for h in range(2):
                 nc.scalar.copy(
                     rounded[:, h, :].rearrange("f (u p e) -> f u p e", u=2, e=2),
@@ -86,28 +87,19 @@ def tile_attend_grope_kernel(tc, q1, q2, G, cs, sn, offs, poffs, out_0, out_1):
                     turned[:].rearrange("p u f -> p f u"),
                 )
 
-        def quantise_q(calls, codes_tag, rounded_tags):
-            blocks = [b for call in calls for b in call]
-            codes = keep.tile([P, 2 * P * len(blocks)], U32, name="q_codes", tag=codes_tag, align_bytes=64)
-            scales = keep.tile([P, 2 * P * len(blocks)], U8, name="q_scales", tag="q_scales%d" % blocks[0], align_bytes=64)
-            for call in calls:
-                width = 2 * QUERIES
-                grouped = keep.tile(
-                    [P, width * len(call)], BF16, name="q_grouped", tag="grouped%d" % call[0], align_bytes=64
-                )
-                for j, b in enumerate(call):
-                    turn_q(b, grouped[:, j * width : (j + 1) * width], rounded_tags[b % len(rounded_tags)])
-                first = 2 * P * blocks.index(call[0])
-                cols = slice(first, first + 2 * P * len(call))
-                nc.vector.quantize_mx(out=codes[:, cols].bitcast(E4M3), scales=scales[:, cols], in_=grouped[:])
+        def quantise_q(blocks, grouped, codes):
+            n = 2 * P * len(blocks)
+            scales = keep.tile([P, n], U8, name="q_scales", tag="q_scales%d" % blocks[0], align_bytes=64)
+            nc.vector.quantize_mx(out=codes[:].bitcast(E4M3), scales=scales[:], in_=grouped[:])
             return {b: (codes, scales, 2 * j * P) for j, b in enumerate(blocks)}
 
         def multiply(b):
             codes, scales, first = quantised[b]
-            sums = []
+            held = keep.tile([P, 3, SLOTS], F32, name="held%d" % b)
+            banks = []
             for h in range(2):
                 cols = slice(first + h * P, first + (h + 1) * P)
-                acc = psum.tile([P, SLOTS], F32, name="acc", tag="bank%d" % h)
+                acc = psum.tile([P, SLOTS], F32, name="acc", tag="bank%d" % h if b == 1 else "acc%d_%d" % (b, h))
                 nc.tensor.matmul_mx(
                     out=acc[:],
                     lhsT=codes[:, cols].bitcast(E4M3),
@@ -117,30 +109,34 @@ def tile_attend_grope_kernel(tc, q1, q2, G, cs, sn, offs, poffs, out_0, out_1):
                     start=True,
                     stop=True,
                 )
-                held = keep.tile([P, SLOTS], F32, name="held%d_%d" % (b, h))
-                nc.scalar.copy(held[:], acc[:])
-                sums.append(held)
-            return sums
+                nc.scalar.copy(held[:, h, :], acc[:])
+                banks.append(acc)
+            return held, banks[0]
+
+        def negate(held, a):
+            nc.scalar.activation(held[:, 2, :], a[:], COPY, scale=-1.0)
 
         def look_up(b, pair):
             nc.vector.tensor_copy(pair[:, 0, :], cos_table[b][:].indirect(position_list[:]))
             nc.vector.tensor_copy(pair[:, 1, :], sin_table[b][:].indirect(position_list[:]))
-            return pair[:, 0, :], pair[:, 1, :]
+            return pair
 
-        def columns(n, tag):
-            return keep.tile([P, n, SLOTS], F32, name="columns", tag=tag, align_bytes=64)
+        def placed(name, shape, dtype, offset):
+            return shared.tile(shape, dtype, name=name, offset=offset, align_bytes=64)
 
-        def rotate(b, h, gradient):
-            c, s = angles[b]
-            x, y = sums[b][h], sums[b][1 - h]
-            cos_term = keep.tile([P, SLOTS], F32, name="cos_term", tag="cos_term%d" % (h if b else 1))
-            sin_term = keep.tile([P, SLOTS], F32, name="sin_term", tag="sin_term%d" % (h if b else 1))
-            nc.gpsimd.tensor_tensor(cos_term[:], x[:], c, MULT)
-            nc.gpsimd.tensor_tensor(sin_term[:], y[:], s, MULT)
-            nc.gpsimd.tensor_tensor(gradient, cos_term[:], sin_term[:], (ADD, SUBTRACT)[h])
+        def put(b, h, terms, gradient):
             window = windows[(2 * b + h) % WINDOWS]
-            nc.vector.tensor_copy(window[:].indirect(token_list[:]), gradient)
+            places = window[:].indirect(token_list[:])
+            if gradient is None:
+                nc.vector.tensor_tensor(places, terms[:, 0, :], terms[:, 1, :], ADD)
+            else:
+                nc.gpsimd.tensor_tensor(gradient, terms[:, 0, :], terms[:, 1, :], ADD)
+                nc.vector.tensor_copy(places, gradient)
             nc.sync.dma_start((out_0, out_1)[h][b * P : (b + 1) * P, :], window[:])
+
+        def rotate(b, h, terms, gradient):
+            nc.gpsimd.tensor_tensor(terms[:], held[b][:, h : h + 2, :], angles[b][:], MULT)
+            put(b, h, terms, gradient)
 
         g_grouped = keep.tile([P, SLOTS, PACK], BF16, name="g_grouped", align_bytes=64)
         nc.vector.tensor_copy(
@@ -149,19 +145,50 @@ def tile_attend_grope_kernel(tc, q1, q2, G, cs, sn, offs, poffs, out_0, out_1):
         nc.vector.quantize_mx(
             out=g_codes[:].bitcast(E5M2), scales=g_scales[:], in_=g_grouped[:].rearrange("p c t -> p (c t)")
         )
-        quantised = quantise_q([[0]], "q_codes0", ["q_rounded0"])
+        KB = 1024
+        pair_shape = [P, 2, SLOTS]
 
-        sums = {0: multiply(0)}
-        angles = {0: look_up(0, columns(2, "grouped0"))}
-        rotate(0, 0, columns(1, "gradient0")[:, 0, :])
-        angles[1] = look_up(1, columns(2, "sin_table0"))
-        quantised.update(quantise_q([[1], [2, 3]], "gradient0", ["q_scales0", "q_codes0"]))
-        angles[2] = look_up(2, columns(2, "grouped2"))
-        rotate(0, 1, columns(1, "gradient0_1")[:, 0, :])
+        def rounded(tag):
+            return keep.tile([P, 2, QUERIES], BF16, name="rounded", tag=tag, align_bytes=64)
+
+        def terms_in(tag):
+            return keep.tile(pair_shape, F32, name="terms", tag=tag)
+
+        grouped = placed("grouped0", [P, 2 * QUERIES], BF16, 0)
+        turn_q(0, grouped, rounded("rounded0"))
+        codes = keep.tile([P, 2 * P], U32, name="q_codes0", align_bytes=64)
+        quantised = quantise_q([0], grouped, codes)
+        first, a = multiply(0)
+        negate(first, a)
+        held = {0: first}
+        angles = {0: look_up(0, placed("angles0", pair_shape, F32, 0))}
+        angles[1] = look_up(1, keep.tile(pair_shape, F32, name="angles1", tag="cos_table0"))
+
+        terms = terms_in("terms0")
+        for n in range(2):
+            nc.gpsimd.tensor_tensor(terms[:, n, :], first[:, n, :], angles[0][:, n, :], MULT)
+        gradient = placed("gradient0", [P, SLOTS], F32, 4 * KB)
+        put(0, 0, terms, gradient[:])
+
+        grouped = keep.tile([P, 2 * QUERIES], BF16, name="grouped1", align_bytes=64)
+        turn_q(1, grouped, rounded("q_codes0"))
+        quantised.update(quantise_q([1], grouped, placed("q_codes1", [P, 2 * P], U32, 4 * KB)))
+        grouped = placed("grouped2", [P, 4 * QUERIES], BF16, 10 * KB)
+        turn_q(2, grouped[:, : 2 * QUERIES], rounded("q_scales0"))
+        turn_q(3, grouped[:, 2 * QUERIES :], rounded("q_codes0"))
+        quantised.update(quantise_q([2, 3], grouped, placed("q_codes2", [P, 4 * P], U32, 5 * KB)))
+        angles[2] = look_up(2, placed("angles2", pair_shape, F32, 12 * KB))
+        gradient = placed("gradient1", [P, SLOTS], F32, 10 * KB)
+        rotate(0, 1, terms_in("terms0"), gradient[:])
+        angles[3] = look_up(3, placed("angles3", pair_shape, F32, 8 * KB))
         for b in range(1, BLOCKS):
-            sums[b] = multiply(b)
-        for b in range(1, BLOCKS):
+            held[b], a = multiply(b)
+            negate(held[b], a)
+
+        gradients = keep.tile(pair_shape, F32, name="gradients1", tag="cos_table3")
+        for h in range(2):
+            rotate(1, h, terms_in("terms%d" % h), gradients[:, h, :])
+        for b in (2, 3):
+            gradients = keep.tile(pair_shape, F32, name="gradients%d" % b)
             for h in range(2):
-                rotate(b, h, columns(1, "gradient%d_%d" % (b, h))[:, 0, :])
-            if b == 1:
-                angles[3] = look_up(3, columns(2, "sin_table0"))
+                rotate(b, h, terms_in("terms0"), None if (b, h) == (3, 1) else gradients[:, h, :])

@@ -24,6 +24,7 @@ POSITIONS = 1024
 TOKENS = 2048
 BLOCKS = FEATURES // P
 WINDOWS = 3
+G_COLS = SLOTS // 2
 
 FLOPS = 2 * 2 * FEATURES * QUERIES * SLOTS
 
@@ -56,12 +57,12 @@ def tile_attend_grope_kernel(tc, q1, q2, G, cs, sn, offs, poffs, out_0, out_1):
             nc.sync.dma_start(cos_table[b][:], cs[rows, :])
             nc.sync.dma_start(sin_table[b][:], sn[rows, :])
 
-        nc.sync.dma_start(g_raw[:], G.rearrange("(p t) i -> p t i", t=PACK))
         load_q(0)
+        nc.sync.dma_start(g_raw[:], G.rearrange("(p t) i -> p t i", t=PACK))
         nc.sync.dma_start(position_list[:], poffs)
         load_tables(0)
-        nc.sync.dma_start(token_list[:], offs)
         load_tables(1)
+        nc.sync.dma_start(token_list[:], offs)
         load_q(1)
         load_q(2)
         load_q(3)
@@ -138,13 +139,12 @@ def tile_attend_grope_kernel(tc, q1, q2, G, cs, sn, offs, poffs, out_0, out_1):
             nc.gpsimd.tensor_tensor(terms[:], held[b][:, h : h + 2, :], angles[b][:], MULT)
             put(b, h, terms, gradient)
 
-        g_grouped = keep.tile([P, SLOTS, PACK], BF16, name="g_grouped", align_bytes=64)
-        nc.vector.tensor_copy(
-            g_grouped[:].rearrange("p (c i) t -> p c t i", i=4), g_raw[:].rearrange("p t (c i) -> p c t i", i=4)
-        )
-        nc.vector.quantize_mx(
-            out=g_codes[:].bitcast(E5M2), scales=g_scales[:], in_=g_grouped[:].rearrange("p c t -> p (c t)")
-        )
+        g_grouped = [keep.tile([P, G_COLS, PACK], BF16, name="g_grouped%d" % u, align_bytes=64) for u in range(2)]
+        for u, copy in enumerate((nc.vector.tensor_copy, nc.scalar.copy)):
+            copy(
+                g_grouped[u][:].rearrange("p (c i) t -> p c t i", i=4),
+                g_raw[:, :, u * G_COLS : (u + 1) * G_COLS].rearrange("p t (c i) -> p c t i", i=4),
+            )
         KB = 1024
         pair_shape = [P, 2, SLOTS]
 
@@ -154,14 +154,21 @@ def tile_attend_grope_kernel(tc, q1, q2, G, cs, sn, offs, poffs, out_0, out_1):
         def terms_in(tag):
             return keep.tile(pair_shape, F32, name="terms", tag=tag)
 
-        grouped = placed("grouped0", [P, 2 * QUERIES], BF16, 0)
+        grouped = keep.tile([P, 2 * QUERIES], BF16, name="grouped0", align_bytes=64)
         turn_q(0, grouped, rounded("rounded0"))
         codes = keep.tile([P, 2 * P], U32, name="q_codes0", align_bytes=64)
         quantised = quantise_q([0], grouped, codes)
+        for u in range(2):
+            cols = slice(u * G_COLS, (u + 1) * G_COLS)
+            nc.vector.quantize_mx(
+                out=g_codes[:, cols].bitcast(E5M2),
+                scales=g_scales[:, cols],
+                in_=g_grouped[u][:].rearrange("p c t -> p (c t)"),
+            )
         first, a = multiply(0)
         negate(first, a)
         held = {0: first}
-        angles = {0: look_up(0, placed("angles0", pair_shape, F32, 0))}
+        angles = {0: look_up(0, keep.tile(pair_shape, F32, name="angles0", tag="grouped0", align_bytes=64))}
         angles[1] = look_up(1, keep.tile(pair_shape, F32, name="angles1", tag="cos_table0"))
 
         terms = terms_in("terms0")

@@ -33,7 +33,6 @@ def tile_attend_grope_kernel(tc, q1, q2, G, cs, sn, offs, poffs, out_0, out_1):
     nc = tc.nc
     with ExitStack() as ctx:
         keep = ctx.enter_context(tc.tile_pool(name="keep", bufs=1))
-        shared = ctx.enter_context(tc.tile_pool(name="shared", bufs=1))
         psum = ctx.enter_context(tc.psum_pool(name="psum", bufs=1))
 
         token_list = keep.tile([P, SLOTS // 16], U16, name="token_list")
@@ -52,28 +51,33 @@ def tile_attend_grope_kernel(tc, q1, q2, G, cs, sn, offs, poffs, out_0, out_1):
             nc.sync.dma_start(q_raw[b][0][:], q1[rows, :])
             nc.sync.dma_start(q_raw[b][1][:], q2[rows, :])
 
-        def load_tables(b):
-            rows = slice(b * P, (b + 1) * P)
-            nc.sync.dma_start(cos_table[b][:], cs[rows, :])
-            nc.sync.dma_start(sin_table[b][:], sn[rows, :])
+        def load_cos(b):
+            nc.sync.dma_start(cos_table[b][:], cs[b * P : (b + 1) * P, :])
+
+        def load_sin(b):
+            nc.sync.dma_start(sin_table[b][:], sn[b * P : (b + 1) * P, :])
 
         load_q(0)
         nc.sync.dma_start(g_raw[:], G.rearrange("(p t) i -> p t i", t=PACK))
-        nc.sync.dma_start(position_list[:], poffs)
-        load_tables(0)
-        load_tables(1)
-        nc.sync.dma_start(token_list[:], offs)
         load_q(1)
+        nc.sync.dma_start(position_list[:], poffs)
+        for b in range(2):
+            load_cos(b)
+            load_sin(b)
+        load_cos(2)
+        nc.sync.dma_start(token_list[:], offs)
         load_q(2)
         load_q(3)
-        load_tables(2)
-        load_tables(3)
+        load_sin(2)
+        load_cos(3)
+        load_sin(3)
 
         make_identity(nc, identity[:])
         for window in windows:
             nc.vector.memset(window[:].bitcast(I32), 0)
 
-        def turn_q(b, grouped, rounded):
+        def turn_q(b, grouped):
+            rounded = keep.tile([P, 2, QUERIES], BF16, name="rounded", tag="rounded%d" % (b % 2), align_bytes=64)
             for h in range(2):
                 nc.scalar.copy(
                     rounded[:, h, :].rearrange("f (u p e) -> f u p e", u=2, e=2),
@@ -84,14 +88,15 @@ def tile_attend_grope_kernel(tc, q1, q2, G, cs, sn, offs, poffs, out_0, out_1):
                 for u in range(2):
                     nc.tensor.transpose(turned[:, u, :], words[:, u * P : (u + 1) * P], identity[:])
                 nc.scalar.copy(
-                    grouped[:, h * QUERIES : (h + 1) * QUERIES].bitcast(F32).rearrange("p (f u) -> p f u", u=2),
+                    grouped[:, h * 2 * P : (h + 1) * 2 * P].rearrange("p (f u) -> p f u", u=2),
                     turned[:].rearrange("p u f -> p f u"),
                 )
 
-        def quantise_q(blocks, grouped, codes):
+        def quantise_q(blocks, grouped):
             n = 2 * P * len(blocks)
-            scales = keep.tile([P, n], U8, name="q_scales", tag="q_scales%d" % blocks[0], align_bytes=64)
-            nc.vector.quantize_mx(out=codes[:].bitcast(E4M3), scales=scales[:], in_=grouped[:])
+            codes = keep.tile([P, n], U32, name="q_codes%d" % blocks[0], align_bytes=64)
+            scales = keep.tile([P, n], U8, name="q_scales%d" % blocks[0], align_bytes=64)
+            nc.vector.quantize_mx(out=codes[:].bitcast(E4M3), scales=scales[:], in_=grouped.bitcast(BF16))
             return {b: (codes, scales, 2 * j * P) for j, b in enumerate(blocks)}
 
         def multiply(b):
@@ -100,7 +105,7 @@ def tile_attend_grope_kernel(tc, q1, q2, G, cs, sn, offs, poffs, out_0, out_1):
             banks = []
             for h in range(2):
                 cols = slice(first + h * P, first + (h + 1) * P)
-                acc = psum.tile([P, SLOTS], F32, name="acc", tag="bank%d" % h if b == 1 else "acc%d_%d" % (b, h))
+                acc = psum.tile([P, SLOTS], F32, name="acc", tag="acc%d_%d" % (b % 2, h))
                 nc.tensor.matmul_mx(
                     out=acc[:],
                     lhsT=codes[:, cols].bitcast(E4M3),
@@ -112,90 +117,86 @@ def tile_attend_grope_kernel(tc, q1, q2, G, cs, sn, offs, poffs, out_0, out_1):
                 )
                 nc.scalar.copy(held[:, h, :], acc[:])
                 banks.append(acc)
-            return held, banks[0]
+            nc.scalar.activation(held[:, 2, :], banks[0][:], COPY, scale=-1.0)
+            return held
 
-        def negate(held, a):
-            nc.scalar.activation(held[:, 2, :], a[:], COPY, scale=-1.0)
+        def look_up(out, table):
+            nc.vector.tensor_copy(out, table[:].indirect(position_list[:]))
 
-        def look_up(b, pair):
-            nc.vector.tensor_copy(pair[:, 0, :], cos_table[b][:].indirect(position_list[:]))
-            nc.vector.tensor_copy(pair[:, 1, :], sin_table[b][:].indirect(position_list[:]))
-            return pair
-
-        def placed(name, shape, dtype, offset):
-            return shared.tile(shape, dtype, name=name, offset=offset, align_bytes=64)
-
-        def put(b, h, terms, gradient):
+        def put(b, h, gradient):
             window = windows[(2 * b + h) % WINDOWS]
             places = window[:].indirect(token_list[:])
-            if gradient is None:
-                nc.vector.tensor_tensor(places, terms[:, 0, :], terms[:, 1, :], ADD)
+            if len(gradient) == 2:
+                nc.vector.tensor_tensor(places, gradient[0], gradient[1], ADD)
             else:
-                nc.gpsimd.tensor_tensor(gradient, terms[:, 0, :], terms[:, 1, :], ADD)
-                nc.vector.tensor_copy(places, gradient)
+                nc.vector.tensor_copy(places, gradient[0])
             nc.sync.dma_start((out_0, out_1)[h][b * P : (b + 1) * P, :], window[:])
 
-        def rotate(b, h, terms, gradient):
-            nc.gpsimd.tensor_tensor(terms[:], held[b][:, h : h + 2, :], angles[b][:], MULT)
-            put(b, h, terms, gradient)
+        def pair(ap):
+            return ap.rearrange("p (n i) -> p n i", n=2)
 
-        g_grouped = [keep.tile([P, G_COLS, PACK], BF16, name="g_grouped%d" % u, align_bytes=64) for u in range(2)]
+        S = SLOTS
+        grouped = keep.tile([P, QUERIES], F32, name="grouped0", align_bytes=64)
+        turn_q(0, grouped[:])
+        quantised = quantise_q([0], grouped[:])
+
+        early = keep.tile([P, 2 * S], F32, name="early", align_bytes=64)
+        g_first = keep.tile([P, S], F32, name="g_first", align_bytes=64)
+        g_grouped = [g_first[:].bitcast(BF16), early[:, :S].bitcast(BF16)]
         for u, copy in enumerate((nc.vector.tensor_copy, nc.scalar.copy)):
             copy(
-                g_grouped[u][:].rearrange("p (c i) t -> p c t i", i=4),
+                g_grouped[u].rearrange("p (c i t) -> p c t i", i=4, t=PACK),
                 g_raw[:, :, u * G_COLS : (u + 1) * G_COLS].rearrange("p t (c i) -> p c t i", i=4),
             )
-        KB = 1024
-        pair_shape = [P, 2, SLOTS]
-
-        def rounded(tag):
-            return keep.tile([P, 2, QUERIES], BF16, name="rounded", tag=tag, align_bytes=64)
-
-        def terms_in(tag):
-            return keep.tile(pair_shape, F32, name="terms", tag=tag)
-
-        grouped = keep.tile([P, 2 * QUERIES], BF16, name="grouped0", align_bytes=64)
-        turn_q(0, grouped, rounded("rounded0"))
-        codes = keep.tile([P, 2 * P], U32, name="q_codes0", align_bytes=64)
-        quantised = quantise_q([0], grouped, codes)
         for u in range(2):
             cols = slice(u * G_COLS, (u + 1) * G_COLS)
-            nc.vector.quantize_mx(
-                out=g_codes[:, cols].bitcast(E5M2),
-                scales=g_scales[:, cols],
-                in_=g_grouped[u][:].rearrange("p c t -> p (c t)"),
-            )
-        first, a = multiply(0)
-        negate(first, a)
-        held = {0: first}
-        angles = {0: look_up(0, keep.tile(pair_shape, F32, name="angles0", tag="grouped0", align_bytes=64))}
-        angles[1] = look_up(1, keep.tile(pair_shape, F32, name="angles1", tag="cos_table0"))
+            nc.vector.quantize_mx(out=g_codes[:, cols].bitcast(E5M2), scales=g_scales[:, cols], in_=g_grouped[u])
+        held = {0: multiply(0)}
+        turn_q(1, early[:, S:])
+        quantised.update(quantise_q([1], early[:, S:]))
+        held[1] = multiply(1)
 
-        terms = terms_in("terms0")
+        late = keep.tile([P, 5 * S], F32, name="late", align_bytes=64)
+        late_grouped = late[:, 2 * S - 128 : 4 * S - 128]
+        angles = {
+            0: early[:],
+            1: keep.tile([P, 2 * S], F32, name="angles1")[:],
+            2: late[:, 0 : 2 * S],
+        }
+        for b in range(2):
+            look_up(angles[b][:, :S], cos_table[b])
+            look_up(angles[b][:, S:], sin_table[b])
+        look_up(angles[2][:, :S], cos_table[2])
+
+        terms = keep.tile([P, 3 * S], F32, name="terms")
+        gradients = keep.tile([P, 8, S], F32, name="gradients")
         for n in range(2):
-            nc.gpsimd.tensor_tensor(terms[:, n, :], first[:, n, :], angles[0][:, n, :], MULT)
-        gradient = placed("gradient0", [P, SLOTS], F32, 4 * KB)
-        put(0, 0, terms, gradient[:])
+            nc.gpsimd.tensor_tensor(terms[:, n * S : (n + 1) * S], held[0][:, n, :], angles[0][:, n * S : (n + 1) * S], MULT)
+        nc.gpsimd.tensor_tensor(gradients[:, 0, :], terms[:, :S], terms[:, S : 2 * S], ADD)
+        put(0, 0, [gradients[:, 0, :]])
+        nc.gpsimd.tensor_tensor(pair(terms[:, S:]), held[0][:, 1:3, :], pair(angles[0]), MULT)
+        nc.gpsimd.tensor_tensor(terms[:, :S], held[1][:, 0, :], angles[1][:, :S], MULT)
 
-        grouped = keep.tile([P, 2 * QUERIES], BF16, name="grouped1", align_bytes=64)
-        turn_q(1, grouped, rounded("q_codes0"))
-        quantised.update(quantise_q([1], grouped, placed("q_codes1", [P, 2 * P], U32, 4 * KB)))
-        grouped = placed("grouped2", [P, 4 * QUERIES], BF16, 10 * KB)
-        turn_q(2, grouped[:, : 2 * QUERIES], rounded("q_scales0"))
-        turn_q(3, grouped[:, 2 * QUERIES :], rounded("q_codes0"))
-        quantised.update(quantise_q([2, 3], grouped, placed("q_codes2", [P, 4 * P], U32, 5 * KB)))
-        angles[2] = look_up(2, placed("angles2", pair_shape, F32, 12 * KB))
-        gradient = placed("gradient1", [P, SLOTS], F32, 10 * KB)
-        rotate(0, 1, terms_in("terms0"), gradient[:])
-        angles[3] = look_up(3, placed("angles3", pair_shape, F32, 8 * KB))
-        for b in range(1, BLOCKS):
-            held[b], a = multiply(b)
-            negate(held[b], a)
+        turn_q(2, late_grouped[:, :QUERIES])
+        turn_q(3, late_grouped[:, QUERIES:])
+        quantised.update(quantise_q([2, 3], late_grouped))
+        look_up(angles[2][:, S:], sin_table[2])
+        second, sine_term = late[:, 2 * S : 3 * S], late[:, 3 * S : 4 * S]
+        nc.gpsimd.tensor_tensor(second, terms[:, S : 2 * S], terms[:, 2 * S :], ADD)
+        nc.gpsimd.tensor_tensor(sine_term, held[1][:, 1, :], angles[1][:, S:], MULT)
+        nc.gpsimd.tensor_tensor(gradients[:, 2, :], terms[:, :S], sine_term, ADD)
+        angles[3] = keep.tile([P, 2 * S], F32, name="angles3", tag="sin_table2")[:]
+        look_up(angles[3][:, :S], cos_table[3])
+        look_up(angles[3][:, S:], sin_table[3])
+        put(0, 1, [second])
+        put(1, 0, [gradients[:, 2, :]])
+        held.update({b: multiply(b) for b in (2, 3)})
 
-        gradients = keep.tile(pair_shape, F32, name="gradients1", tag="cos_table3")
-        for h in range(2):
-            rotate(1, h, terms_in("terms%d" % h), gradients[:, h, :])
-        for b in (2, 3):
-            gradients = keep.tile(pair_shape, F32, name="gradients%d" % b)
-            for h in range(2):
-                rotate(b, h, terms_in("terms0"), None if (b, h) == (3, 1) else gradients[:, h, :])
+        for k in range(3, 2 * BLOCKS):
+            b, h = divmod(k, 2)
+            nc.gpsimd.tensor_tensor(pair(terms[:, : 2 * S]), held[b][:, h : h + 2, :], pair(angles[b]), MULT)
+            if k < 2 * BLOCKS - 1:
+                nc.gpsimd.tensor_tensor(gradients[:, k, :], terms[:, :S], terms[:, S : 2 * S], ADD)
+                put(b, h, [gradients[:, k, :]])
+            else:
+                put(b, h, [terms[:, :S], terms[:, S : 2 * S]])

@@ -33,6 +33,7 @@ def tile_attend_grope_kernel(tc, q1, q2, G, cs, sn, offs, poffs, out_0, out_1):
     nc = tc.nc
     with ExitStack() as ctx:
         keep = ctx.enter_context(tc.tile_pool(name="keep", bufs=1))
+        shared = ctx.enter_context(tc.tile_pool(name="shared", bufs=1))
         psum = ctx.enter_context(tc.psum_pool(name="psum", bufs=1))
 
         token_list = keep.tile([P, SLOTS // 16], U16, name="token_list")
@@ -58,8 +59,8 @@ def tile_attend_grope_kernel(tc, q1, q2, G, cs, sn, offs, poffs, out_0, out_1):
             nc.sync.dma_start(sin_table[b][:], sn[b * P : (b + 1) * P, :])
 
         load_q(0)
-        nc.sync.dma_start(g_raw[:], G.rearrange("(p t) i -> p t i", t=PACK))
         load_q(1)
+        nc.sync.dma_start(g_raw[:], G.rearrange("(p t) i -> p t i", t=PACK))
         nc.sync.dma_start(position_list[:], poffs)
         for b in range(2):
             load_cos(b)
@@ -76,32 +77,35 @@ def tile_attend_grope_kernel(tc, q1, q2, G, cs, sn, offs, poffs, out_0, out_1):
         for window in windows:
             nc.vector.memset(window[:].bitcast(I32), 0)
 
-        def turn_q(b, grouped):
-            rounded = keep.tile([P, 2, QUERIES], BF16, name="rounded", tag="rounded%d" % (b % 2), align_bytes=64)
+        def turn_q(b, grouped, copy_out):
             for h in range(2):
+                if (b, h) == (1, 1):
+                    words = early[:, S : S + 2 * P]
+                elif (b, h) == (3, 1):
+                    words = held[1][:, 2 * S : 2 * S + 2 * P]
+                else:
+                    words = keep.tile([P, 2 * P], F32, name="rounded%d_%d" % (h, b), align_bytes=64)[:]
                 nc.scalar.copy(
-                    rounded[:, h, :].rearrange("f (u p e) -> f u p e", u=2, e=2),
+                    words.bitcast(BF16).rearrange("f (u p e) -> f u p e", u=2, e=2),
                     q_raw[b][h][:].rearrange("f (p u e) -> f u p e", u=2, e=2),
                 )
-                words = rounded[:, h, :].bitcast(F32)
                 turned = psum.tile([P, 2, P], F32, name="turned", tag="bank%d" % h)
                 for u in range(2):
                     nc.tensor.transpose(turned[:, u, :], words[:, u * P : (u + 1) * P], identity[:])
-                nc.scalar.copy(
+                copy_out(
                     grouped[:, h * 2 * P : (h + 1) * 2 * P].rearrange("p (f u) -> p f u", u=2),
                     turned[:].rearrange("p u f -> p f u"),
                 )
 
-        def quantise_q(blocks, grouped):
+        def quantise_q(blocks, grouped, tag):
             n = 2 * P * len(blocks)
-            codes = keep.tile([P, n], U32, name="q_codes%d" % blocks[0], align_bytes=64)
+            codes = keep.tile([P, n], U32, name="q_codes", tag=tag, align_bytes=64)
             scales = keep.tile([P, n], U8, name="q_scales%d" % blocks[0], align_bytes=64)
             nc.vector.quantize_mx(out=codes[:].bitcast(E4M3), scales=scales[:], in_=grouped.bitcast(BF16))
             return {b: (codes, scales, 2 * j * P) for j, b in enumerate(blocks)}
 
         def multiply(b):
             codes, scales, first = quantised[b]
-            held = keep.tile([P, 3, SLOTS], F32, name="held%d" % b)
             banks = []
             for h in range(2):
                 cols = slice(first + h * P, first + (h + 1) * P)
@@ -115,16 +119,18 @@ def tile_attend_grope_kernel(tc, q1, q2, G, cs, sn, offs, poffs, out_0, out_1):
                     start=True,
                     stop=True,
                 )
-                nc.scalar.copy(held[:, h, :], acc[:])
+                nc.scalar.copy(held[b][:, h * S : (h + 1) * S], acc[:])
                 banks.append(acc)
-            nc.scalar.activation(held[:, 2, :], banks[0][:], COPY, scale=-1.0)
-            return held
+            return banks[0]
+
+        def negate(b, a):
+            nc.scalar.activation(held[b][:, 2 * S :], a[:], COPY, scale=-1.0)
 
         def look_up(out, table):
             nc.vector.tensor_copy(out, table[:].indirect(position_list[:]))
 
-        def put(b, h, gradient):
-            window = windows[(2 * b + h) % WINDOWS]
+        def put(b, h, gradient, turn):
+            window = windows[turn % WINDOWS]
             places = window[:].indirect(token_list[:])
             if len(gradient) == 2:
                 nc.vector.tensor_tensor(places, gradient[0], gradient[1], ADD)
@@ -132,17 +138,28 @@ def tile_attend_grope_kernel(tc, q1, q2, G, cs, sn, offs, poffs, out_0, out_1):
                 nc.vector.tensor_copy(places, gradient[0])
             nc.sync.dma_start((out_0, out_1)[h][b * P : (b + 1) * P, :], window[:])
 
-        def pair(ap):
-            return ap.rearrange("p (n i) -> p n i", n=2)
+        def add_on_tensor(out, first, second):
+            summed = psum.tile([P, PACK, P], F32, name="summed", tag="bank1")
+            for j in range(PACK):
+                for n, term in enumerate((first, second)):
+                    nc.tensor.matmul(
+                        summed[:, j, :], term[:, j * P : (j + 1) * P], identity[:], start=n == 0, stop=n == 1, is_transpose=True
+                    )
+            across = keep.tile([P, PACK, P], F32, name="across")
+            nc.scalar.copy(across[:], summed[:])
+            back = psum.tile([P, PACK, P], F32, name="back", tag="bank0")
+            for j in range(PACK):
+                nc.tensor.transpose(back[:, j, :], across[:, j, :], identity[:])
+            nc.scalar.copy(out, back[:].rearrange("p j i -> p (j i)"))
 
         S = SLOTS
-        grouped = keep.tile([P, QUERIES], F32, name="grouped0", align_bytes=64)
-        turn_q(0, grouped[:])
-        quantised = quantise_q([0], grouped[:])
-
-        early = keep.tile([P, 2 * S], F32, name="early", align_bytes=64)
-        g_first = keep.tile([P, S], F32, name="g_first", align_bytes=64)
-        g_grouped = [g_first[:].bitcast(BF16), early[:, :S].bitcast(BF16)]
+        early = shared.tile([P, 3 * S], F32, name="early", offset=4096 - 64, align_bytes=64)[:]
+        quantised = {}
+        for b in range(2):
+            grouped = early[:, 2 * b * S : (2 * b + 1) * S]
+            turn_q(b, grouped, nc.vector.tensor_copy)
+            quantised.update(quantise_q([b], grouped, "q_codes%d" % b))
+        g_grouped = [early[:, u * S : (u + 1) * S].bitcast(BF16) for u in range(2)]
         for u, copy in enumerate((nc.vector.tensor_copy, nc.scalar.copy)):
             copy(
                 g_grouped[u].rearrange("p (c i t) -> p c t i", i=4, t=PACK),
@@ -151,16 +168,15 @@ def tile_attend_grope_kernel(tc, q1, q2, G, cs, sn, offs, poffs, out_0, out_1):
         for u in range(2):
             cols = slice(u * G_COLS, (u + 1) * G_COLS)
             nc.vector.quantize_mx(out=g_codes[:, cols].bitcast(E5M2), scales=g_scales[:, cols], in_=g_grouped[u])
-        held = {0: multiply(0)}
-        turn_q(1, early[:, S:])
-        quantised.update(quantise_q([1], early[:, S:]))
-        held[1] = multiply(1)
+        held = [keep.tile([P, 3 * S], F32, name="held%d" % b, align_bytes=64) for b in range(BLOCKS)]
+        negate(0, multiply(0))
+        a = multiply(1)
 
-        late = keep.tile([P, 5 * S], F32, name="late", align_bytes=64)
+        late = shared.tile([P, 5 * S], F32, name="late", offset=8192, align_bytes=64)
         late_grouped = late[:, 2 * S - 128 : 4 * S - 128]
         angles = {
-            0: early[:],
-            1: keep.tile([P, 2 * S], F32, name="angles1")[:],
+            0: shared.tile([P, 2 * S], F32, name="angles0", offset=0, align_bytes=64)[:],
+            1: shared.tile([P, 2 * S], F32, name="angles1", offset=4096, align_bytes=64)[:],
             2: late[:, 0 : 2 * S],
         }
         for b in range(2):
@@ -168,35 +184,41 @@ def tile_attend_grope_kernel(tc, q1, q2, G, cs, sn, offs, poffs, out_0, out_1):
             look_up(angles[b][:, S:], sin_table[b])
         look_up(angles[2][:, :S], cos_table[2])
 
-        terms = keep.tile([P, 3 * S], F32, name="terms")
+        row = keep.tile([P, 4 * S], F32, name="terms")
+        terms = row[:, S:]
         gradients = keep.tile([P, 8, S], F32, name="gradients")
         for n in range(2):
-            nc.gpsimd.tensor_tensor(terms[:, n * S : (n + 1) * S], held[0][:, n, :], angles[0][:, n * S : (n + 1) * S], MULT)
+            nc.gpsimd.tensor_tensor(terms[:, n * S : (n + 1) * S], held[0][:, n * S : (n + 1) * S], angles[0][:, n * S : (n + 1) * S], MULT)
         nc.gpsimd.tensor_tensor(gradients[:, 0, :], terms[:, :S], terms[:, S : 2 * S], ADD)
-        put(0, 0, [gradients[:, 0, :]])
-        nc.gpsimd.tensor_tensor(pair(terms[:, S:]), held[0][:, 1:3, :], pair(angles[0]), MULT)
-        nc.gpsimd.tensor_tensor(terms[:, :S], held[1][:, 0, :], angles[1][:, :S], MULT)
+        put(0, 0, [gradients[:, 0, :]], 0)
+        nc.gpsimd.tensor_tensor(terms[:, S:], held[0][:, S:], angles[0], MULT)
+        nc.gpsimd.tensor_tensor(terms[:, :S], held[1][:, :S], angles[1][:, :S], MULT)
 
-        turn_q(2, late_grouped[:, :QUERIES])
-        turn_q(3, late_grouped[:, QUERIES:])
-        quantised.update(quantise_q([2, 3], late_grouped))
+        turn_q(2, late_grouped[:, :QUERIES], nc.scalar.copy)
+        turn_q(3, late_grouped[:, QUERIES:], nc.scalar.copy)
+        negate(1, a)
+        quantised.update(quantise_q([2, 3], late_grouped, "q_codes2"))
         look_up(angles[2][:, S:], sin_table[2])
-        second, sine_term = late[:, 2 * S : 3 * S], late[:, 3 * S : 4 * S]
-        nc.gpsimd.tensor_tensor(second, terms[:, S : 2 * S], terms[:, 2 * S :], ADD)
-        nc.gpsimd.tensor_tensor(sine_term, held[1][:, 1, :], angles[1][:, S:], MULT)
+        sine_term = late[:, 2 * S : 3 * S]
+        nc.gpsimd.tensor_tensor(sine_term, held[1][:, S : 2 * S], angles[1][:, S:], MULT)
         nc.gpsimd.tensor_tensor(gradients[:, 2, :], terms[:, :S], sine_term, ADD)
-        angles[3] = keep.tile([P, 2 * S], F32, name="angles3", tag="sin_table2")[:]
+        second = row[:, S // 2 : 3 * S // 2]
+        add_on_tensor(second, terms[:, S : 2 * S], terms[:, 2 * S : 3 * S])
+        angles[3] = late[:, 3 * S :]
         look_up(angles[3][:, :S], cos_table[3])
         look_up(angles[3][:, S:], sin_table[3])
-        put(0, 1, [second])
-        put(1, 0, [gradients[:, 2, :]])
-        held.update({b: multiply(b) for b in (2, 3)})
+        put(1, 0, [gradients[:, 2, :]], 1)
+        for b in (2, 3):
+            negate(b, multiply(b))
 
+        products = row[:, 3 * S // 2 : 7 * S // 2]
         for k in range(3, 2 * BLOCKS):
             b, h = divmod(k, 2)
-            nc.gpsimd.tensor_tensor(pair(terms[:, : 2 * S]), held[b][:, h : h + 2, :], pair(angles[b]), MULT)
+            nc.gpsimd.tensor_tensor(products, held[b][:, h * S : (h + 2) * S], angles[b], MULT)
             if k < 2 * BLOCKS - 1:
-                nc.gpsimd.tensor_tensor(gradients[:, k, :], terms[:, :S], terms[:, S : 2 * S], ADD)
-                put(b, h, [gradients[:, k, :]])
+                nc.gpsimd.tensor_tensor(gradients[:, k, :], products[:, :S], products[:, S:], ADD)
+                put(b, h, [gradients[:, k, :]], 2 if k == 3 else k)
+                if k == 3:
+                    put(0, 1, [second], 3)
             else:
-                put(b, h, [terms[:, :S], terms[:, S : 2 * S]])
+                put(b, h, [products[:, :S], products[:, S:]], k)

@@ -13,6 +13,7 @@ E4M3 = mybir.dt.float8_e4m3fn_x4
 E5M2 = mybir.dt.float8_e5m2_x4
 MULT = mybir.AluOpType.mult
 ADD = mybir.AluOpType.add
+SUBTRACT = mybir.AluOpType.subtract
 COPY = mybir.ActivationFunctionType.Copy
 
 P = 128
@@ -23,8 +24,13 @@ SLOTS = 512
 POSITIONS = 1024
 TOKENS = 2048
 BLOCKS = FEATURES // P
-WINDOWS = 3
-G_COLS = SLOTS // 2
+LAST = BLOCKS - 1
+BAND = 16
+HALF = SLOTS // 2
+QUARTER = SLOTS // 4
+ROW_WORDS = QUERIES // 2
+WORD_BYTES = 4
+OVERLAP = 16
 
 FLOPS = 2 * 2 * FEATURES * QUERIES * SLOTS
 
@@ -33,192 +39,237 @@ def tile_attend_grope_kernel(tc, q1, q2, G, cs, sn, offs, poffs, out_0, out_1):
     nc = tc.nc
     with ExitStack() as ctx:
         keep = ctx.enter_context(tc.tile_pool(name="keep", bufs=1))
-        shared = ctx.enter_context(tc.tile_pool(name="shared", bufs=1))
+        placed = ctx.enter_context(tc.tile_pool(name="placed", bufs=1))
         psum = ctx.enter_context(tc.psum_pool(name="psum", bufs=1))
 
-        token_list = keep.tile([P, SLOTS // 16], U16, name="token_list")
-        position_list = keep.tile([P, SLOTS // 16], U16, name="position_list")
-        q_raw = [[keep.tile([P, QUERIES], F32, name="q_raw%d_%d" % (h, b)) for h in range(2)] for b in range(BLOCKS)]
-        g_raw = keep.tile([P, PACK, SLOTS], F32, name="g_raw")
-        cos_table = [keep.tile([P, POSITIONS], F32, name="cos_table%d" % b) for b in range(BLOCKS)]
-        sin_table = [keep.tile([P, POSITIONS], F32, name="sin_table%d" % b) for b in range(BLOCKS)]
-        windows = [keep.tile([P, TOKENS], F32, name="window%d" % w) for w in range(WINDOWS)]
+        def rows(x, block):
+            g, j = divmod(block, 2)
+            return x[g * 2 * P : (g + 1) * 2 * P, :].rearrange("(p j) n -> p j n", j=2)[:, j, :]
+
+        def buffer(tag, columns=SLOTS, dtype=F32):
+            return keep.tile([P, columns], dtype, name=tag, tag=tag, align_bytes=64)
+
+        def bank(number, shape):
+            return psum.tile([P] + shape, F32, name="bank", tag="bank%d" % number)
+
+        token_list = keep.tile([P, SLOTS // BAND], U16, name="token_list")
+        position_list = keep.tile([P, SLOTS // BAND], U16, name="position_list")
+        q_raw = [[keep.tile([P, 2 * QUERIES], F32, name="q_raw%d_%d" % (g, h)) for h in range(2)] for g in range(2)]
+        g_raw = [keep.tile([P, PACK, HALF], F32, name="g_raw%d" % u) for u in range(2)]
+        cos_table = [buffer("cos_table%d" % block, POSITIONS) for block in range(BLOCKS)]
+        sin_table = [buffer("sin_table%d" % block, POSITIONS) for block in range(BLOCKS)]
+        windows = [[keep.tile([P, TOKENS], F32, name="window%d_%d" % (h, w)) for w in range(2)] for h in range(2)]
         identity = keep.tile([P, P], F32, name="identity")
         g_codes = keep.tile([P, SLOTS], U32, name="g_codes", align_bytes=64)
         g_scales = keep.tile([P, SLOTS], U8, name="g_scales", align_bytes=64)
 
-        def load_q(b):
-            rows = slice(b * P, (b + 1) * P)
-            nc.sync.dma_start(q_raw[b][0][:], q1[rows, :])
-            nc.sync.dma_start(q_raw[b][1][:], q2[rows, :])
+        def load_q(g):
+            for h, q in enumerate((q1, q2)):
+                nc.sync.dma_start(q_raw[g][h][:], q[g * 2 * P : (g + 1) * 2 * P, :].rearrange("(p j) r -> p (j r)", j=2))
 
-        def load_cos(b):
-            nc.sync.dma_start(cos_table[b][:], cs[b * P : (b + 1) * P, :])
+        def load_tables(block):
+            nc.sync.dma_start(cos_table[block][:], rows(cs, block))
+            nc.sync.dma_start(sin_table[block][:], rows(sn, block))
 
-        def load_sin(b):
-            nc.sync.dma_start(sin_table[b][:], sn[b * P : (b + 1) * P, :])
+        def load_g(u):
+            nc.sync.dma_start(g_raw[u][:], G[:, u * HALF : (u + 1) * HALF].rearrange("(p t) i -> p t i", t=PACK))
 
         load_q(0)
-        load_q(1)
-        nc.sync.dma_start(g_raw[:], G.rearrange("(p t) i -> p t i", t=PACK))
+        load_g(0)
         nc.sync.dma_start(position_list[:], poffs)
-        for b in range(2):
-            load_cos(b)
-            load_sin(b)
-        load_cos(2)
+        nc.sync.dma_start(cos_table[0][:], rows(cs, 0))
+        load_g(1)
+        nc.sync.dma_start(sin_table[0][:], rows(sn, 0))
+        load_tables(1)
         nc.sync.dma_start(token_list[:], offs)
-        load_q(2)
-        load_q(3)
-        load_sin(2)
-        load_cos(3)
-        load_sin(3)
+        load_q(1)
+        load_tables(2)
+        load_tables(3)
 
         make_identity(nc, identity[:])
-        for window in windows:
-            nc.vector.memset(window[:].bitcast(I32), 0)
+        for w in range(2):
+            for h in (1, 0):
+                nc.vector.memset(windows[h][w][:].bitcast(I32), 0)
 
-        def turn_q(b, grouped, copy_out):
-            for h in range(2):
-                if (b, h) == (1, 1):
-                    words = early[:, S : S + 2 * P]
-                elif (b, h) == (3, 1):
-                    words = held[1][:, 2 * S : 2 * S + 2 * P]
-                else:
-                    words = keep.tile([P, 2 * P], F32, name="rounded%d_%d" % (h, b), align_bytes=64)[:]
-                nc.scalar.copy(
-                    words.bitcast(BF16).rearrange("f (u p e) -> f u p e", u=2, e=2),
-                    q_raw[b][h][:].rearrange("f (p u e) -> f u p e", u=2, e=2),
-                )
-                turned = psum.tile([P, 2, P], F32, name="turned", tag="bank%d" % h)
-                for u in range(2):
-                    nc.tensor.transpose(turned[:, u, :], words[:, u * P : (u + 1) * P], identity[:])
-                copy_out(
-                    grouped[:, h * 2 * P : (h + 1) * 2 * P].rearrange("p (f u) -> p f u", u=2),
-                    turned[:].rearrange("p u f -> p f u"),
-                )
-
-        def quantise_q(blocks, grouped, tag):
-            n = 2 * P * len(blocks)
-            codes = keep.tile([P, n], U32, name="q_codes", tag=tag, align_bytes=64)
-            scales = keep.tile([P, n], U8, name="q_scales%d" % blocks[0], align_bytes=64)
-            nc.vector.quantize_mx(out=codes[:].bitcast(E4M3), scales=scales[:], in_=grouped.bitcast(BF16))
-            return {b: (codes, scales, 2 * j * P) for j, b in enumerate(blocks)}
-
-        def multiply(b):
-            codes, scales, first = quantised[b]
-            banks = []
-            for h in range(2):
-                cols = slice(first + h * P, first + (h + 1) * P)
-                acc = psum.tile([P, SLOTS], F32, name="acc", tag="acc%d_%d" % (b % 2, h))
-                nc.tensor.matmul_mx(
-                    out=acc[:],
-                    lhsT=codes[:, cols].bitcast(E4M3),
-                    lhsT_scale=scales[:, cols],
-                    rhs=g_codes[:].bitcast(E5M2),
-                    rhs_scale=g_scales[:],
-                    start=True,
-                    stop=True,
-                )
-                nc.scalar.copy(held[b][:, h * S : (h + 1) * S], acc[:])
-                banks.append(acc)
-            return banks[0]
-
-        def negate(b, a):
-            nc.scalar.activation(held[b][:, 2 * S :], a[:], COPY, scale=-1.0)
-
-        def look_up(out, table):
-            nc.vector.tensor_copy(out, table[:].indirect(position_list[:]))
-
-        def put(b, h, gradient, turn):
-            window = windows[turn % WINDOWS]
-            places = window[:].indirect(token_list[:])
-            if len(gradient) == 2:
-                nc.vector.tensor_tensor(places, gradient[0], gradient[1], ADD)
-            else:
-                nc.vector.tensor_copy(places, gradient[0])
-            nc.sync.dma_start((out_0, out_1)[h][b * P : (b + 1) * P, :], window[:])
-
-        def add_on_tensor(out, first, second):
-            summed = psum.tile([P, PACK, P], F32, name="summed", tag="bank1")
-            for j in range(PACK):
-                for n, term in enumerate((first, second)):
-                    nc.tensor.matmul(
-                        summed[:, j, :], term[:, j * P : (j + 1) * P], identity[:], start=n == 0, stop=n == 1, is_transpose=True
-                    )
-            across = keep.tile([P, PACK, P], F32, name="across")
-            nc.scalar.copy(across[:], summed[:])
-            back = psum.tile([P, PACK, P], F32, name="back", tag="bank0")
-            for j in range(PACK):
-                nc.tensor.transpose(back[:, j, :], across[:, j, :], identity[:])
-            nc.scalar.copy(out, back[:].rearrange("p j i -> p (j i)"))
-
-        S = SLOTS
-        early = shared.tile([P, 3 * S], F32, name="early", offset=4096 - 64, align_bytes=64)[:]
-        quantised = {}
-        for b in range(2):
-            grouped = early[:, 2 * b * S : (2 * b + 1) * S]
-            turn_q(b, grouped, nc.vector.tensor_copy)
-            quantised.update(quantise_q([b], grouped, "q_codes%d" % b))
-        g_grouped = [early[:, u * S : (u + 1) * S].bitcast(BF16) for u in range(2)]
-        for u, copy in enumerate((nc.vector.tensor_copy, nc.scalar.copy)):
-            copy(
-                g_grouped[u].rearrange("p (c i t) -> p c t i", i=4, t=PACK),
-                g_raw[:, :, u * G_COLS : (u + 1) * G_COLS].rearrange("p t (c i) -> p c t i", i=4),
+        def round_and_turn_on_scalar(h, j, words, turned):
+            nc.scalar.copy(
+                words.bitcast(BF16).rearrange("f (v p e) -> f v p e", v=2, e=2),
+                q_raw[0][h][:, j * QUERIES : (j + 1) * QUERIES].rearrange("f (p v e) -> f v p e", v=2, e=2),
             )
-        for u in range(2):
-            cols = slice(u * G_COLS, (u + 1) * G_COLS)
-            nc.vector.quantize_mx(out=g_codes[:, cols].bitcast(E5M2), scales=g_scales[:, cols], in_=g_grouped[u])
-        held = [keep.tile([P, 3 * S], F32, name="held%d" % b, align_bytes=64) for b in range(BLOCKS)]
-        negate(0, multiply(0))
-        a = multiply(1)
+            for v in range(2):
+                nc.tensor.transpose(turned[:, v, :], words[:, v * P : (v + 1) * P], identity[:])
 
-        late = shared.tile([P, 5 * S], F32, name="late", offset=8192, align_bytes=64)
-        late_grouped = late[:, 2 * S - 128 : 4 * S - 128]
-        angles = {
-            0: shared.tile([P, 2 * S], F32, name="angles0", offset=0, align_bytes=64)[:],
-            1: shared.tile([P, 2 * S], F32, name="angles1", offset=4096, align_bytes=64)[:],
-            2: late[:, 0 : 2 * S],
-        }
-        for b in range(2):
-            look_up(angles[b][:, :S], cos_table[b])
-            look_up(angles[b][:, S:], sin_table[b])
-        look_up(angles[2][:, :S], cos_table[2])
+        def round_and_turn_on_gpsimd(h, j, words, turned):
+            nc.gpsimd.tensor_scalar(words.bitcast(BF16), q_raw[1][h][:, j * QUERIES : (j + 1) * QUERIES], 1.0, 0.0, MULT, ADD)
+            for v in range(2):
+                nc.tensor.transpose(turned[:, v, :], words[:, v:ROW_WORDS:2], identity[:])
 
-        row = keep.tile([P, 4 * S], F32, name="terms")
-        terms = row[:, S:]
-        gradients = keep.tile([P, 8, S], F32, name="gradients")
-        for n in range(2):
-            nc.gpsimd.tensor_tensor(terms[:, n * S : (n + 1) * S], held[0][:, n * S : (n + 1) * S], angles[0][:, n * S : (n + 1) * S], MULT)
-        nc.gpsimd.tensor_tensor(gradients[:, 0, :], terms[:, :S], terms[:, S : 2 * S], ADD)
-        put(0, 0, [gradients[:, 0, :]], 0)
-        nc.gpsimd.tensor_tensor(terms[:, S:], held[0][:, S:], angles[0], MULT)
-        nc.gpsimd.tensor_tensor(terms[:, :S], held[1][:, :S], angles[1][:, :S], MULT)
+        def copy_two_rows(copy, grouped, turned):
+            copy(grouped.rearrange("p (n f v) -> p n f v", n=2, v=2), turned[:].rearrange("p n v f -> p n f v"))
 
-        turn_q(2, late_grouped[:, :QUERIES], nc.scalar.copy)
-        turn_q(3, late_grouped[:, QUERIES:], nc.scalar.copy)
-        negate(1, a)
-        quantised.update(quantise_q([2, 3], late_grouped, "q_codes2"))
-        look_up(angles[2][:, S:], sin_table[2])
-        sine_term = late[:, 2 * S : 3 * S]
-        nc.gpsimd.tensor_tensor(sine_term, held[1][:, S : 2 * S], angles[1][:, S:], MULT)
-        nc.gpsimd.tensor_tensor(gradients[:, 2, :], terms[:, :S], sine_term, ADD)
-        second = row[:, S // 2 : 3 * S // 2]
-        add_on_tensor(second, terms[:, S : 2 * S], terms[:, 2 * S : 3 * S])
-        angles[3] = late[:, 3 * S :]
-        look_up(angles[3][:, :S], cos_table[3])
-        look_up(angles[3][:, S:], sin_table[3])
-        put(1, 0, [gradients[:, 2, :]], 1)
-        for b in (2, 3):
-            negate(b, multiply(b))
+        def copy_one_row(grouped, turned):
+            nc.vector.tensor_copy(grouped.rearrange("p (f v) -> p f v", v=2), turned[:].rearrange("p v f -> p f v"))
 
-        products = row[:, 3 * S // 2 : 7 * S // 2]
-        for k in range(3, 2 * BLOCKS):
-            b, h = divmod(k, 2)
-            nc.gpsimd.tensor_tensor(products, held[b][:, h * S : (h + 2) * S], angles[b], MULT)
-            if k < 2 * BLOCKS - 1:
-                nc.gpsimd.tensor_tensor(gradients[:, k, :], products[:, :S], products[:, S:], ADD)
-                put(b, h, [gradients[:, k, :]], 2 if k == 3 else k)
-                if k == 3:
-                    put(0, 1, [second], 3)
+        q_codes = buffer("q_codes", 2 * BLOCKS * P, U32)
+        q_scales = buffer("q_scales", 2 * BLOCKS * P, U8)
+
+        def quantise_q(call, grouped):
+            cols = slice(call * 2 * P, (call + 1) * 2 * P)
+            nc.vector.quantize_mx(out=q_codes[:, cols].bitcast(E4M3), scales=q_scales[:, cols], in_=grouped.bitcast(BF16))
+
+        def multiply(block, parts, order):
+            g, j = divmod(block, 2)
+            banks = [bank(2 * block + h, [SLOTS]) for h in range(2)]
+            width = SLOTS // parts
+            for part in range(parts):
+                slots = slice(part * width, (part + 1) * width)
+                for h in order:
+                    run = 2 * h + j if g == 0 else BLOCKS + 2 * j + h
+                    cols = slice(run * P, (run + 1) * P)
+                    nc.tensor.matmul_mx(
+                        out=banks[h][:, slots],
+                        lhsT=q_codes[:, cols].bitcast(E4M3),
+                        lhsT_scale=q_scales[:, cols],
+                        rhs=g_codes[:, slots].bitcast(E5M2),
+                        rhs_scale=g_scales[:, slots],
+                        start=True,
+                        stop=True,
+                    )
+            return banks
+
+        first_angles_bytes = 4 * SLOTS * WORD_BYTES
+        turned = bank(4, [2, 2, P])
+        for j in range(2):
+            round_and_turn_on_scalar(0, j, buffer("rounded0_%d" % j, ROW_WORDS)[:], turned[:, j])
+        grouped = buffer("grouped0")
+        copy_two_rows(nc.vector.tensor_copy, grouped[:], turned)
+        quantise_q(0, grouped[:])
+        grouped = buffer("grouped1")
+        turned = [bank(5 + j, [2, P]) for j in range(2)]
+        round_and_turn_on_scalar(1, 0, buffer("rounded1_0", ROW_WORDS)[:], turned[0])
+        last_words = placed.tile(
+            [P, ROW_WORDS], F32, name="last_words", offset=first_angles_bytes - P * WORD_BYTES, align_bytes=64
+        )
+        round_and_turn_on_scalar(1, 1, last_words[:], turned[1])
+        for j in range(2):
+            copy_one_row(grouped[:, j * ROW_WORDS : (j + 1) * ROW_WORDS], turned[j])
+        quantise_q(1, grouped[:])
+
+        g_grouped = [
+            buffer("rounded1_0"),
+            placed.tile([P, SLOTS], F32, name="g_second_half", offset=first_angles_bytes, align_bytes=64),
+        ]
+
+        def interleave_g(u, lo, hi):
+            nc.vector.tensor_copy(
+                g_grouped[u][:, 2 * lo : 2 * hi].bitcast(BF16).rearrange("p (c i t) -> p c t i", i=4, t=PACK),
+                g_raw[u][:, :, lo:hi].rearrange("p t (c i) -> p c t i", i=4),
+            )
+
+        def quantise_g(u, lo, hi):
+            cols = slice(u * HALF + lo, u * HALF + hi)
+            nc.vector.quantize_mx(
+                out=g_codes[:, cols].bitcast(E5M2), scales=g_scales[:, cols], in_=g_grouped[u][:, 2 * lo : 2 * hi].bitcast(BF16)
+            )
+
+        interleave_g(0, 0, HALF)
+        quantise_g(0, 0, HALF)
+        for step in (interleave_g, quantise_g):
+            step(1, 0, QUARTER)
+            step(1, QUARTER, HALF)
+        sums = [multiply(0, 2, (1, 0)), multiply(1, 1, (0, 1))]
+
+        first_angles = placed.tile([P, 4 * SLOTS], F32, name="first_angles", offset=0, align_bytes=64)
+        after_block0 = buffer("after_block0", 2 * SLOTS)
+        around_block3 = buffer("around_block3", 2 * SLOTS)
+        after_quantiser = buffer("after_quantiser", 2 * SLOTS)
+        around_block2 = buffer("around_block2", 3 * SLOTS)
+        tail = buffer("tail", 2 * SLOTS)
+
+        def run_of(tile, start):
+            return tile[:, start : start + SLOTS]
+
+        cos = [run_of(first_angles, 0), run_of(first_angles, 2 * SLOTS), run_of(around_block3, OVERLAP), run_of(around_block2, HALF)]
+        sin = [
+            run_of(first_angles, SLOTS),
+            run_of(first_angles, 3 * SLOTS),
+            run_of(after_block0, 0),
+            run_of(around_block2, SLOTS + HALF),
+        ]
+        d2 = [run_of(after_block0, HALF), run_of(around_block2, SLOTS), buffer("d2_2")[:], buffer("d2_3")[:]]
+        d1 = [buffer("d1_0")[:], run_of(after_quantiser, HALF), run_of(tail, HALF)]
+        ca = [run_of(around_block2, SLOTS), buffer("ca1")[:], buffer("ca2")[:], run_of(tail, 0)]
+        cb = [buffer("cb%d" % block)[:] for block in range(BLOCKS)]
+        sa = [buffer("sa%d" % block)[:] for block in range(BLOCKS)]
+        sb = [run_of(around_block3, SLOTS), buffer("sb1")[:], buffer("sb2")[:], run_of(tail, SLOTS)]
+
+        def look_up(block):
+            nc.scalar.activation(cos[block], cos_table[block][:].indirect(position_list[:]), COPY)
+            nc.scalar.activation(sin[block], sin_table[block][:].indirect(position_list[:]), COPY)
+
+        def products(block, names):
+            a_sum, b_sum = sums[block]
+            steps = {"ca": (ca, a_sum, cos), "cb": (cb, b_sum, cos), "sa": (sa, a_sum, sin), "sb": (sb, b_sum, sin)}
+            for name in names.split():
+                term, acc, angle = steps[name]
+                nc.vector.tensor_tensor(term[block], acc[:], angle[block], MULT)
+
+        def form_d2(block):
+            nc.gpsimd.tensor_tensor(d2[block], cb[block], sa[block], SUBTRACT)
+
+        def form_d1(block):
+            nc.gpsimd.tensor_tensor(d1[block], ca[block], sb[block], ADD)
+
+        def put(block):
+            window = windows[1][block % 2]
+            for u in range(2):
+                nc.scalar.activation(
+                    window[:].indirect(token_list[:, u * HALF // BAND : (u + 1) * HALF // BAND]),
+                    d2[block][:, u * HALF : (u + 1) * HALF],
+                    COPY,
+                )
+            nc.sync.dma_start(rows(out_1, block), window[:])
+            window = windows[0][block % 2]
+            if block < LAST:
+                nc.vector.tensor_copy(window[:].indirect(token_list[:]), d1[block])
             else:
-                put(b, h, [products[:, :S], products[:, S:]], k)
+                nc.vector.tensor_tensor(window[:].indirect(token_list[:]), ca[block], sb[block], ADD)
+            nc.sync.dma_start(rows(out_0, block), window[:])
+
+        look_up(0)
+        products(0, "cb sa ca sb")
+        form_d2(0)
+        form_d1(0)
+        look_up(1)
+        products(1, "ca cb sa sb")
+        put(0)
+
+        turned_block2 = bank(6, [2, 2, P])
+        for h in range(2):
+            round_and_turn_on_gpsimd(h, 0, ca[0][:, h * ROW_WORDS : (h + 1) * ROW_WORDS], turned_block2[:, h])
+        turned_block3 = [bank(4 + h, [2, P]) for h in range(2)]
+        for h in range(2):
+            round_and_turn_on_gpsimd(h, 1, sb[0][:, h * ROW_WORDS : (h + 1) * ROW_WORDS], turned_block3[h])
+        grouped = buffer("grouped2")
+        copy_two_rows(nc.vector.tensor_copy, grouped[:], turned_block2)
+        quantise_q(2, grouped[:])
+        grouped = run_of(after_quantiser, SLOTS)
+        for h in range(2):
+            copy_one_row(grouped[:, h * ROW_WORDS : (h + 1) * ROW_WORDS], turned_block3[h])
+        quantise_q(3, grouped)
+        sums.extend(multiply(block, 1, (0, 1)) for block in (2, 3))
+
+        look_up(2)
+        form_d2(1)
+        form_d1(1)
+        products(2, "sa ca cb sb")
+        put(1)
+        form_d2(2)
+        form_d1(2)
+
+        look_up(3)
+        products(3, "cb sa")
+        put(2)
+        form_d2(3)
+        products(3, "ca sb")
+        put(3)

@@ -49,47 +49,57 @@ def tile_attend_grope_kernel(tc, q1, q2, G, cs, sn, offs, poffs, out_0, out_1):
         def buffer(tag, columns=SLOTS, dtype=F32):
             return keep.tile([P, columns], dtype, name=tag, tag=tag, align_bytes=64)
 
+        def place(name, start, columns):
+            return placed.tile([P, columns], F32, name=name, offset=start * WORD_BYTES, align_bytes=64)
+
         def bank(number, shape):
             return psum.tile([P] + shape, F32, name="bank", tag="bank%d" % number)
 
         token_list = keep.tile([P, SLOTS // BAND], U16, name="token_list")
         position_list = keep.tile([P, SLOTS // BAND], U16, name="position_list")
-        q_raw = [[keep.tile([P, 2 * QUERIES], F32, name="q_raw%d_%d" % (g, h)) for h in range(2)] for g in range(2)]
-        g_raw = [keep.tile([P, PACK, HALF], F32, name="g_raw%d" % u) for u in range(2)]
+        G_RAW = SLOTS + TOKENS
+        g_raw = placed.tile([P, PACK, SLOTS], F32, name="g_raw", offset=G_RAW * WORD_BYTES, align_bytes=64)
         cos_table = [buffer("cos_table%d" % block, POSITIONS) for block in range(BLOCKS)]
         sin_table = [buffer("sin_table%d" % block, POSITIONS) for block in range(BLOCKS)]
-        windows = [[keep.tile([P, TOKENS], F32, name="window%d_%d" % (h, w)) for w in range(2)] for h in range(2)]
         identity = keep.tile([P, P], F32, name="identity")
         g_codes = keep.tile([P, SLOTS], U32, name="g_codes", align_bytes=64)
         g_scales = keep.tile([P, SLOTS], U8, name="g_scales", align_bytes=64)
 
-        def load_q(g):
-            for h, q in enumerate((q1, q2)):
-                nc.sync.dma_start(q_raw[g][h][:], q[g * 2 * P : (g + 1) * 2 * P, :].rearrange("(p j) r -> p (j r)", j=2))
+        D2A = SLOTS - OVERLAP
+        SIN3 = D2A + HALF - OVERLAP
+        late = buffer("late", SIN3 + SLOTS)
+        q_raw = [[buffer("q_raw%d_%d" % (g, h), 2 * QUERIES)[:] for h in range(2)] for g in range(2)]
 
-        def load_tables(block):
+        def load_q(g, h):
+            q = (q1, q2)[h]
+            nc.sync.dma_start(q_raw[g][h], q[g * 2 * P : (g + 1) * 2 * P, :].rearrange("(p j) r -> p (j r)", j=2))
+
+        def load_cos(block):
             nc.sync.dma_start(cos_table[block][:], rows(cs, block))
+
+        def load_sin(block):
             nc.sync.dma_start(sin_table[block][:], rows(sn, block))
 
-        def load_g(u):
-            nc.sync.dma_start(g_raw[u][:], G[:, u * HALF : (u + 1) * HALF].rearrange("(p t) i -> p t i", t=PACK))
-
-        load_q(0)
-        load_g(0)
+        load_q(0, 1)
+        load_q(0, 0)
+        nc.sync.dma_start(g_raw[:], G.rearrange("(p t) i -> p t i", t=PACK))
         nc.sync.dma_start(position_list[:], poffs)
-        nc.sync.dma_start(cos_table[0][:], rows(cs, 0))
-        load_g(1)
-        nc.sync.dma_start(sin_table[0][:], rows(sn, 0))
-        load_tables(1)
+        load_cos(0)
+        load_sin(0)
+        load_cos(1)
+        load_sin(1)
+        load_cos(2)
         nc.sync.dma_start(token_list[:], offs)
-        load_q(1)
-        load_tables(2)
-        load_tables(3)
+        load_q(1, 0)
+        load_q(1, 1)
+        load_sin(2)
+        load_cos(3)
+        load_sin(3)
 
         make_identity(nc, identity[:])
-        for w in range(2):
-            for h in (1, 0):
-                nc.vector.memset(windows[h][w][:].bitcast(I32), 0)
+        windows = [keep.tile([P, TOKENS], F32, name="window%d" % w) for w in range(3)]
+        for window in windows:
+            nc.vector.memset(window[:].bitcast(I32), 0)
 
         def round_and_turn_on_scalar(h, j, words, turned):
             nc.scalar.copy(
@@ -104,11 +114,11 @@ def tile_attend_grope_kernel(tc, q1, q2, G, cs, sn, offs, poffs, out_0, out_1):
             for v in range(2):
                 nc.tensor.transpose(turned[:, v, :], words[:, v:ROW_WORDS:2], identity[:])
 
-        def copy_two_rows(copy, grouped, turned):
-            copy(grouped.rearrange("p (n f v) -> p n f v", n=2, v=2), turned[:].rearrange("p n v f -> p n f v"))
+        def copy_two_rows(grouped, turned):
+            nc.vector.tensor_copy(grouped.rearrange("p (n f v) -> p n f v", n=2, v=2), turned[:].rearrange("p n v f -> p n f v"))
 
         def copy_one_row(grouped, turned):
-            nc.vector.tensor_copy(grouped.rearrange("p (f v) -> p f v", v=2), turned[:].rearrange("p v f -> p f v"))
+            nc.scalar.copy(grouped.rearrange("p (f v) -> p f v", v=2), turned[:].rearrange("p v f -> p f v"))
 
         q_codes = buffer("q_codes", 2 * BLOCKS * P, U32)
         q_scales = buffer("q_scales", 2 * BLOCKS * P, U8)
@@ -137,74 +147,67 @@ def tile_attend_grope_kernel(tc, q1, q2, G, cs, sn, offs, poffs, out_0, out_1):
                     )
             return banks
 
-        first_angles_bytes = 4 * SLOTS * WORD_BYTES
         turned = bank(4, [2, 2, P])
         for j in range(2):
-            round_and_turn_on_scalar(0, j, buffer("rounded0_%d" % j, ROW_WORDS)[:], turned[:, j])
-        grouped = buffer("grouped0")
-        copy_two_rows(nc.vector.tensor_copy, grouped[:], turned)
-        quantise_q(0, grouped[:])
-        grouped = buffer("grouped1")
+            round_and_turn_on_scalar(1, j, buffer("rounded1_%d" % j, ROW_WORDS)[:], turned[:, j])
+        grouped_q2 = buffer("grouped_q2")
+        copy_two_rows(grouped_q2[:], turned)
+        quantise_q(1, grouped_q2[:])
+        grouped_q1 = buffer("grouped_q1")
         turned = [bank(5 + j, [2, P]) for j in range(2)]
-        round_and_turn_on_scalar(1, 0, buffer("rounded1_0", ROW_WORDS)[:], turned[0])
-        last_words = placed.tile(
-            [P, ROW_WORDS], F32, name="last_words", offset=first_angles_bytes - P * WORD_BYTES, align_bytes=64
-        )
-        round_and_turn_on_scalar(1, 1, last_words[:], turned[1])
+        round_and_turn_on_scalar(0, 0, buffer("rounded0_0", ROW_WORDS)[:], turned[0])
+        round_and_turn_on_scalar(0, 1, place("last_words", SLOTS, ROW_WORDS)[:], turned[1])
         for j in range(2):
-            copy_one_row(grouped[:, j * ROW_WORDS : (j + 1) * ROW_WORDS], turned[j])
-        quantise_q(1, grouped[:])
+            copy_one_row(grouped_q1[:, j * ROW_WORDS : (j + 1) * ROW_WORDS], turned[j])
 
-        g_grouped = [
-            buffer("rounded1_0"),
-            placed.tile([P, SLOTS], F32, name="g_second_half", offset=first_angles_bytes, align_bytes=64),
-        ]
+        g_grouped = [buffer("grouped_q2"), place("g_second_half", SLOTS, SLOTS)]
 
-        def interleave_g(u, lo, hi):
-            nc.vector.tensor_copy(
+        def interleave_g(copy, u, lo, hi):
+            copy(
                 g_grouped[u][:, 2 * lo : 2 * hi].bitcast(BF16).rearrange("p (c i t) -> p c t i", i=4, t=PACK),
-                g_raw[u][:, :, lo:hi].rearrange("p t (c i) -> p c t i", i=4),
+                g_raw[:, :, u * HALF + lo : u * HALF + hi].rearrange("p t (c i) -> p c t i", i=4),
             )
 
-        def quantise_g(u, lo, hi):
-            cols = slice(u * HALF + lo, u * HALF + hi)
-            nc.vector.quantize_mx(
-                out=g_codes[:, cols].bitcast(E5M2), scales=g_scales[:, cols], in_=g_grouped[u][:, 2 * lo : 2 * hi].bitcast(BF16)
-            )
+        def quantise_g(u):
+            cols = slice(u * HALF, (u + 1) * HALF)
+            nc.vector.quantize_mx(out=g_codes[:, cols].bitcast(E5M2), scales=g_scales[:, cols], in_=g_grouped[u][:].bitcast(BF16))
 
-        interleave_g(0, 0, HALF)
-        quantise_g(0, 0, HALF)
-        for step in (interleave_g, quantise_g):
-            step(1, 0, QUARTER)
-            step(1, QUARTER, HALF)
-        sums = [multiply(0, 2, (1, 0)), multiply(1, 1, (0, 1))]
+        interleave_g(nc.vector.tensor_copy, 0, 0, HALF)
+        interleave_g(nc.vector.tensor_copy, 1, 0, HALF // 4)
+        interleave_g(nc.scalar.copy, 1, HALF // 4, HALF)
+        quantise_g(0)
+        quantise_q(0, grouped_q1[:])
+        quantise_g(1)
+        windows.append(place("window3", SLOTS, TOKENS))
+        nc.gpsimd.memset(windows[3][:].bitcast(I32), 0)
+        sums = [multiply(0, 2, (1, 0)), multiply(1, 1, (1, 0))]
 
-        first_angles = placed.tile([P, 4 * SLOTS], F32, name="first_angles", offset=0, align_bytes=64)
+        tail = buffer("tail", 2 * SLOTS)
+        after_d2 = buffer("after_d2", 4 * SLOTS)
+        first_angles = place("first_angles", G_RAW, 5 * SLOTS)
         after_block0 = buffer("after_block0", 2 * SLOTS)
         around_block3 = buffer("around_block3", 2 * SLOTS)
-        after_quantiser = buffer("after_quantiser", 2 * SLOTS)
-        around_block2 = buffer("around_block2", 3 * SLOTS)
-        tail = buffer("tail", 2 * SLOTS)
 
         def run_of(tile, start):
             return tile[:, start : start + SLOTS]
 
-        cos = [run_of(first_angles, 0), run_of(first_angles, 2 * SLOTS), run_of(around_block3, OVERLAP), run_of(around_block2, HALF)]
-        sin = [
-            run_of(first_angles, SLOTS),
-            run_of(first_angles, 3 * SLOTS),
-            run_of(after_block0, 0),
-            run_of(around_block2, SLOTS + HALF),
-        ]
-        d2 = [run_of(after_block0, HALF), run_of(around_block2, SLOTS), buffer("d2_2")[:], buffer("d2_3")[:]]
-        d1 = [buffer("d1_0")[:], run_of(after_quantiser, HALF), run_of(tail, HALF)]
-        ca = [run_of(around_block2, SLOTS), buffer("ca1")[:], buffer("ca2")[:], run_of(tail, 0)]
-        cb = [buffer("cb%d" % block)[:] for block in range(BLOCKS)]
-        sa = [buffer("sa%d" % block)[:] for block in range(BLOCKS)]
-        sb = [run_of(around_block3, SLOTS), buffer("sb1")[:], buffer("sb2")[:], run_of(tail, SLOTS)]
+        cos = [run_of(first_angles, 2 * block * SLOTS) for block in range(LAST)] + [run_of(late, 0)]
+        sin = [run_of(first_angles, SLOTS), run_of(first_angles, 3 * SLOTS), run_of(after_block0, OVERLAP), run_of(late, SIN3)]
 
-        def look_up(block):
+        cb = [buffer("cb0")[:], buffer("cb1")[:], run_of(after_d2, SLOTS - OVERLAP), run_of(after_d2, 2 * SLOTS)]
+        sa = [run_of(around_block3, SLOTS), buffer("sa1")[:], run_of(after_d2, 3 * SLOTS - OVERLAP), run_of(after_d2, 3 * SLOTS)]
+        ca = [buffer("ca0")[:], buffer("ca1")[:], run_of(after_d2, 0), tail[:, 0:SLOTS]]
+        sb = [buffer("sb0")[:], run_of(around_block3, OVERLAP), run_of(after_d2, SLOTS), tail[:, SLOTS : 2 * SLOTS]]
+        after_quantiser = buffer("after_quantiser", 2 * SLOTS)
+        d1 = [buffer("d1_0")[:], run_of(after_quantiser, OVERLAP), tail[:, HALF : HALF + SLOTS]]
+
+        d2 = [[run[:, 0:HALF], run[:, HALF:SLOTS]] for run in (run_of(after_block0, SLOTS), buffer("d2_2")[:], buffer("d2_3")[:])]
+        d2.insert(1, [late[:, D2A : D2A + HALF], buffer("d2_1", HALF)[:]])
+
+        def look_up_cos(block):
             nc.scalar.activation(cos[block], cos_table[block][:].indirect(position_list[:]), COPY)
+
+        def look_up_sin(block):
             nc.scalar.activation(sin[block], sin_table[block][:].indirect(position_list[:]), COPY)
 
         def products(block, names):
@@ -215,61 +218,74 @@ def tile_attend_grope_kernel(tc, q1, q2, G, cs, sn, offs, poffs, out_0, out_1):
                 nc.vector.tensor_tensor(term[block], acc[:], angle[block], MULT)
 
         def form_d2(block):
-            nc.gpsimd.tensor_tensor(d2[block], cb[block], sa[block], SUBTRACT)
+            for u in range(2):
+                cols = slice(u * HALF, (u + 1) * HALF)
+                nc.gpsimd.tensor_tensor(d2[block][u], cb[block][:, cols], sa[block][:, cols], SUBTRACT)
 
         def form_d1(block):
             nc.gpsimd.tensor_tensor(d1[block], ca[block], sb[block], ADD)
 
-        def put(block):
-            window = windows[1][block % 2]
-            for u in range(2):
-                nc.scalar.activation(
-                    window[:].indirect(token_list[:, u * HALF // BAND : (u + 1) * HALF // BAND]),
-                    d2[block][:, u * HALF : (u + 1) * HALF],
-                    COPY,
-                )
-            nc.sync.dma_start(rows(out_1, block), window[:])
-            window = windows[0][block % 2]
+        scalar_window = [0, 2, 1, 2]
+        vector_window = [1, 3, 0, 3]
+
+        def put_d2_half(block, u):
+            window = windows[scalar_window[block]]
+            nc.scalar.activation(window[:].indirect(token_list[:, u * HALF // BAND : (u + 1) * HALF // BAND]), d2[block][u], COPY)
+            if u == 1:
+                nc.sync.dma_start(rows(out_1, block), window[:])
+
+        def put_d1(block):
+            window = windows[vector_window[block]]
             if block < LAST:
                 nc.vector.tensor_copy(window[:].indirect(token_list[:]), d1[block])
             else:
                 nc.vector.tensor_tensor(window[:].indirect(token_list[:]), ca[block], sb[block], ADD)
             nc.sync.dma_start(rows(out_0, block), window[:])
 
-        look_up(0)
-        products(0, "cb sa ca sb")
+        look_up_cos(0)
+        look_up_sin(0)
+        products(0, "cb ca sa sb")
         form_d2(0)
         form_d1(0)
-        look_up(1)
-        products(1, "ca cb sa sb")
-        put(0)
+        look_up_cos(1)
+        look_up_sin(1)
+        products(1, "cb ca sa")
+        look_up_cos(2)
+        put_d1(0)
+        put_d2_half(0, 0)
+        put_d2_half(0, 1)
 
-        turned_block2 = bank(6, [2, 2, P])
+        turned = [bank(4 + 2 * j, [2, 2, P]) for j in range(2)]
         for h in range(2):
-            round_and_turn_on_gpsimd(h, 0, ca[0][:, h * ROW_WORDS : (h + 1) * ROW_WORDS], turned_block2[:, h])
-        turned_block3 = [bank(4 + h, [2, P]) for h in range(2)]
-        for h in range(2):
-            round_and_turn_on_gpsimd(h, 1, sb[0][:, h * ROW_WORDS : (h + 1) * ROW_WORDS], turned_block3[h])
-        grouped = buffer("grouped2")
-        copy_two_rows(nc.vector.tensor_copy, grouped[:], turned_block2)
+            for j, term in enumerate((cb[0], sa[0])):
+                round_and_turn_on_gpsimd(h, j, term[:, h * ROW_WORDS : (h + 1) * ROW_WORDS], turned[j][:, h])
+        form_d2(1)
+        grouped = buffer("grouped_q2")
+        copy_two_rows(grouped[:], turned[0])
         quantise_q(2, grouped[:])
         grouped = run_of(after_quantiser, SLOTS)
-        for h in range(2):
-            copy_one_row(grouped[:, h * ROW_WORDS : (h + 1) * ROW_WORDS], turned_block3[h])
+        copy_two_rows(grouped, turned[1])
+        products(1, "sb")
         quantise_q(3, grouped)
-        sums.extend(multiply(block, 1, (0, 1)) for block in (2, 3))
-
-        look_up(2)
-        form_d2(1)
         form_d1(1)
-        products(2, "sa ca cb sb")
-        put(1)
-        form_d2(2)
-        form_d1(2)
+        sums.extend(multiply(block, 1, (1, 0)) for block in (2, 3))
 
-        look_up(3)
+        look_up_sin(2)
+        products(2, "cb sa")
+        form_d2(2)
+        put_d2_half(1, 0)
+        look_up_cos(3)
+        put_d2_half(1, 1)
+        look_up_sin(3)
+        put_d1(1)
+        products(2, "ca sb")
+        form_d1(2)
         products(3, "cb sa")
-        put(2)
         form_d2(3)
+        put_d2_half(2, 0)
+        put_d2_half(2, 1)
+        put_d1(2)
         products(3, "ca sb")
-        put(3)
+        put_d2_half(3, 0)
+        put_d2_half(3, 1)
+        put_d1(3)

@@ -97,7 +97,7 @@ def tile_attend_grope_kernel(tc, q1, q2, G, cs, sn, offs, poffs, out_0, out_1):
         load_sin(3)
 
         make_identity(nc, identity[:])
-        windows = [keep.tile([P, TOKENS], F32, name="window%d" % w) for w in range(3)]
+        windows = [keep.tile([P, TOKENS], F32, name="window%d" % w) for w in range(4)]
         for window in windows:
             nc.vector.memset(window[:].bitcast(I32), 0)
 
@@ -178,8 +178,6 @@ def tile_attend_grope_kernel(tc, q1, q2, G, cs, sn, offs, poffs, out_0, out_1):
         quantise_g(0)
         quantise_q(0, grouped_q1[:])
         quantise_g(1)
-        windows.append(place("window3", SLOTS, TOKENS))
-        nc.gpsimd.memset(windows[3][:].bitcast(I32), 0)
         sums = [multiply(0, 2, (1, 0)), multiply(1, 1, (1, 0))]
 
         tail = buffer("tail", 2 * SLOTS)

@@ -39,7 +39,6 @@ def tile_attend_grope_kernel(tc, q1, q2, G, cs, sn, offs, poffs, out_0, out_1):
     nc = tc.nc
     with ExitStack() as ctx:
         keep = ctx.enter_context(tc.tile_pool(name="keep", bufs=1))
-        placed = ctx.enter_context(tc.tile_pool(name="placed", bufs=1))
         psum = ctx.enter_context(tc.psum_pool(name="psum", bufs=1))
 
         def rows(x, block):
@@ -49,16 +48,16 @@ def tile_attend_grope_kernel(tc, q1, q2, G, cs, sn, offs, poffs, out_0, out_1):
         def buffer(tag, columns=SLOTS, dtype=F32):
             return keep.tile([P, columns], dtype, name=tag, tag=tag, align_bytes=64)
 
-        def place(name, start, columns):
-            return placed.tile([P, columns], F32, name=name, offset=start * WORD_BYTES, align_bytes=64)
+        def run_of(tile, start, columns=SLOTS):
+            return tile[:, start : start + columns]
 
         def bank(number, shape):
             return psum.tile([P] + shape, F32, name="bank", tag="bank%d" % number)
 
         token_list = keep.tile([P, SLOTS // BAND], U16, name="token_list")
         position_list = keep.tile([P, SLOTS // BAND], U16, name="position_list")
-        G_RAW = SLOTS + TOKENS
-        g_raw = placed.tile([P, PACK, SLOTS], F32, name="g_raw", offset=G_RAW * WORD_BYTES, align_bytes=64)
+        g_row = buffer("g_row", SLOTS + PACK * SLOTS)
+        g_raw = g_row[:, SLOTS:].rearrange("p (t i) -> p t i", t=PACK)
         cos_table = [buffer("cos_table%d" % block, POSITIONS) for block in range(BLOCKS)]
         sin_table = [buffer("sin_table%d" % block, POSITIONS) for block in range(BLOCKS)]
         identity = keep.tile([P, P], F32, name="identity")
@@ -67,8 +66,11 @@ def tile_attend_grope_kernel(tc, q1, q2, G, cs, sn, offs, poffs, out_0, out_1):
 
         D2A = SLOTS - OVERLAP
         SIN3 = D2A + HALF - OVERLAP
-        late = buffer("late", SIN3 + SLOTS)
-        q_raw = [[buffer("q_raw%d_%d" % (g, h), 2 * QUERIES)[:] for h in range(2)] for g in range(2)]
+        late = buffer("late", 4 * QUERIES)
+        q_raw = [
+            [buffer("q_raw0_%d" % h, 2 * QUERIES)[:] for h in range(2)],
+            [run_of(late, h * 2 * QUERIES, 2 * QUERIES) for h in range(2)],
+        ]
 
         def load_q(g, h):
             q = (q1, q2)[h]
@@ -82,16 +84,16 @@ def tile_attend_grope_kernel(tc, q1, q2, G, cs, sn, offs, poffs, out_0, out_1):
 
         load_q(0, 1)
         load_q(0, 0)
-        nc.sync.dma_start(g_raw[:], G.rearrange("(p t) i -> p t i", t=PACK))
+        nc.sync.dma_start(g_row[:, SLOTS:], G.rearrange("(p t) i -> p (t i)", t=PACK))
         nc.sync.dma_start(position_list[:], poffs)
         load_cos(0)
         load_sin(0)
         load_cos(1)
         load_sin(1)
-        load_cos(2)
         nc.sync.dma_start(token_list[:], offs)
         load_q(1, 0)
         load_q(1, 1)
+        load_cos(2)
         load_sin(2)
         load_cos(3)
         load_sin(3)
@@ -109,10 +111,12 @@ def tile_attend_grope_kernel(tc, q1, q2, G, cs, sn, offs, poffs, out_0, out_1):
             for v in range(2):
                 nc.tensor.transpose(turned[:, v, :], words[:, v * P : (v + 1) * P], identity[:])
 
-        def round_and_turn_on_gpsimd(h, j, words, turned):
-            nc.gpsimd.tensor_scalar(words.bitcast(BF16), q_raw[1][h][:, j * QUERIES : (j + 1) * QUERIES], 1.0, 0.0, MULT, ADD)
-            for v in range(2):
-                nc.tensor.transpose(turned[:, v, :], words[:, v:ROW_WORDS:2], identity[:])
+        def round_and_turn_on_gpsimd(j, words, turned):
+            raw = late[:].rearrange("f (h j r) -> f h j r", h=2, j=2)[:, :, j, :]
+            nc.gpsimd.tensor_scalar(words.bitcast(BF16), raw, 1.0, 0.0, MULT, ADD)
+            for h in range(2):
+                for v in range(2):
+                    nc.tensor.transpose(turned[:, h, v, :], words[:, h, v:ROW_WORDS:2], identity[:])
 
         def copy_two_rows(grouped, turned):
             nc.vector.tensor_copy(grouped.rearrange("p (n f v) -> p n f v", n=2, v=2), turned[:].rearrange("p n v f -> p n f v"))
@@ -127,86 +131,97 @@ def tile_attend_grope_kernel(tc, q1, q2, G, cs, sn, offs, poffs, out_0, out_1):
             cols = slice(call * 2 * P, (call + 1) * 2 * P)
             nc.vector.quantize_mx(out=q_codes[:, cols].bitcast(E4M3), scales=q_scales[:, cols], in_=grouped.bitcast(BF16))
 
-        def multiply(block, parts, order):
+        def multiply(out, block, h, slots):
             g, j = divmod(block, 2)
+            run = 2 * h + j if g == 0 else BLOCKS + 2 * j + h
+            cols = slice(run * P, (run + 1) * P)
+            nc.tensor.matmul_mx(
+                out=out,
+                lhsT=q_codes[:, cols].bitcast(E4M3),
+                lhsT_scale=q_scales[:, cols],
+                rhs=g_codes[:, slots].bitcast(E5M2),
+                rhs_scale=g_scales[:, slots],
+                start=True,
+                stop=True,
+            )
+
+        def multiply_block(block):
             banks = [bank(2 * block + h, [SLOTS]) for h in range(2)]
-            width = SLOTS // parts
-            for part in range(parts):
-                slots = slice(part * width, (part + 1) * width)
-                for h in order:
-                    run = 2 * h + j if g == 0 else BLOCKS + 2 * j + h
-                    cols = slice(run * P, (run + 1) * P)
-                    nc.tensor.matmul_mx(
-                        out=banks[h][:, slots],
-                        lhsT=q_codes[:, cols].bitcast(E4M3),
-                        lhsT_scale=q_scales[:, cols],
-                        rhs=g_codes[:, slots].bitcast(E5M2),
-                        rhs_scale=g_scales[:, slots],
-                        start=True,
-                        stop=True,
-                    )
+            for h in (1, 0):
+                multiply(banks[h][:], block, h, slice(0, SLOTS))
             return banks
 
+        def half(u):
+            return slice(u * HALF, (u + 1) * HALF)
+
+        g_grouped = buffer("g_grouped", 2 * SLOTS)
         turned = bank(4, [2, 2, P])
         for j in range(2):
             round_and_turn_on_scalar(1, j, buffer("rounded1_%d" % j, ROW_WORDS)[:], turned[:, j])
         grouped_q2 = buffer("grouped_q2")
         copy_two_rows(grouped_q2[:], turned)
-        quantise_q(1, grouped_q2[:])
         grouped_q1 = buffer("grouped_q1")
         turned = [bank(5 + j, [2, P]) for j in range(2)]
         round_and_turn_on_scalar(0, 0, buffer("rounded0_0", ROW_WORDS)[:], turned[0])
-        round_and_turn_on_scalar(0, 1, place("last_words", SLOTS, ROW_WORDS)[:], turned[1])
+        round_and_turn_on_scalar(0, 1, run_of(g_grouped, 0, ROW_WORDS), turned[1])
         for j in range(2):
             copy_one_row(grouped_q1[:, j * ROW_WORDS : (j + 1) * ROW_WORDS], turned[j])
 
-        g_grouped = [buffer("grouped_q2"), place("g_second_half", SLOTS, SLOTS)]
-
-        def interleave_g(copy, u, lo, hi):
+        def interleave_g(copy, lo, hi):
             copy(
-                g_grouped[u][:, 2 * lo : 2 * hi].bitcast(BF16).rearrange("p (c i t) -> p c t i", i=4, t=PACK),
-                g_raw[:, :, u * HALF + lo : u * HALF + hi].rearrange("p t (c i) -> p c t i", i=4),
+                g_grouped[:, 2 * lo : 2 * hi].bitcast(BF16).rearrange("p (c i t) -> p c t i", i=4, t=PACK),
+                g_raw[:, :, lo:hi].rearrange("p t (c i) -> p c t i", i=4),
             )
 
         def quantise_g(u):
-            cols = slice(u * HALF, (u + 1) * HALF)
-            nc.vector.quantize_mx(out=g_codes[:, cols].bitcast(E5M2), scales=g_scales[:, cols], in_=g_grouped[u][:].bitcast(BF16))
+            nc.vector.quantize_mx(
+                out=g_codes[:, half(u)].bitcast(E5M2), scales=g_scales[:, half(u)], in_=run_of(g_grouped, u * SLOTS).bitcast(BF16)
+            )
 
-        interleave_g(nc.vector.tensor_copy, 0, 0, HALF)
-        interleave_g(nc.vector.tensor_copy, 1, 0, HALF // 4)
-        interleave_g(nc.scalar.copy, 1, HALF // 4, HALF)
-        quantise_g(0)
-        quantise_q(0, grouped_q1[:])
+        SCALAR_SHARE = 3 * SLOTS // 8
+        interleave_g(nc.scalar.copy, 0, SCALAR_SHARE)
+        interleave_g(nc.vector.tensor_copy, HALF, SLOTS)
+        interleave_g(nc.vector.tensor_copy, SCALAR_SHARE, HALF)
+        quantise_q(1, grouped_q2[:])
         quantise_g(1)
-        sums = [multiply(0, 2, (1, 0)), multiply(1, 1, (1, 0))]
+        quantise_q(0, grouped_q1[:])
+        quantise_g(0)
+        first_sums = [bank(u, [2, HALF]) for u in range(2)]
+        for u in (1, 0):
+            for h in (1, 0):
+                multiply(first_sums[u][:, h, :], 0, h, half(u))
+        sums = [None, multiply_block(1)]
 
         tail = buffer("tail", 2 * SLOTS)
-        after_d2 = buffer("after_d2", 4 * SLOTS)
-        first_angles = place("first_angles", G_RAW, 5 * SLOTS)
-        after_block0 = buffer("after_block0", 2 * SLOTS)
-        around_block3 = buffer("around_block3", 2 * SLOTS)
-
-        def run_of(tile, start):
-            return tile[:, start : start + SLOTS]
-
-        cos = [run_of(first_angles, 2 * block * SLOTS) for block in range(LAST)] + [run_of(late, 0)]
-        sin = [run_of(first_angles, SLOTS), run_of(first_angles, 3 * SLOTS), run_of(after_block0, OVERLAP), run_of(late, SIN3)]
-
-        cb = [buffer("cb0")[:], buffer("cb1")[:], run_of(after_d2, SLOTS - OVERLAP), run_of(after_d2, 2 * SLOTS)]
-        sa = [run_of(around_block3, SLOTS), buffer("sa1")[:], run_of(after_d2, 3 * SLOTS - OVERLAP), run_of(after_d2, 3 * SLOTS)]
-        ca = [buffer("ca0")[:], buffer("ca1")[:], run_of(after_d2, 0), tail[:, 0:SLOTS]]
-        sb = [buffer("sb0")[:], run_of(around_block3, OVERLAP), run_of(after_d2, SLOTS), tail[:, SLOTS : 2 * SLOTS]]
+        early = buffer("early", SIN3 + SLOTS)
         after_quantiser = buffer("after_quantiser", 2 * SLOTS)
+        cos = [run_of(g_row, OVERLAP), run_of(g_row, 3 * SLOTS), run_of(early, 0), run_of(late, 0)]
+        sin = [run_of(g_row, 2 * SLOTS), run_of(g_row, 4 * SLOTS), run_of(early, SIN3), run_of(late, SIN3)]
+        by_cos, by_sin = [buffer(tag, 2 * SLOTS)[:].rearrange("p (u h n) -> p u h n", u=2, h=2) for tag in ("by_cos", "by_sin")]
+        cb = [None] + [buffer("cb%d" % block)[:] for block in range(1, BLOCKS)]
+        sa = [None] + [buffer("sa%d" % block)[:] for block in range(1, BLOCKS)]
+        ca = [None, buffer("ca1")[:], buffer("ca2")[:], tail[:, 0:SLOTS]]
+        sb = [None, buffer("sb1")[:], buffer("sb2")[:], tail[:, SLOTS : 2 * SLOTS]]
         d1 = [buffer("d1_0")[:], run_of(after_quantiser, OVERLAP), tail[:, HALF : HALF + SLOTS]]
-
-        d2 = [[run[:, 0:HALF], run[:, HALF:SLOTS]] for run in (run_of(after_block0, SLOTS), buffer("d2_2")[:], buffer("d2_3")[:])]
-        d2.insert(1, [late[:, D2A : D2A + HALF], buffer("d2_1", HALF)[:]])
+        d2 = [
+            [buffer("d2_0", HALF)[:], run_of(early, D2A, HALF)],
+            [run_of(late, D2A, HALF), run_of(late, 4 * QUERIES - HALF, HALF)],
+        ] + [[run[:, half(u)] for u in range(2)] for run in (buffer("d2_2")[:], buffer("d2_3")[:])]
 
         def look_up_cos(block):
             nc.scalar.activation(cos[block], cos_table[block][:].indirect(position_list[:]), COPY)
 
         def look_up_sin(block):
             nc.scalar.activation(sin[block], sin_table[block][:].indirect(position_list[:]), COPY)
+
+        def first_products(terms, angle):
+            for u in (1, 0):
+                nc.vector.tensor_tensor(
+                    terms[:, u],
+                    first_sums[u][:],
+                    angle[:, half(u)].unsqueeze(1).to_broadcast([P, 2, HALF]),
+                    MULT,
+                )
 
         def products(block, names):
             a_sum, b_sum = sums[block]
@@ -215,25 +230,28 @@ def tile_attend_grope_kernel(tc, q1, q2, G, cs, sn, offs, poffs, out_0, out_1):
                 term, acc, angle = steps[name]
                 nc.vector.tensor_tensor(term[block], acc[:], angle[block], MULT)
 
+        def form_first_d2(u):
+            nc.gpsimd.tensor_tensor(d2[0][u], by_cos[:, u, 1], by_sin[:, u, 0], SUBTRACT)
+
+        def form_first_d1():
+            nc.gpsimd.tensor_tensor(d1[0].rearrange("p (u n) -> p u n", u=2), by_cos[:, :, 0], by_sin[:, :, 1], ADD)
+
         def form_d2(block):
             for u in range(2):
-                cols = slice(u * HALF, (u + 1) * HALF)
-                nc.gpsimd.tensor_tensor(d2[block][u], cb[block][:, cols], sa[block][:, cols], SUBTRACT)
+                nc.gpsimd.tensor_tensor(d2[block][u], cb[block][:, half(u)], sa[block][:, half(u)], SUBTRACT)
 
         def form_d1(block):
             nc.gpsimd.tensor_tensor(d1[block], ca[block], sb[block], ADD)
 
-        scalar_window = [0, 2, 1, 2]
-        vector_window = [1, 3, 0, 3]
-
         def put_d2_half(block, u):
-            window = windows[scalar_window[block]]
+            window = windows[2 * (block % 2)]
             nc.scalar.activation(window[:].indirect(token_list[:, u * HALF // BAND : (u + 1) * HALF // BAND]), d2[block][u], COPY)
-            if u == 1:
-                nc.sync.dma_start(rows(out_1, block), window[:])
+
+        def store_d2(block):
+            nc.sync.dma_start(rows(out_1, block), windows[2 * (block % 2)][:])
 
         def put_d1(block):
-            window = windows[vector_window[block]]
+            window = windows[2 * (block % 2) + 1]
             if block < LAST:
                 nc.vector.tensor_copy(window[:].indirect(token_list[:]), d1[block])
             else:
@@ -242,48 +260,50 @@ def tile_attend_grope_kernel(tc, q1, q2, G, cs, sn, offs, poffs, out_0, out_1):
 
         look_up_cos(0)
         look_up_sin(0)
-        products(0, "cb ca sa sb")
-        form_d2(0)
-        form_d1(0)
+        first_products(by_cos, cos[0])
+        first_products(by_sin, sin[0])
+        form_first_d2(1)
+        form_first_d2(0)
+        form_first_d1()
         look_up_cos(1)
         look_up_sin(1)
-        products(1, "cb ca sa")
+        products(1, "cb ca sa sb")
+        put_d2_half(0, 1)
+        put_d2_half(0, 0)
+        store_d2(0)
         look_up_cos(2)
         put_d1(0)
-        put_d2_half(0, 0)
-        put_d2_half(0, 1)
 
         turned = [bank(4 + 2 * j, [2, 2, P]) for j in range(2)]
-        for h in range(2):
-            for j, term in enumerate((cb[0], sa[0])):
-                round_and_turn_on_gpsimd(h, j, term[:, h * ROW_WORDS : (h + 1) * ROW_WORDS], turned[j][:, h])
+        for j, words in enumerate((by_cos[:, :, 0], by_sin[:, :, 1])):
+            round_and_turn_on_gpsimd(j, words, turned[j])
         form_d2(1)
-        grouped = buffer("grouped_q2")
-        copy_two_rows(grouped[:], turned[0])
-        quantise_q(2, grouped[:])
-        grouped = run_of(after_quantiser, SLOTS)
-        copy_two_rows(grouped, turned[1])
-        products(1, "sb")
-        quantise_q(3, grouped)
+        grouped = [buffer("grouped_q2")[:], run_of(after_quantiser, SLOTS)]
+        for j in range(2):
+            copy_two_rows(grouped[j], turned[j])
+        for j in range(2):
+            quantise_q(2 + j, grouped[j])
         form_d1(1)
-        sums.extend(multiply(block, 1, (1, 0)) for block in (2, 3))
+        sums.extend(multiply_block(block) for block in (2, 3))
 
         look_up_sin(2)
-        products(2, "cb sa")
+        products(2, "cb sa ca sb")
         form_d2(2)
+        form_d1(2)
         put_d2_half(1, 0)
         look_up_cos(3)
         put_d2_half(1, 1)
+        store_d2(1)
         look_up_sin(3)
         put_d1(1)
-        products(2, "ca sb")
-        form_d1(2)
         products(3, "cb sa")
         form_d2(3)
         put_d2_half(2, 0)
         put_d2_half(2, 1)
+        store_d2(2)
         put_d1(2)
         products(3, "ca sb")
         put_d2_half(3, 0)
         put_d2_half(3, 1)
+        store_d2(3)
         put_d1(3)

@@ -66,15 +66,16 @@ def tile_attend_grope_kernel(tc, q1, q2, G, cs, sn, offs, poffs, out_0, out_1):
 
         D2A = SLOTS - OVERLAP
         SIN3 = D2A + HALF - OVERLAP
+        LATE = SLOTS + 2 * OVERLAP
         late = buffer("late", 4 * QUERIES)
         q_raw = [
             [buffer("q_raw0_%d" % h, 2 * QUERIES)[:] for h in range(2)],
-            [run_of(late, h * 2 * QUERIES, 2 * QUERIES) for h in range(2)],
+            [late[:].rearrange("f (j h r) -> f h j r", j=2, h=2)[:, h] for h in range(2)],
         ]
 
         def load_q(g, h):
-            q = (q1, q2)[h]
-            nc.sync.dma_start(q_raw[g][h], q[g * 2 * P : (g + 1) * 2 * P, :].rearrange("(p j) r -> p (j r)", j=2))
+            q = (q1, q2)[h][g * 2 * P : (g + 1) * 2 * P, :]
+            nc.sync.dma_start(q_raw[g][h], q.rearrange("(p j) r -> p j r" if g else "(p j) r -> p (j r)", j=2))
 
         def load_cos(block):
             nc.sync.dma_start(cos_table[block][:], rows(cs, block))
@@ -112,11 +113,10 @@ def tile_attend_grope_kernel(tc, q1, q2, G, cs, sn, offs, poffs, out_0, out_1):
                 nc.tensor.transpose(turned[:, v, :], words[:, v * P : (v + 1) * P], identity[:])
 
         def round_and_turn_on_gpsimd(j, words, turned):
-            raw = late[:].rearrange("f (h j r) -> f h j r", h=2, j=2)[:, :, j, :]
-            nc.gpsimd.tensor_scalar(words.bitcast(BF16), raw, 1.0, 0.0, MULT, ADD)
+            nc.gpsimd.tensor_scalar(words.bitcast(BF16), run_of(late, j * 2 * QUERIES, 2 * QUERIES), 1.0, 0.0, MULT, ADD)
             for h in range(2):
                 for v in range(2):
-                    nc.tensor.transpose(turned[:, h, v, :], words[:, h, v:ROW_WORDS:2], identity[:])
+                    nc.tensor.transpose(turned[:, h, v, :], words[:, h * ROW_WORDS + v : (h + 1) * ROW_WORDS : 2], identity[:])
 
         def copy_two_rows(grouped, turned):
             nc.vector.tensor_copy(grouped.rearrange("p (n f v) -> p n f v", n=2, v=2), turned[:].rearrange("p n v f -> p n f v"))
@@ -195,9 +195,9 @@ def tile_attend_grope_kernel(tc, q1, q2, G, cs, sn, offs, poffs, out_0, out_1):
         tail = buffer("tail", 2 * SLOTS)
         early = buffer("early", SIN3 + SLOTS)
         after_quantiser = buffer("after_quantiser", 2 * SLOTS)
-        cos = [run_of(g_row, OVERLAP), run_of(g_row, 3 * SLOTS), run_of(early, 0), run_of(late, 0)]
-        sin = [run_of(g_row, 2 * SLOTS), run_of(g_row, 4 * SLOTS), run_of(early, SIN3), run_of(late, SIN3)]
-        by_cos, by_sin = [buffer(tag, 2 * SLOTS)[:].rearrange("p (u h n) -> p u h n", u=2, h=2) for tag in ("by_cos", "by_sin")]
+        cos = [run_of(g_row, OVERLAP), run_of(g_row, 3 * SLOTS), run_of(early, 0), run_of(late, LATE)]
+        sin = [run_of(g_row, 2 * SLOTS), run_of(g_row, 4 * SLOTS), run_of(early, SIN3), run_of(late, LATE + SIN3)]
+        by_cos, by_sin = [buffer(tag, 2 * SLOTS) for tag in ("by_cos", "by_sin")]
         cb = [None] + [buffer("cb%d" % block)[:] for block in range(1, BLOCKS)]
         sa = [None] + [buffer("sa%d" % block)[:] for block in range(1, BLOCKS)]
         ca = [None, buffer("ca1")[:], buffer("ca2")[:], tail[:, 0:SLOTS]]
@@ -205,7 +205,7 @@ def tile_attend_grope_kernel(tc, q1, q2, G, cs, sn, offs, poffs, out_0, out_1):
         d1 = [buffer("d1_0")[:], run_of(after_quantiser, OVERLAP), tail[:, HALF : HALF + SLOTS]]
         d2 = [
             [buffer("d2_0", HALF)[:], run_of(early, D2A, HALF)],
-            [run_of(late, D2A, HALF), run_of(late, 4 * QUERIES - HALF, HALF)],
+            [run_of(late, LATE + D2A, HALF), run_of(late, 4 * QUERIES - HALF, HALF)],
         ] + [[run[:, half(u)] for u in range(2)] for run in (buffer("d2_2")[:], buffer("d2_3")[:])]
 
         def look_up_cos(block):
@@ -217,7 +217,7 @@ def tile_attend_grope_kernel(tc, q1, q2, G, cs, sn, offs, poffs, out_0, out_1):
         def first_products(terms, angle):
             for u in (1, 0):
                 nc.vector.tensor_tensor(
-                    terms[:, u],
+                    terms[:].rearrange("p (h u n) -> p u h n", u=2, h=2)[:, u],
                     first_sums[u][:],
                     angle[:, half(u)].unsqueeze(1).to_broadcast([P, 2, HALF]),
                     MULT,
@@ -231,10 +231,10 @@ def tile_attend_grope_kernel(tc, q1, q2, G, cs, sn, offs, poffs, out_0, out_1):
                 nc.vector.tensor_tensor(term[block], acc[:], angle[block], MULT)
 
         def form_first_d2(u):
-            nc.gpsimd.tensor_tensor(d2[0][u], by_cos[:, u, 1], by_sin[:, u, 0], SUBTRACT)
+            nc.gpsimd.tensor_tensor(d2[0][u], run_of(by_cos, SLOTS + u * HALF, HALF), run_of(by_sin, u * HALF, HALF), SUBTRACT)
 
         def form_first_d1():
-            nc.gpsimd.tensor_tensor(d1[0].rearrange("p (u n) -> p u n", u=2), by_cos[:, :, 0], by_sin[:, :, 1], ADD)
+            nc.gpsimd.tensor_tensor(d1[0], run_of(by_cos, 0), run_of(by_sin, SLOTS), ADD)
 
         def form_d2(block):
             for u in range(2):
@@ -275,7 +275,7 @@ def tile_attend_grope_kernel(tc, q1, q2, G, cs, sn, offs, poffs, out_0, out_1):
         put_d1(0)
 
         turned = [bank(4 + 2 * j, [2, 2, P]) for j in range(2)]
-        for j, words in enumerate((by_cos[:, :, 0], by_sin[:, :, 1])):
+        for j, words in enumerate((run_of(by_cos, 0), run_of(by_sin, SLOTS))):
             round_and_turn_on_gpsimd(j, words, turned[j])
         form_d2(1)
         grouped = [buffer("grouped_q2")[:], run_of(after_quantiser, SLOTS)]

@@ -30,6 +30,7 @@ HALF = SLOTS // 2
 QUARTER = SLOTS // 4
 ROW_WORDS = QUERIES // 2
 WORD_BYTES = 4
+VECTOR_SHARE = 3 * SLOTS // 8
 OVERLAP = 16
 
 FLOPS = 2 * 2 * FEATURES * QUERIES * SLOTS
@@ -39,6 +40,7 @@ def tile_attend_grope_kernel(tc, q1, q2, G, cs, sn, offs, poffs, out_0, out_1):
     nc = tc.nc
     with ExitStack() as ctx:
         keep = ctx.enter_context(tc.tile_pool(name="keep", bufs=1))
+        placed = ctx.enter_context(tc.tile_pool(name="placed", bufs=1))
         psum = ctx.enter_context(tc.psum_pool(name="psum", bufs=1))
 
         def rows(x, block):
@@ -48,6 +50,9 @@ def tile_attend_grope_kernel(tc, q1, q2, G, cs, sn, offs, poffs, out_0, out_1):
         def buffer(tag, columns=SLOTS, dtype=F32):
             return keep.tile([P, columns], dtype, name=tag, tag=tag, align_bytes=64)
 
+        def place(name, start, columns):
+            return placed.tile([P, columns], F32, name=name, offset=start * WORD_BYTES, align_bytes=64)
+
         def run_of(tile, start, columns=SLOTS):
             return tile[:, start : start + columns]
 
@@ -56,8 +61,8 @@ def tile_attend_grope_kernel(tc, q1, q2, G, cs, sn, offs, poffs, out_0, out_1):
 
         token_list = keep.tile([P, SLOTS // BAND], U16, name="token_list")
         position_list = keep.tile([P, SLOTS // BAND], U16, name="position_list")
-        g_row = buffer("g_row", SLOTS + PACK * SLOTS)
-        g_raw = g_row[:, SLOTS:].rearrange("p (t i) -> p t i", t=PACK)
+        g_row = buffer("g_row", PACK * SLOTS)
+        g_raw = g_row[:].rearrange("p (t u i) -> p u t i", t=PACK, u=2)
         cos_table = [buffer("cos_table%d" % block, POSITIONS) for block in range(BLOCKS)]
         sin_table = [buffer("sin_table%d" % block, POSITIONS) for block in range(BLOCKS)]
         identity = keep.tile([P, P], F32, name="identity")
@@ -66,11 +71,11 @@ def tile_attend_grope_kernel(tc, q1, q2, G, cs, sn, offs, poffs, out_0, out_1):
 
         D2A = SLOTS - OVERLAP
         SIN3 = D2A + HALF - OVERLAP
-        LATE = SLOTS + 2 * OVERLAP
-        late = buffer("late", 4 * QUERIES)
+        LATE = SLOTS - OVERLAP
+        late = buffer("late", SLOTS + 4 * QUERIES)
         q_raw = [
             [buffer("q_raw0_%d" % h, 2 * QUERIES)[:] for h in range(2)],
-            [late[:].rearrange("f (j h r) -> f h j r", j=2, h=2)[:, h] for h in range(2)],
+            [run_of(late, SLOTS, 4 * QUERIES).rearrange("f (j h r) -> f h j r", j=2, h=2)[:, h] for h in range(2)],
         ]
 
         def load_q(g, h):
@@ -83,9 +88,13 @@ def tile_attend_grope_kernel(tc, q1, q2, G, cs, sn, offs, poffs, out_0, out_1):
         def load_sin(block):
             nc.sync.dma_start(sin_table[block][:], rows(sn, block))
 
-        load_q(0, 1)
+        def load_g(u):
+            nc.sync.dma_start(run_of(g_row, u * 2 * SLOTS, 2 * SLOTS), run_of(G.rearrange("(p t) i -> p (t i)", t=PACK), u * 2 * SLOTS, 2 * SLOTS))
+
         load_q(0, 0)
-        nc.sync.dma_start(g_row[:, SLOTS:], G.rearrange("(p t) i -> p (t i)", t=PACK))
+        load_q(0, 1)
+        load_g(0)
+        load_g(1)
         nc.sync.dma_start(position_list[:], poffs)
         load_cos(0)
         load_sin(0)
@@ -113,16 +122,16 @@ def tile_attend_grope_kernel(tc, q1, q2, G, cs, sn, offs, poffs, out_0, out_1):
                 nc.tensor.transpose(turned[:, v, :], words[:, v * P : (v + 1) * P], identity[:])
 
         def round_and_turn_on_gpsimd(j, words, turned):
-            nc.gpsimd.tensor_scalar(words.bitcast(BF16), run_of(late, j * 2 * QUERIES, 2 * QUERIES), 1.0, 0.0, MULT, ADD)
+            nc.gpsimd.tensor_scalar(words.bitcast(BF16), run_of(late, SLOTS + j * 2 * QUERIES, 2 * QUERIES), 1.0, 0.0, MULT, ADD)
             for h in range(2):
                 for v in range(2):
-                    nc.tensor.transpose(turned[:, h, v, :], words[:, h * ROW_WORDS + v : (h + 1) * ROW_WORDS : 2], identity[:])
+                    nc.tensor.transpose(turned[h][:, v, :], words[:, h * ROW_WORDS + v : (h + 1) * ROW_WORDS : 2], identity[:])
 
         def copy_two_rows(grouped, turned):
             nc.vector.tensor_copy(grouped.rearrange("p (n f v) -> p n f v", n=2, v=2), turned[:].rearrange("p n v f -> p n f v"))
 
         def copy_one_row(grouped, turned):
-            nc.scalar.copy(grouped.rearrange("p (f v) -> p f v", v=2), turned[:].rearrange("p v f -> p f v"))
+            nc.vector.tensor_copy(grouped.rearrange("p (f v) -> p f v", v=2), turned[:].rearrange("p v f -> p f v"))
 
         q_codes = buffer("q_codes", 2 * BLOCKS * P, U32)
         q_scales = buffer("q_scales", 2 * BLOCKS * P, U8)
@@ -154,59 +163,69 @@ def tile_attend_grope_kernel(tc, q1, q2, G, cs, sn, offs, poffs, out_0, out_1):
         def half(u):
             return slice(u * HALF, (u + 1) * HALF)
 
-        g_grouped = buffer("g_grouped", 2 * SLOTS)
         turned = bank(4, [2, 2, P])
         for j in range(2):
-            round_and_turn_on_scalar(1, j, buffer("rounded1_%d" % j, ROW_WORDS)[:], turned[:, j])
-        grouped_q2 = buffer("grouped_q2")
-        copy_two_rows(grouped_q2[:], turned)
-        grouped_q1 = buffer("grouped_q1")
+            round_and_turn_on_scalar(0, j, buffer("rounded0_%d" % j, ROW_WORDS)[:], turned[:, j])
+        grouped = buffer("grouped0")
+        copy_two_rows(grouped[:], turned)
+        quantise_q(0, grouped[:])
+        grouped = buffer("grouped1")
         turned = [bank(5 + j, [2, P]) for j in range(2)]
-        round_and_turn_on_scalar(0, 0, buffer("rounded0_0", ROW_WORDS)[:], turned[0])
-        round_and_turn_on_scalar(0, 1, run_of(g_grouped, 0, ROW_WORDS), turned[1])
+        round_and_turn_on_scalar(1, 0, buffer("rounded1_0", ROW_WORDS)[:], turned[0])
+        round_and_turn_on_scalar(1, 1, place("last_words", 4 * SLOTS - P, ROW_WORDS)[:], turned[1])
         for j in range(2):
-            copy_one_row(grouped_q1[:, j * ROW_WORDS : (j + 1) * ROW_WORDS], turned[j])
+            copy_one_row(grouped[:, j * ROW_WORDS : (j + 1) * ROW_WORDS], turned[j])
+        quantise_q(1, grouped[:])
 
-        def interleave_g(copy, lo, hi):
-            copy(
-                g_grouped[:, 2 * lo : 2 * hi].bitcast(BF16).rearrange("p (c i t) -> p c t i", i=4, t=PACK),
-                g_raw[:, :, lo:hi].rearrange("p t (c i) -> p c t i", i=4),
+        second_half = place("second_half", 4 * SLOTS, 3 * SLOTS)
+        g_grouped = [place("first_half", 4 * SLOTS, SLOTS), second_half]
+
+        def interleave_g(u, lo, hi):
+            nc.vector.tensor_copy(
+                g_grouped[u][:, 2 * lo : 2 * hi].bitcast(BF16).rearrange("p (c i t) -> p c t i", i=4, t=PACK),
+                g_raw[:, u, :, lo:hi].rearrange("p t (c i) -> p c t i", i=4),
             )
 
-        def quantise_g(u):
+        def quantise_g(u, lo, hi):
+            cols = slice(u * HALF + lo, u * HALF + hi)
             nc.vector.quantize_mx(
-                out=g_codes[:, half(u)].bitcast(E5M2), scales=g_scales[:, half(u)], in_=run_of(g_grouped, u * SLOTS).bitcast(BF16)
+                out=g_codes[:, cols].bitcast(E5M2), scales=g_scales[:, cols], in_=g_grouped[u][:, 2 * lo : 2 * hi].bitcast(BF16)
             )
 
-        SCALAR_SHARE = 3 * SLOTS // 8
-        interleave_g(nc.scalar.copy, 0, SCALAR_SHARE)
-        interleave_g(nc.vector.tensor_copy, HALF, SLOTS)
-        interleave_g(nc.vector.tensor_copy, SCALAR_SHARE, HALF)
-        quantise_q(1, grouped_q2[:])
-        quantise_g(1)
-        quantise_q(0, grouped_q1[:])
-        quantise_g(0)
+        interleave_g(0, 0, HALF)
+        quantise_g(0, 0, HALF)
+        for step in (interleave_g, quantise_g):
+            step(1, QUARTER, HALF)
+            step(1, 0, QUARTER)
         first_sums = [bank(u, [2, HALF]) for u in range(2)]
-        for u in (1, 0):
-            for h in (1, 0):
+        for u in range(2):
+            for h in range(2):
                 multiply(first_sums[u][:, h, :], 0, h, half(u))
         sums = [None, multiply_block(1)]
 
         tail = buffer("tail", 2 * SLOTS)
         early = buffer("early", SIN3 + SLOTS)
         after_quantiser = buffer("after_quantiser", 2 * SLOTS)
-        cos = [run_of(g_row, OVERLAP), run_of(g_row, 3 * SLOTS), run_of(early, 0), run_of(late, LATE)]
-        sin = [run_of(g_row, 2 * SLOTS), run_of(g_row, 4 * SLOTS), run_of(early, SIN3), run_of(late, LATE + SIN3)]
-        by_cos, by_sin = [buffer(tag, 2 * SLOTS) for tag in ("by_cos", "by_sin")]
-        cb = [None] + [buffer("cb%d" % block)[:] for block in range(1, BLOCKS)]
+        around_block2 = buffer("around_block2", 3 * SLOTS)
+        after_d1 = buffer("after_d1", 2 * SLOTS)
+        first_angles = place("first_angles", 0, 4 * SLOTS)
+        cos = [run_of(first_angles, 0), run_of(first_angles, 2 * SLOTS), run_of(early, 0), run_of(late, LATE)]
+        sin = [run_of(first_angles, SLOTS), run_of(first_angles, 3 * SLOTS), run_of(early, SIN3), run_of(after_d1, 0)]
+        by_cos, by_sin = run_of(second_half, SLOTS - OVERLAP, 2 * SLOTS), buffer("by_sin", 2 * SLOTS)[:]
+        cb = [None, buffer("cb1")[:], run_of(late, 0), buffer("cb3")[:]]
         sa = [None] + [buffer("sa%d" % block)[:] for block in range(1, BLOCKS)]
-        ca = [None, buffer("ca1")[:], buffer("ca2")[:], tail[:, 0:SLOTS]]
-        sb = [None, buffer("sb1")[:], buffer("sb2")[:], tail[:, SLOTS : 2 * SLOTS]]
-        d1 = [buffer("d1_0")[:], run_of(after_quantiser, OVERLAP), tail[:, HALF : HALF + SLOTS]]
+        ca = [None, run_of(after_d1, SLOTS - OVERLAP), buffer("ca2")[:], tail[:, 0:SLOTS]]
+        sb = [None, run_of(around_block2, 0), buffer("sb2")[:], tail[:, SLOTS : 2 * SLOTS]]
+        d1 = [buffer("d1_0")[:], run_of(after_quantiser, OVERLAP), buffer("d1_2")[:]]
         d2 = [
-            [buffer("d2_0", HALF)[:], run_of(early, D2A, HALF)],
-            [run_of(late, LATE + D2A, HALF), run_of(late, 4 * QUERIES - HALF, HALF)],
-        ] + [[run[:, half(u)] for u in range(2)] for run in (buffer("d2_2")[:], buffer("d2_3")[:])]
+            [run_of(early, D2A, HALF), buffer("d2_0", HALF)[:]],
+            [run_of(late, LATE + D2A, HALF), run_of(around_block2, 2 * (SLOTS - OVERLAP), HALF)],
+            [buffer("d2_2", HALF)[:], run_of(tail, SLOTS - QUARTER, HALF)],
+            [buffer("d2_3_%d" % u, HALF)[:] for u in range(2)],
+        ]
+
+        def entries(listed, u):
+            return listed[:, u * HALF // BAND : (u + 1) * HALF // BAND]
 
         def look_up_cos(block):
             nc.scalar.activation(cos[block], cos_table[block][:].indirect(position_list[:]), COPY)
@@ -214,10 +233,10 @@ def tile_attend_grope_kernel(tc, q1, q2, G, cs, sn, offs, poffs, out_0, out_1):
         def look_up_sin(block):
             nc.scalar.activation(sin[block], sin_table[block][:].indirect(position_list[:]), COPY)
 
-        def first_products(terms, angle):
-            for u in (1, 0):
+        def first_products(u):
+            for terms, angle in ((by_cos, cos[0]), (by_sin, sin[0])):
                 nc.vector.tensor_tensor(
-                    terms[:].rearrange("p (h u n) -> p u h n", u=2, h=2)[:, u],
+                    terms.rearrange("p (h u n) -> p u h n", u=2, h=2)[:, u],
                     first_sums[u][:],
                     angle[:, half(u)].unsqueeze(1).to_broadcast([P, 2, HALF]),
                     MULT,
@@ -233,25 +252,31 @@ def tile_attend_grope_kernel(tc, q1, q2, G, cs, sn, offs, poffs, out_0, out_1):
         def form_first_d2(u):
             nc.gpsimd.tensor_tensor(d2[0][u], run_of(by_cos, SLOTS + u * HALF, HALF), run_of(by_sin, u * HALF, HALF), SUBTRACT)
 
-        def form_first_d1():
-            nc.gpsimd.tensor_tensor(d1[0], run_of(by_cos, 0), run_of(by_sin, SLOTS), ADD)
+        def form_first_d1(u):
+            nc.gpsimd.tensor_tensor(d1[0][:, half(u)], run_of(by_cos, u * HALF, HALF), run_of(by_sin, SLOTS + u * HALF, HALF), ADD)
+
+        def form_d2_half(block, u):
+            nc.gpsimd.tensor_tensor(d2[block][u], cb[block][:, half(u)], sa[block][:, half(u)], SUBTRACT)
 
         def form_d2(block):
             for u in range(2):
-                nc.gpsimd.tensor_tensor(d2[block][u], cb[block][:, half(u)], sa[block][:, half(u)], SUBTRACT)
+                form_d2_half(block, u)
 
         def form_d1(block):
             nc.gpsimd.tensor_tensor(d1[block], ca[block], sb[block], ADD)
 
+        scalar_windows = [windows[w] for w in (0, 2, 1, 2)]
+        vector_windows = [windows[w] for w in (1, 3, 0, 3)]
+
         def put_d2_half(block, u):
-            window = windows[2 * (block % 2)]
-            nc.scalar.activation(window[:].indirect(token_list[:, u * HALF // BAND : (u + 1) * HALF // BAND]), d2[block][u], COPY)
+            window = scalar_windows[block]
+            nc.scalar.activation(window[:].indirect(entries(token_list, u)), d2[block][u], COPY)
 
         def store_d2(block):
-            nc.sync.dma_start(rows(out_1, block), windows[2 * (block % 2)][:])
+            nc.sync.dma_start(rows(out_1, block), scalar_windows[block][:])
 
         def put_d1(block):
-            window = windows[2 * (block % 2) + 1]
+            window = vector_windows[block]
             if block < LAST:
                 nc.vector.tensor_copy(window[:].indirect(token_list[:]), d1[block])
             else:
@@ -259,30 +284,37 @@ def tile_attend_grope_kernel(tc, q1, q2, G, cs, sn, offs, poffs, out_0, out_1):
             nc.sync.dma_start(rows(out_0, block), window[:])
 
         look_up_cos(0)
-        look_up_sin(0)
-        first_products(by_cos, cos[0])
-        first_products(by_sin, sin[0])
-        form_first_d2(1)
+        for u in range(2):
+            nc.scalar.activation(sin[0][:, half(u)], sin_table[0][:].indirect(entries(position_list, u)), COPY)
+        first_products(0)
         form_first_d2(0)
-        form_first_d1()
+        form_first_d1(0)
+        first_products(1)
+        form_first_d1(1)
+        form_first_d2(1)
         look_up_cos(1)
         look_up_sin(1)
-        products(1, "cb ca sa sb")
-        put_d2_half(0, 1)
+        products(1, "cb ca sa")
         put_d2_half(0, 0)
+        put_d2_half(0, 1)
         store_d2(0)
         look_up_cos(2)
         put_d1(0)
 
-        turned = [bank(4 + 2 * j, [2, 2, P]) for j in range(2)]
-        for j, words in enumerate((run_of(by_cos, 0), run_of(by_sin, SLOTS))):
-            round_and_turn_on_gpsimd(j, words, turned[j])
-        form_d2(1)
-        grouped = [buffer("grouped_q2")[:], run_of(after_quantiser, SLOTS)]
-        for j in range(2):
-            copy_two_rows(grouped[j], turned[j])
-        for j in range(2):
-            quantise_q(2 + j, grouped[j])
+        turned_block2 = bank(6, [2, 2, P])
+        round_and_turn_on_gpsimd(0, run_of(by_cos, 0), [turned_block2[:, h] for h in range(2)])
+        turned_block3 = [bank(h, [2, P]) for h in range(2)]
+        round_and_turn_on_gpsimd(1, run_of(by_sin, SLOTS), turned_block3)
+        form_d2_half(1, 0)
+        grouped = run_of(around_block2, SLOTS - OVERLAP)
+        copy_two_rows(grouped, turned_block2)
+        quantise_q(2, grouped)
+        form_d2_half(1, 1)
+        grouped = run_of(after_quantiser, SLOTS)
+        copy_one_row(grouped[:, 0:ROW_WORDS], turned_block3[0])
+        products(1, "sb")
+        copy_one_row(grouped[:, ROW_WORDS:SLOTS], turned_block3[1])
+        quantise_q(3, grouped)
         form_d1(1)
         sums.extend(multiply_block(block) for block in (2, 3))
 
@@ -291,12 +323,13 @@ def tile_attend_grope_kernel(tc, q1, q2, G, cs, sn, offs, poffs, out_0, out_1):
         form_d2(2)
         form_d1(2)
         put_d2_half(1, 0)
-        look_up_cos(3)
         put_d2_half(1, 1)
         store_d2(1)
+        nc.scalar.activation(cos[LAST][:, VECTOR_SHARE:], cos_table[LAST][:].indirect(position_list[:, VECTOR_SHARE // BAND :]), COPY)
         look_up_sin(3)
         put_d1(1)
-        products(3, "cb sa")
+        nc.vector.tensor_copy(cos[LAST][:, :VECTOR_SHARE], cos_table[LAST][:].indirect(position_list[:, : VECTOR_SHARE // BAND]))
+        products(3, "sa cb")
         form_d2(3)
         put_d2_half(2, 0)
         put_d2_half(2, 1)

@@ -24,13 +24,11 @@ SLOTS = 512
 POSITIONS = 1024
 TOKENS = 2048
 BLOCKS = FEATURES // P
-LAST = BLOCKS - 1
 BAND = 16
 HALF = SLOTS // 2
 QUARTER = SLOTS // 4
 ROW_WORDS = QUERIES // 2
 WORD_BYTES = 4
-VECTOR_SHARE = 3 * SLOTS // 8
 OVERLAP = 16
 
 FLOPS = 2 * 2 * FEATURES * QUERIES * SLOTS
@@ -50,14 +48,17 @@ def tile_attend_grope_kernel(tc, q1, q2, G, cs, sn, offs, poffs, out_0, out_1):
         def buffer(tag, columns=SLOTS, dtype=F32):
             return keep.tile([P, columns], dtype, name=tag, tag=tag, align_bytes=64)
 
-        def place(name, start, columns):
-            return placed.tile([P, columns], F32, name=name, offset=start * WORD_BYTES, align_bytes=64)
+        def place(name, start, columns, dtype=F32):
+            return placed.tile([P, columns], dtype, name=name, offset=start * WORD_BYTES, align_bytes=64)
 
         def run_of(tile, start, columns=SLOTS):
             return tile[:, start : start + columns]
 
         def bank(number, shape):
             return psum.tile([P] + shape, F32, name="bank", tag="bank%d" % number)
+
+        def half(u):
+            return slice(u * HALF, (u + 1) * HALF)
 
         token_list = keep.tile([P, SLOTS // BAND], U16, name="token_list")
         position_list = keep.tile([P, SLOTS // BAND], U16, name="position_list")
@@ -66,21 +67,16 @@ def tile_attend_grope_kernel(tc, q1, q2, G, cs, sn, offs, poffs, out_0, out_1):
         cos_table = [buffer("cos_table%d" % block, POSITIONS) for block in range(BLOCKS)]
         sin_table = [buffer("sin_table%d" % block, POSITIONS) for block in range(BLOCKS)]
         identity = keep.tile([P, P], F32, name="identity")
-        g_codes = keep.tile([P, SLOTS], U32, name="g_codes", align_bytes=64)
-        g_scales = keep.tile([P, SLOTS], U8, name="g_scales", align_bytes=64)
+        one = keep.tile([P, 1], F32, name="one")
+        early_q = [buffer("early_q%d" % h, 2 * QUERIES) for h in range(2)]
+        late_q = {block: buffer("late_q%d" % block, 2 * QUERIES) for block in (2, 3)}
 
-        D2A = SLOTS - OVERLAP
-        SIN3 = D2A + HALF - OVERLAP
-        LATE = SLOTS - OVERLAP
-        late = buffer("late", SLOTS + 4 * QUERIES)
-        q_raw = [
-            [buffer("q_raw0_%d" % h, 2 * QUERIES)[:] for h in range(2)],
-            [run_of(late, SLOTS, 4 * QUERIES).rearrange("f (j h r) -> f h j r", j=2, h=2)[:, h] for h in range(2)],
-        ]
+        def load_early_q(h):
+            nc.sync.dma_start(early_q[h][:], (q1, q2)[h][0 : 2 * P, :].rearrange("(p j) r -> p (j r)", j=2))
 
-        def load_q(g, h):
-            q = (q1, q2)[h][g * 2 * P : (g + 1) * 2 * P, :]
-            nc.sync.dma_start(q_raw[g][h], q.rearrange("(p j) r -> p j r" if g else "(p j) r -> p (j r)", j=2))
+        def load_late_q(block):
+            for h in range(2):
+                nc.sync.dma_start(run_of(late_q[block], h * QUERIES, QUERIES), rows((q1, q2)[h], block))
 
         def load_cos(block):
             nc.sync.dma_start(cos_table[block][:], rows(cs, block))
@@ -91,8 +87,8 @@ def tile_attend_grope_kernel(tc, q1, q2, G, cs, sn, offs, poffs, out_0, out_1):
         def load_g(u):
             nc.sync.dma_start(run_of(g_row, u * 2 * SLOTS, 2 * SLOTS), run_of(G.rearrange("(p t) i -> p (t i)", t=PACK), u * 2 * SLOTS, 2 * SLOTS))
 
-        load_q(0, 0)
-        load_q(0, 1)
+        load_early_q(0)
+        load_early_q(1)
         load_g(0)
         load_g(1)
         nc.sync.dma_start(position_list[:], poffs)
@@ -101,9 +97,9 @@ def tile_attend_grope_kernel(tc, q1, q2, G, cs, sn, offs, poffs, out_0, out_1):
         load_cos(1)
         load_sin(1)
         nc.sync.dma_start(token_list[:], offs)
-        load_q(1, 0)
-        load_q(1, 1)
+        load_late_q(2)
         load_cos(2)
+        load_late_q(3)
         load_sin(2)
         load_cos(3)
         load_sin(3)
@@ -112,38 +108,59 @@ def tile_attend_grope_kernel(tc, q1, q2, G, cs, sn, offs, poffs, out_0, out_1):
         windows = [keep.tile([P, TOKENS], F32, name="window%d" % w) for w in range(4)]
         for window in windows:
             nc.vector.memset(window[:].bitcast(I32), 0)
+        nc.vector.memset(one[:], 1.0)
 
-        def round_and_turn_on_scalar(h, j, words, turned):
-            nc.scalar.copy(
-                words.bitcast(BF16).rearrange("f (v p e) -> f v p e", v=2, e=2),
-                q_raw[0][h][:, j * QUERIES : (j + 1) * QUERIES].rearrange("f (p v e) -> f v p e", v=2, e=2),
-            )
-            for v in range(2):
-                nc.tensor.transpose(turned[:, v, :], words[:, v * P : (v + 1) * P], identity[:])
-
-        def round_and_turn_on_gpsimd(j, words, turned):
-            nc.gpsimd.tensor_scalar(words.bitcast(BF16), run_of(late, SLOTS + j * 2 * QUERIES, 2 * QUERIES), 1.0, 0.0, MULT, ADD)
-            for h in range(2):
-                for v in range(2):
-                    nc.tensor.transpose(turned[h][:, v, :], words[:, h * ROW_WORDS + v : (h + 1) * ROW_WORDS : 2], identity[:])
-
-        def copy_two_rows(grouped, turned):
-            nc.vector.tensor_copy(grouped.rearrange("p (n f v) -> p n f v", n=2, v=2), turned[:].rearrange("p n v f -> p n f v"))
-
-        def copy_one_row(grouped, turned):
-            nc.vector.tensor_copy(grouped.rearrange("p (f v) -> p f v", v=2), turned[:].rearrange("p v f -> p f v"))
-
+        GROUPED_Q1 = 4 * SLOTS - OVERLAP
+        G_CODES = GROUPED_Q1 + SLOTS - OVERLAP
+        GROUPED_Q2 = G_CODES + SLOTS
+        early_grouped = [place("grouped_q1", GROUPED_Q1, SLOTS), place("grouped_q2", GROUPED_Q2, SLOTS)]
         q_codes = buffer("q_codes", 2 * BLOCKS * P, U32)
         q_scales = buffer("q_scales", 2 * BLOCKS * P, U8)
 
-        def quantise_q(call, grouped):
-            cols = slice(call * 2 * P, (call + 1) * 2 * P)
+        def quantise_q(run, runs, grouped):
+            cols = slice(run * P, (run + runs) * P)
             nc.vector.quantize_mx(out=q_codes[:, cols].bitcast(E4M3), scales=q_scales[:, cols], in_=grouped.bitcast(BF16))
 
-        def multiply(out, block, h, slots):
+        def q_run(block, h):
             g, j = divmod(block, 2)
-            run = 2 * h + j if g == 0 else BLOCKS + 2 * j + h
-            cols = slice(run * P, (run + 1) * P)
+            return 2 * h + j if g == 0 else BLOCKS + 2 * j + h
+
+        early_turned = [bank(4 + h, [2, 2, P]) for h in range(2)]
+        for h in range(2):
+            for j in range(2):
+                words = buffer("rounded%d_%d" % (h, j), ROW_WORDS)
+                nc.scalar.copy(
+                    words[:].bitcast(BF16).rearrange("f (v p e) -> f v p e", v=2, e=2),
+                    run_of(early_q[h], j * QUERIES, QUERIES).rearrange("f (p v e) -> f v p e", v=2, e=2),
+                )
+                for v in range(2):
+                    nc.tensor.transpose(early_turned[h][:, j, v, :], words[:, v * P : (v + 1) * P], identity[:])
+        for h in range(2):
+            nc.scalar.copy(early_grouped[h][:].rearrange("p (n f v) -> p n f v", n=2, v=2), early_turned[h][:].rearrange("p n v f -> p n f v"))
+
+        second_half = place("second_half", GROUPED_Q2, 3 * SLOTS)
+        g_grouped = [buffer("first_half"), second_half]
+        g_scales = buffer("g_scales", SLOTS, U8)
+
+        def interleave_g(u, lo, hi):
+            nc.vector.tensor_copy(
+                g_grouped[u][:, 2 * lo : 2 * hi].bitcast(BF16).rearrange("p (c i t) -> p c t i", i=4, t=PACK),
+                g_raw[:, u, :, lo:hi].rearrange("p t (c i) -> p c t i", i=4),
+            )
+
+        quantise_q(0, 2, early_grouped[0][:])
+        interleave_g(0, 0, HALF)
+        quantise_q(2, 2, early_grouped[1][:])
+        g_codes = place("g_codes", G_CODES, SLOTS, U32)
+
+        def quantise_g(u, lo, hi):
+            cols = slice(u * HALF + lo, u * HALF + hi)
+            nc.vector.quantize_mx(
+                out=g_codes[:, cols].bitcast(E5M2), scales=g_scales[:, cols], in_=g_grouped[u][:, 2 * lo : 2 * hi].bitcast(BF16)
+            )
+
+        def multiply(out, block, h, slots):
+            cols = slice(q_run(block, h) * P, (q_run(block, h) + 1) * P)
             nc.tensor.matmul_mx(
                 out=out,
                 lhsT=q_codes[:, cols].bitcast(E4M3),
@@ -154,45 +171,12 @@ def tile_attend_grope_kernel(tc, q1, q2, G, cs, sn, offs, poffs, out_0, out_1):
                 stop=True,
             )
 
-        def multiply_block(block):
-            banks = [bank(2 * block + h, [SLOTS]) for h in range(2)]
+        def multiply_block(block, a_bank, b_bank):
+            banks = [bank(a_bank, [SLOTS]), bank(b_bank, [SLOTS])]
             for h in (1, 0):
                 multiply(banks[h][:], block, h, slice(0, SLOTS))
             return banks
 
-        def half(u):
-            return slice(u * HALF, (u + 1) * HALF)
-
-        turned = bank(4, [2, 2, P])
-        for j in range(2):
-            round_and_turn_on_scalar(0, j, buffer("rounded0_%d" % j, ROW_WORDS)[:], turned[:, j])
-        grouped = buffer("grouped0")
-        copy_two_rows(grouped[:], turned)
-        quantise_q(0, grouped[:])
-        grouped = buffer("grouped1")
-        turned = [bank(5 + j, [2, P]) for j in range(2)]
-        round_and_turn_on_scalar(1, 0, buffer("rounded1_0", ROW_WORDS)[:], turned[0])
-        round_and_turn_on_scalar(1, 1, place("last_words", 4 * SLOTS - P, ROW_WORDS)[:], turned[1])
-        for j in range(2):
-            copy_one_row(grouped[:, j * ROW_WORDS : (j + 1) * ROW_WORDS], turned[j])
-        quantise_q(1, grouped[:])
-
-        second_half = place("second_half", 4 * SLOTS, 3 * SLOTS)
-        g_grouped = [place("first_half", 4 * SLOTS, SLOTS), second_half]
-
-        def interleave_g(u, lo, hi):
-            nc.vector.tensor_copy(
-                g_grouped[u][:, 2 * lo : 2 * hi].bitcast(BF16).rearrange("p (c i t) -> p c t i", i=4, t=PACK),
-                g_raw[:, u, :, lo:hi].rearrange("p t (c i) -> p c t i", i=4),
-            )
-
-        def quantise_g(u, lo, hi):
-            cols = slice(u * HALF + lo, u * HALF + hi)
-            nc.vector.quantize_mx(
-                out=g_codes[:, cols].bitcast(E5M2), scales=g_scales[:, cols], in_=g_grouped[u][:, 2 * lo : 2 * hi].bitcast(BF16)
-            )
-
-        interleave_g(0, 0, HALF)
         quantise_g(0, 0, HALF)
         for step in (interleave_g, quantise_g):
             step(1, QUARTER, HALF)
@@ -201,28 +185,26 @@ def tile_attend_grope_kernel(tc, q1, q2, G, cs, sn, offs, poffs, out_0, out_1):
         for u in range(2):
             for h in range(2):
                 multiply(first_sums[u][:, h, :], 0, h, half(u))
-        sums = [None, multiply_block(1)]
+        sums = {1: multiply_block(1, 2, 3)}
 
-        tail = buffer("tail", 2 * SLOTS)
-        early = buffer("early", SIN3 + SLOTS)
-        after_quantiser = buffer("after_quantiser", 2 * SLOTS)
-        around_block2 = buffer("around_block2", 3 * SLOTS)
-        after_d1 = buffer("after_d1", 2 * SLOTS)
         first_angles = place("first_angles", 0, 4 * SLOTS)
-        cos = [run_of(first_angles, 0), run_of(first_angles, 2 * SLOTS), run_of(early, 0), run_of(late, LATE)]
-        sin = [run_of(first_angles, SLOTS), run_of(first_angles, 3 * SLOTS), run_of(early, SIN3), run_of(after_d1, 0)]
         by_cos, by_sin = run_of(second_half, SLOTS - OVERLAP, 2 * SLOTS), buffer("by_sin", 2 * SLOTS)[:]
-        cb = [None, buffer("cb1")[:], run_of(late, 0), buffer("cb3")[:]]
-        sa = [None] + [buffer("sa%d" % block)[:] for block in range(1, BLOCKS)]
-        ca = [None, run_of(after_d1, SLOTS - OVERLAP), buffer("ca2")[:], tail[:, 0:SLOTS]]
-        sb = [None, run_of(around_block2, 0), buffer("sb2")[:], tail[:, SLOTS : 2 * SLOTS]]
-        d1 = [buffer("d1_0")[:], run_of(after_quantiser, OVERLAP), buffer("d1_2")[:]]
-        d2 = [
-            [run_of(early, D2A, HALF), buffer("d2_0", HALF)[:]],
-            [run_of(late, LATE + D2A, HALF), run_of(around_block2, 2 * (SLOTS - OVERLAP), HALF)],
-            [buffer("d2_2", HALF)[:], run_of(tail, SLOTS - QUARTER, HALF)],
-            [buffer("d2_3_%d" % u, HALF)[:] for u in range(2)],
-        ]
+        around_b3 = buffer("around_b3", 2 * SLOTS + ROW_WORDS - 2 * OVERLAP)
+        after_a3 = buffer("after_a3")
+        tail = buffer("tail", 3 * SLOTS - 2 * OVERLAP)
+        cb = {1: buffer("cb1")[:], 2: run_of(around_b3, 0), 3: buffer("cb3")[:]}
+        sa = {block: buffer("sa%d" % block)[:] for block in (1, 2, 3)}
+        ca = {1: buffer("ca1")[:], 2: buffer("ca2")[:], 3: run_of(tail, 0)}
+        sb = {1: buffer("sb1")[:], 2: run_of(around_b3, SLOTS + ROW_WORDS - 2 * OVERLAP), 3: run_of(tail, 2 * SLOTS - 2 * OVERLAP)}
+        cos = [run_of(first_angles, 0), run_of(first_angles, 2 * SLOTS), run_of(by_cos, SLOTS), cb[1]]
+        sin = [run_of(first_angles, SLOTS), run_of(first_angles, 3 * SLOTS), run_of(by_sin, 0), sa[1]]
+        d1 = [buffer("d1_0")[:], after_a3[:], run_of(tail, SLOTS - OVERLAP)]
+        d2 = [buffer("d2_0")[:], run_of(late_q[3], 0), buffer("d2_2")[:], buffer("d2_3")[:]]
+        late_words = {2: run_of(by_cos, 0), 3: run_of(by_sin, SLOTS)}
+        late_grouped = {
+            2: [buffer("grouped2_%d" % h, ROW_WORDS)[:] for h in range(2)],
+            3: [run_of(after_a3, 0, ROW_WORDS), run_of(around_b3, SLOTS - OVERLAP, ROW_WORDS)],
+        }
 
         def entries(listed, u):
             return listed[:, u * HALF // BAND : (u + 1) * HALF // BAND]
@@ -250,38 +232,45 @@ def tile_attend_grope_kernel(tc, q1, q2, G, cs, sn, offs, poffs, out_0, out_1):
                 nc.vector.tensor_tensor(term[block], acc[:], angle[block], MULT)
 
         def form_first_d2(u):
-            nc.gpsimd.tensor_tensor(d2[0][u], run_of(by_cos, SLOTS + u * HALF, HALF), run_of(by_sin, u * HALF, HALF), SUBTRACT)
+            nc.gpsimd.tensor_tensor(d2[0][:, half(u)], run_of(by_cos, SLOTS + u * HALF, HALF), run_of(by_sin, u * HALF, HALF), SUBTRACT)
 
         def form_first_d1(u):
             nc.gpsimd.tensor_tensor(d1[0][:, half(u)], run_of(by_cos, u * HALF, HALF), run_of(by_sin, SLOTS + u * HALF, HALF), ADD)
 
-        def form_d2_half(block, u):
-            nc.gpsimd.tensor_tensor(d2[block][u], cb[block][:, half(u)], sa[block][:, half(u)], SUBTRACT)
-
         def form_d2(block):
-            for u in range(2):
-                form_d2_half(block, u)
+            nc.gpsimd.tensor_tensor(d2[block], cb[block], sa[block], SUBTRACT)
 
         def form_d1(block):
             nc.gpsimd.tensor_tensor(d1[block], ca[block], sb[block], ADD)
 
-        scalar_windows = [windows[w] for w in (0, 2, 1, 2)]
-        vector_windows = [windows[w] for w in (1, 3, 0, 3)]
+        def round_and_turn(block, bank_number):
+            words = late_words[block]
+            turned = bank(bank_number, [2, 2, P])
+            nc.gpsimd.tensor_scalar(words.bitcast(BF16), late_q[block][:], 1.0, 0.0, MULT, ADD)
+            for h in (1, 0):
+                for v in range(2):
+                    nc.tensor.transpose(turned[:, h, v, :], words[:, h * ROW_WORDS + v : (h + 1) * ROW_WORDS : 2], identity[:])
+            return turned
 
-        def put_d2_half(block, u):
-            window = scalar_windows[block]
-            nc.scalar.activation(window[:].indirect(entries(token_list, u)), d2[block][u], COPY)
+        def group_and_quantise(block, turned):
+            for h in (1, 0):
+                nc.vector.tensor_copy(late_grouped[block][h].rearrange("p (f v) -> p f v", v=2), turned[:, h].rearrange("p v f -> p f v"))
+            for h in (1, 0):
+                quantise_q(q_run(block, h), 1, late_grouped[block][h])
 
-        def store_d2(block):
+        scalar_windows = [windows[w] for w in (0, 2, 0, 2)]
+        vector_windows = [windows[w] for w in (1, 3, 1, 3)]
+
+        def put_first_d2(u):
+            nc.scalar.activation(scalar_windows[0][:].indirect(entries(token_list, u)), d2[0][:, half(u)], COPY)
+
+        def put_d2(block):
+            nc.scalar.activation(scalar_windows[block][:].indirect(token_list[:]), d2[block], COPY, scale=one[:])
             nc.sync.dma_start(rows(out_1, block), scalar_windows[block][:])
 
         def put_d1(block):
-            window = vector_windows[block]
-            if block < LAST:
-                nc.vector.tensor_copy(window[:].indirect(token_list[:]), d1[block])
-            else:
-                nc.vector.tensor_tensor(window[:].indirect(token_list[:]), ca[block], sb[block], ADD)
-            nc.sync.dma_start(rows(out_0, block), window[:])
+            nc.vector.tensor_copy(vector_windows[block][:].indirect(token_list[:]), d1[block])
+            nc.sync.dma_start(rows(out_0, block), vector_windows[block][:])
 
         look_up_cos(0)
         for u in range(2):
@@ -294,49 +283,34 @@ def tile_attend_grope_kernel(tc, q1, q2, G, cs, sn, offs, poffs, out_0, out_1):
         form_first_d2(1)
         look_up_cos(1)
         look_up_sin(1)
-        products(1, "cb ca sa")
-        put_d2_half(0, 0)
-        put_d2_half(0, 1)
-        store_d2(0)
+        products(1, "cb ca sa sb")
+        put_first_d2(0)
         look_up_cos(2)
+        put_first_d2(1)
+        nc.sync.dma_start(rows(out_1, 0), scalar_windows[0][:])
         put_d1(0)
 
-        turned_block2 = bank(6, [2, 2, P])
-        round_and_turn_on_gpsimd(0, run_of(by_cos, 0), [turned_block2[:, h] for h in range(2)])
-        turned_block3 = [bank(h, [2, P]) for h in range(2)]
-        round_and_turn_on_gpsimd(1, run_of(by_sin, SLOTS), turned_block3)
-        form_d2_half(1, 0)
-        grouped = run_of(around_block2, SLOTS - OVERLAP)
-        copy_two_rows(grouped, turned_block2)
-        quantise_q(2, grouped)
-        form_d2_half(1, 1)
-        grouped = run_of(after_quantiser, SLOTS)
-        copy_one_row(grouped[:, 0:ROW_WORDS], turned_block3[0])
-        products(1, "sb")
-        copy_one_row(grouped[:, ROW_WORDS:SLOTS], turned_block3[1])
-        quantise_q(3, grouped)
+        turned = {block: round_and_turn(block, block - 2) for block in (2, 3)}
+        form_d2(1)
+        for block in (2, 3):
+            group_and_quantise(block, turned[block])
         form_d1(1)
-        sums.extend(multiply_block(block) for block in (2, 3))
+        sums[2] = multiply_block(2, 1, 4)
+        sums[3] = multiply_block(3, 6, 7)
 
         look_up_sin(2)
-        products(2, "cb sa ca sb")
+        products(2, "cb sb sa ca")
         form_d2(2)
         form_d1(2)
-        put_d2_half(1, 0)
-        put_d2_half(1, 1)
-        store_d2(1)
-        nc.scalar.activation(cos[LAST][:, VECTOR_SHARE:], cos_table[LAST][:].indirect(position_list[:, VECTOR_SHARE // BAND :]), COPY)
+        put_d2(1)
+        look_up_cos(3)
         look_up_sin(3)
         put_d1(1)
-        nc.vector.tensor_copy(cos[LAST][:, :VECTOR_SHARE], cos_table[LAST][:].indirect(position_list[:, : VECTOR_SHARE // BAND]))
         products(3, "sa cb")
         form_d2(3)
-        put_d2_half(2, 0)
-        put_d2_half(2, 1)
-        store_d2(2)
+        put_d2(2)
         put_d1(2)
         products(3, "ca sb")
-        put_d2_half(3, 0)
-        put_d2_half(3, 1)
-        store_d2(3)
-        put_d1(3)
+        put_d2(3)
+        nc.vector.tensor_tensor(vector_windows[3][:].indirect(token_list[:]), ca[3], sb[3], ADD)
+        nc.sync.dma_start(rows(out_0, 3), vector_windows[3][:])

@@ -67,7 +67,6 @@ def tile_attend_grope_kernel(tc, q1, q2, G, cs, sn, offs, poffs, out_0, out_1):
         cos_table = [buffer("cos_table%d" % block, POSITIONS) for block in range(BLOCKS)]
         sin_table = [buffer("sin_table%d" % block, POSITIONS) for block in range(BLOCKS)]
         identity = keep.tile([P, P], F32, name="identity")
-        one = keep.tile([P, 1], F32, name="one")
         early_q = [buffer("early_q%d" % h, 2 * QUERIES) for h in range(2)]
         late_q = {block: buffer("late_q%d" % block, 2 * QUERIES) for block in (2, 3)}
 
@@ -108,18 +107,23 @@ def tile_attend_grope_kernel(tc, q1, q2, G, cs, sn, offs, poffs, out_0, out_1):
         windows = [keep.tile([P, TOKENS], F32, name="window%d" % w) for w in range(4)]
         for window in windows:
             nc.vector.memset(window[:].bitcast(I32), 0)
-        nc.vector.memset(one[:], 1.0)
 
         GROUPED_Q1 = 4 * SLOTS - OVERLAP
         G_CODES = GROUPED_Q1 + SLOTS - OVERLAP
         GROUPED_Q2 = G_CODES + SLOTS
         early_grouped = [place("grouped_q1", GROUPED_Q1, SLOTS), place("grouped_q2", GROUPED_Q2, SLOTS)]
         q_codes = buffer("q_codes", 2 * BLOCKS * P, U32)
-        q_scales = buffer("q_scales", 2 * BLOCKS * P, U8)
+        BY_SIN = GROUPED_Q2 + 3 * SLOTS
+        q_scales = {0: buffer("early_scales", 4 * P, U8)[:], 3: buffer("scales3", 2 * P, U8)[:]}
+
+        def scales_of(run, runs):
+            first = 0 if run < 4 else run // 2
+            start = run if run < 4 else run % 2
+            return q_scales[first][:, start * P : (start + runs) * P]
 
         def quantise_q(run, runs, grouped):
             cols = slice(run * P, (run + runs) * P)
-            nc.vector.quantize_mx(out=q_codes[:, cols].bitcast(E4M3), scales=q_scales[:, cols], in_=grouped.bitcast(BF16))
+            nc.vector.quantize_mx(out=q_codes[:, cols].bitcast(E4M3), scales=scales_of(run, runs), in_=grouped.bitcast(BF16))
 
         def q_run(block, h):
             g, j = divmod(block, 2)
@@ -164,7 +168,7 @@ def tile_attend_grope_kernel(tc, q1, q2, G, cs, sn, offs, poffs, out_0, out_1):
             nc.tensor.matmul_mx(
                 out=out,
                 lhsT=q_codes[:, cols].bitcast(E4M3),
-                lhsT_scale=q_scales[:, cols],
+                lhsT_scale=scales_of(q_run(block, h), 1),
                 rhs=g_codes[:, slots].bitcast(E5M2),
                 rhs_scale=g_scales[:, slots],
                 start=True,
@@ -188,7 +192,7 @@ def tile_attend_grope_kernel(tc, q1, q2, G, cs, sn, offs, poffs, out_0, out_1):
         sums = {1: multiply_block(1, 2, 3)}
 
         first_angles = place("first_angles", 0, 4 * SLOTS)
-        by_cos, by_sin = run_of(second_half, SLOTS - OVERLAP, 2 * SLOTS), buffer("by_sin", 2 * SLOTS)[:]
+        by_cos, by_sin = run_of(second_half, SLOTS - OVERLAP, 2 * SLOTS), place("by_sin", BY_SIN, 2 * SLOTS)[:]
         around_b3 = buffer("around_b3", 2 * SLOTS + ROW_WORDS - 2 * OVERLAP)
         after_a3 = buffer("after_a3")
         tail = buffer("tail", 3 * SLOTS - 2 * OVERLAP)
@@ -197,10 +201,10 @@ def tile_attend_grope_kernel(tc, q1, q2, G, cs, sn, offs, poffs, out_0, out_1):
         ca = {1: buffer("ca1")[:], 2: buffer("ca2")[:], 3: run_of(tail, 0)}
         sb = {1: buffer("sb1")[:], 2: run_of(around_b3, SLOTS + ROW_WORDS - 2 * OVERLAP), 3: run_of(tail, 2 * SLOTS - 2 * OVERLAP)}
         cos = [run_of(first_angles, 0), run_of(first_angles, 2 * SLOTS), run_of(by_cos, SLOTS), cb[1]]
-        sin = [run_of(first_angles, SLOTS), run_of(first_angles, 3 * SLOTS), run_of(by_sin, 0), sa[1]]
+        sin = [run_of(first_angles, SLOTS), run_of(first_angles, 3 * SLOTS), None, sa[1]]
         d1 = [buffer("d1_0")[:], after_a3[:], run_of(tail, SLOTS - OVERLAP)]
         d2 = [buffer("d2_0")[:], run_of(late_q[3], 0), buffer("d2_2")[:], buffer("d2_3")[:]]
-        late_words = {2: run_of(by_cos, 0), 3: run_of(by_sin, SLOTS)}
+        late_words = {2: run_of(by_cos, 0)}
         late_grouped = {
             2: [buffer("grouped2_%d" % h, ROW_WORDS)[:] for h in range(2)],
             3: [run_of(after_a3, 0, ROW_WORDS), run_of(around_b3, SLOTS - OVERLAP, ROW_WORDS)],
@@ -261,12 +265,10 @@ def tile_attend_grope_kernel(tc, q1, q2, G, cs, sn, offs, poffs, out_0, out_1):
         scalar_windows = [windows[w] for w in (0, 2, 0, 2)]
         vector_windows = [windows[w] for w in (1, 3, 1, 3)]
 
-        def put_first_d2(u):
-            nc.scalar.activation(scalar_windows[0][:].indirect(entries(token_list, u)), d2[0][:, half(u)], COPY)
-
-        def put_d2(block):
-            nc.scalar.activation(scalar_windows[block][:].indirect(token_list[:]), d2[block], COPY, scale=one[:])
-            nc.sync.dma_start(rows(out_1, block), scalar_windows[block][:])
+        def put_d2(block, u):
+            nc.scalar.activation(scalar_windows[block][:].indirect(entries(token_list, u)), d2[block][:, half(u)], COPY)
+            if u == 1:
+                nc.sync.dma_start(rows(out_1, block), scalar_windows[block][:])
 
         def put_d1(block):
             nc.vector.tensor_copy(vector_windows[block][:].indirect(token_list[:]), d1[block])
@@ -284,13 +286,15 @@ def tile_attend_grope_kernel(tc, q1, q2, G, cs, sn, offs, poffs, out_0, out_1):
         look_up_cos(1)
         look_up_sin(1)
         products(1, "cb ca sa sb")
-        put_first_d2(0)
+        put_d2(0, 0)
         look_up_cos(2)
-        put_first_d2(1)
-        nc.sync.dma_start(rows(out_1, 0), scalar_windows[0][:])
+        put_d2(0, 1)
         put_d1(0)
 
+        late_words[3] = place("words3", BY_SIN + SLOTS, SLOTS)[:]
         turned = {block: round_and_turn(block, block - 2) for block in (2, 3)}
+        q_scales[2] = place("scales2", BY_SIN + SLOTS, 2 * P, U8)[:]
+        sin[2] = place("sin2", BY_SIN, SLOTS)[:]
         form_d2(1)
         for block in (2, 3):
             group_and_quantise(block, turned[block])
@@ -302,15 +306,18 @@ def tile_attend_grope_kernel(tc, q1, q2, G, cs, sn, offs, poffs, out_0, out_1):
         products(2, "cb sb sa ca")
         form_d2(2)
         form_d1(2)
-        put_d2(1)
+        put_d2(1, 0)
         look_up_cos(3)
+        put_d2(1, 1)
         look_up_sin(3)
         put_d1(1)
         products(3, "sa cb")
         form_d2(3)
-        put_d2(2)
+        put_d2(2, 0)
+        put_d2(2, 1)
         put_d1(2)
         products(3, "ca sb")
-        put_d2(3)
+        put_d2(3, 0)
+        put_d2(3, 1)
         nc.vector.tensor_tensor(vector_windows[3][:].indirect(token_list[:]), ca[3], sb[3], ADD)
         nc.sync.dma_start(rows(out_0, 3), vector_windows[3][:])

@@ -29,6 +29,7 @@ HALF = SLOTS // 2
 QUARTER = SLOTS // 4
 ROW_WORDS = QUERIES // 2
 WORD_BYTES = 4
+VECTOR_SHARE = SLOTS // 4
 OVERLAP = 16
 
 FLOPS = 2 * 2 * FEATURES * QUERIES * SLOTS
@@ -67,6 +68,7 @@ def tile_attend_grope_kernel(tc, q1, q2, G, cs, sn, offs, poffs, out_0, out_1):
         cos_table = [buffer("cos_table%d" % block, POSITIONS) for block in range(BLOCKS)]
         sin_table = [buffer("sin_table%d" % block, POSITIONS) for block in range(BLOCKS)]
         identity = keep.tile([P, P], F32, name="identity")
+        one = keep.tile([P, 1], F32, name="one")
         early_q = [buffer("early_q%d" % h, 2 * QUERIES) for h in range(2)]
         late_q = {block: buffer("late_q%d" % block, 2 * QUERIES) for block in (2, 3)}
 
@@ -107,8 +109,10 @@ def tile_attend_grope_kernel(tc, q1, q2, G, cs, sn, offs, poffs, out_0, out_1):
         windows = [keep.tile([P, TOKENS], F32, name="window%d" % w) for w in range(4)]
         for window in windows:
             nc.vector.memset(window[:].bitcast(I32), 0)
+        nc.vector.memset(one[:], 1.0)
 
-        GROUPED_Q1 = 4 * SLOTS - OVERLAP
+        LAST_WORDS = 4 * SLOTS - OVERLAP
+        GROUPED_Q1 = LAST_WORDS + ROW_WORDS
         G_CODES = GROUPED_Q1 + SLOTS - OVERLAP
         GROUPED_Q2 = G_CODES + SLOTS
         early_grouped = [place("grouped_q1", GROUPED_Q1, SLOTS), place("grouped_q2", GROUPED_Q2, SLOTS)]
@@ -129,18 +133,23 @@ def tile_attend_grope_kernel(tc, q1, q2, G, cs, sn, offs, poffs, out_0, out_1):
             g, j = divmod(block, 2)
             return 2 * h + j if g == 0 else BLOCKS + 2 * j + h
 
-        early_turned = [bank(4 + h, [2, 2, P]) for h in range(2)]
-        for h in range(2):
-            for j in range(2):
-                words = buffer("rounded%d_%d" % (h, j), ROW_WORDS)
-                nc.scalar.copy(
-                    words[:].bitcast(BF16).rearrange("f (v p e) -> f v p e", v=2, e=2),
-                    run_of(early_q[h], j * QUERIES, QUERIES).rearrange("f (p v e) -> f v p e", v=2, e=2),
-                )
-                for v in range(2):
-                    nc.tensor.transpose(early_turned[h][:, j, v, :], words[:, v * P : (v + 1) * P], identity[:])
-        for h in range(2):
-            nc.scalar.copy(early_grouped[h][:].rearrange("p (n f v) -> p n f v", n=2, v=2), early_turned[h][:].rearrange("p n v f -> p n f v"))
+        def round_and_turn_early(h, j, words, turned):
+            nc.scalar.copy(
+                words[:].bitcast(BF16).rearrange("f (v p e) -> f v p e", v=2, e=2),
+                run_of(early_q[h], j * QUERIES, QUERIES).rearrange("f (p v e) -> f v p e", v=2, e=2),
+            )
+            for v in range(2):
+                nc.tensor.transpose(turned[:, v, :], words[:, v * P : (v + 1) * P], identity[:])
+
+        turned_q1 = bank(4, [2, 2, P])
+        turned_q2 = [bank(5 + j, [2, P]) for j in range(2)]
+        for j in range(2):
+            round_and_turn_early(0, j, buffer("rounded0_%d" % j, ROW_WORDS), turned_q1[:, j])
+        round_and_turn_early(1, 0, buffer("rounded1_0", ROW_WORDS), turned_q2[0])
+        round_and_turn_early(1, 1, place("last_words", LAST_WORDS, ROW_WORDS), turned_q2[1])
+        nc.scalar.copy(early_grouped[0][:].rearrange("p (n f v) -> p n f v", n=2, v=2), turned_q1[:].rearrange("p n v f -> p n f v"))
+        for j, copy in enumerate((nc.scalar.copy, nc.vector.tensor_copy)):
+            copy(run_of(early_grouped[1], j * ROW_WORDS, ROW_WORDS).rearrange("p (f v) -> p f v", v=2), turned_q2[j][:].rearrange("p v f -> p f v"))
 
         second_half = place("second_half", GROUPED_Q2, 3 * SLOTS)
         g_grouped = [buffer("first_half"), second_half]
@@ -196,11 +205,12 @@ def tile_attend_grope_kernel(tc, q1, q2, G, cs, sn, offs, poffs, out_0, out_1):
         around_b3 = buffer("around_b3", 2 * SLOTS + ROW_WORDS - 2 * OVERLAP)
         after_a3 = buffer("after_a3")
         tail = buffer("tail", 3 * SLOTS - 2 * OVERLAP)
-        cb = {1: buffer("cb1")[:], 2: run_of(around_b3, 0), 3: buffer("cb3")[:]}
+        b1_terms = buffer("b1_terms", 2 * SLOTS)
+        cb = {1: run_of(b1_terms, SLOTS), 2: run_of(around_b3, 0), 3: buffer("cb3")[:]}
         sa = {block: buffer("sa%d" % block)[:] for block in (1, 2, 3)}
         ca = {1: buffer("ca1")[:], 2: buffer("ca2")[:], 3: run_of(tail, 0)}
-        sb = {1: buffer("sb1")[:], 2: run_of(around_b3, SLOTS + ROW_WORDS - 2 * OVERLAP), 3: run_of(tail, 2 * SLOTS - 2 * OVERLAP)}
-        cos = [run_of(first_angles, 0), run_of(first_angles, 2 * SLOTS), run_of(by_cos, SLOTS), cb[1]]
+        sb = {1: run_of(b1_terms, 0), 2: run_of(around_b3, SLOTS + ROW_WORDS - 2 * OVERLAP), 3: run_of(tail, 2 * SLOTS - 2 * OVERLAP)}
+        cos = [run_of(first_angles, 0), run_of(first_angles, 2 * SLOTS), run_of(by_cos, SLOTS), run_of(b1_terms, SLOTS - VECTOR_SHARE)]
         sin = [run_of(first_angles, SLOTS), run_of(first_angles, 3 * SLOTS), None, sa[1]]
         d1 = [buffer("d1_0")[:], after_a3[:], run_of(tail, SLOTS - OVERLAP)]
         d2 = [buffer("d2_0")[:], run_of(late_q[3], 0), buffer("d2_2")[:], buffer("d2_3")[:]]
@@ -270,6 +280,10 @@ def tile_attend_grope_kernel(tc, q1, q2, G, cs, sn, offs, poffs, out_0, out_1):
             if u == 1:
                 nc.sync.dma_start(rows(out_1, block), scalar_windows[block][:])
 
+        def put_whole_d2(block):
+            nc.scalar.activation(scalar_windows[block][:].indirect(token_list[:]), d2[block], COPY, scale=one[:])
+            nc.sync.dma_start(rows(out_1, block), scalar_windows[block][:])
+
         def put_d1(block):
             nc.vector.tensor_copy(vector_windows[block][:].indirect(token_list[:]), d1[block])
             nc.sync.dma_start(rows(out_0, block), vector_windows[block][:])
@@ -307,17 +321,16 @@ def tile_attend_grope_kernel(tc, q1, q2, G, cs, sn, offs, poffs, out_0, out_1):
         form_d2(2)
         form_d1(2)
         put_d2(1, 0)
-        look_up_cos(3)
+        nc.scalar.activation(cos[3][:, VECTOR_SHARE:], cos_table[3][:].indirect(position_list[:, VECTOR_SHARE // BAND :]), COPY)
         put_d2(1, 1)
         look_up_sin(3)
         put_d1(1)
+        nc.vector.tensor_copy(cos[3][:, :VECTOR_SHARE], cos_table[3][:].indirect(position_list[:, : VECTOR_SHARE // BAND]))
         products(3, "sa cb")
         form_d2(3)
-        put_d2(2, 0)
-        put_d2(2, 1)
+        put_whole_d2(2)
         put_d1(2)
         products(3, "ca sb")
-        put_d2(3, 0)
-        put_d2(3, 1)
+        put_whole_d2(3)
         nc.vector.tensor_tensor(vector_windows[3][:].indirect(token_list[:]), ca[3], sb[3], ADD)
         nc.sync.dma_start(rows(out_0, 3), vector_windows[3][:])

@@ -117,17 +117,11 @@ def tile_attend_grope_kernel(tc, q1, q2, G, cs, sn, offs, poffs, out_0, out_1):
         GROUPED_Q2 = G_CODES + SLOTS
         early_grouped = [place("grouped_q1", GROUPED_Q1, SLOTS), place("grouped_q2", GROUPED_Q2, SLOTS)]
         q_codes = buffer("q_codes", 2 * BLOCKS * P, U32)
-        BY_SIN = GROUPED_Q2 + 3 * SLOTS
-        q_scales = {0: buffer("early_scales", 4 * P, U8)[:], 3: buffer("scales3", 2 * P, U8)[:]}
-
-        def scales_of(run, runs):
-            first = 0 if run < 4 else run // 2
-            start = run if run < 4 else run % 2
-            return q_scales[first][:, start * P : (start + runs) * P]
+        q_scales = buffer("q_scales", 2 * BLOCKS * P, U8)
 
         def quantise_q(run, runs, grouped):
             cols = slice(run * P, (run + runs) * P)
-            nc.vector.quantize_mx(out=q_codes[:, cols].bitcast(E4M3), scales=scales_of(run, runs), in_=grouped.bitcast(BF16))
+            nc.vector.quantize_mx(out=q_codes[:, cols].bitcast(E4M3), scales=q_scales[:, cols], in_=grouped.bitcast(BF16))
 
         def q_run(block, h):
             g, j = divmod(block, 2)
@@ -151,7 +145,7 @@ def tile_attend_grope_kernel(tc, q1, q2, G, cs, sn, offs, poffs, out_0, out_1):
         for j, copy in enumerate((nc.scalar.copy, nc.vector.tensor_copy)):
             copy(run_of(early_grouped[1], j * ROW_WORDS, ROW_WORDS).rearrange("p (f v) -> p f v", v=2), turned_q2[j][:].rearrange("p v f -> p f v"))
 
-        second_half = place("second_half", GROUPED_Q2, 3 * SLOTS)
+        second_half = place("second_half", GROUPED_Q2, 4 * SLOTS)
         g_grouped = [buffer("first_half"), second_half]
         g_scales = buffer("g_scales", SLOTS, U8)
 
@@ -177,7 +171,7 @@ def tile_attend_grope_kernel(tc, q1, q2, G, cs, sn, offs, poffs, out_0, out_1):
             nc.tensor.matmul_mx(
                 out=out,
                 lhsT=q_codes[:, cols].bitcast(E4M3),
-                lhsT_scale=scales_of(q_run(block, h), 1),
+                lhsT_scale=q_scales[:, cols],
                 rhs=g_codes[:, slots].bitcast(E5M2),
                 rhs_scale=g_scales[:, slots],
                 start=True,
@@ -201,7 +195,7 @@ def tile_attend_grope_kernel(tc, q1, q2, G, cs, sn, offs, poffs, out_0, out_1):
         sums = {1: multiply_block(1, 2, 3)}
 
         first_angles = place("first_angles", 0, 4 * SLOTS)
-        by_cos, by_sin = run_of(second_half, SLOTS - OVERLAP, 2 * SLOTS), place("by_sin", BY_SIN, 2 * SLOTS)[:]
+        by_cos, by_sin = run_of(second_half, SLOTS - OVERLAP, 2 * SLOTS), buffer("by_sin", 2 * SLOTS)[:]
         around_b3 = buffer("around_b3", 2 * SLOTS + ROW_WORDS - 2 * OVERLAP)
         after_a3 = buffer("after_a3")
         tail = buffer("tail", 3 * SLOTS - 2 * OVERLAP)
@@ -210,13 +204,13 @@ def tile_attend_grope_kernel(tc, q1, q2, G, cs, sn, offs, poffs, out_0, out_1):
         sa = {block: buffer("sa%d" % block)[:] for block in (1, 2, 3)}
         ca = {1: buffer("ca1")[:], 2: buffer("ca2")[:], 3: run_of(tail, 0)}
         sb = {1: run_of(b1_terms, 0), 2: run_of(around_b3, SLOTS + ROW_WORDS - 2 * OVERLAP), 3: run_of(tail, 2 * SLOTS - 2 * OVERLAP)}
-        cos = [run_of(first_angles, 0), run_of(first_angles, 2 * SLOTS), run_of(by_cos, SLOTS), run_of(b1_terms, SLOTS - VECTOR_SHARE)]
-        sin = [run_of(first_angles, SLOTS), run_of(first_angles, 3 * SLOTS), None, sa[1]]
-        d1 = [buffer("d1_0")[:], after_a3[:], run_of(tail, SLOTS - OVERLAP)]
-        d2 = [buffer("d2_0")[:], run_of(late_q[3], 0), buffer("d2_2")[:], buffer("d2_3")[:]]
-        late_words = {2: run_of(by_cos, 0)}
+        cos = [run_of(first_angles, 0), run_of(first_angles, 2 * SLOTS), run_of(second_half, 3 * SLOTS - OVERLAP - HALF), run_of(b1_terms, SLOTS - VECTOR_SHARE)]
+        sin = [run_of(first_angles, SLOTS), run_of(first_angles, 3 * SLOTS), run_of(by_sin, 0), sa[1]]
+        d1 = [buffer("d1_0")[:], after_a3[:], buffer("d1_2")[:]]
+        d2 = [run_of(second_half, 3 * SLOTS - OVERLAP), run_of(late_q[3], 0), run_of(tail, SLOTS - OVERLAP), buffer("d2_3")[:]]
+        late_words = {2: run_of(by_cos, 0), 3: run_of(by_sin, SLOTS)}
         late_grouped = {
-            2: [buffer("grouped2_%d" % h, ROW_WORDS)[:] for h in range(2)],
+            2: [run_of(late_q[3], SLOTS + h * ROW_WORDS, ROW_WORDS) for h in range(2)],
             3: [run_of(after_a3, 0, ROW_WORDS), run_of(around_b3, SLOTS - OVERLAP, ROW_WORDS)],
         }
 
@@ -272,8 +266,8 @@ def tile_attend_grope_kernel(tc, q1, q2, G, cs, sn, offs, poffs, out_0, out_1):
             for h in (1, 0):
                 quantise_q(q_run(block, h), 1, late_grouped[block][h])
 
-        scalar_windows = [windows[w] for w in (0, 2, 0, 2)]
-        vector_windows = [windows[w] for w in (1, 3, 1, 3)]
+        scalar_windows = [windows[w] for w in (0, 2, 1, 2)]
+        vector_windows = [windows[w] for w in (1, 3, 0, 3)]
 
         def put_d2(block, u):
             nc.scalar.activation(scalar_windows[block][:].indirect(entries(token_list, u)), d2[block][:, half(u)], COPY)
@@ -300,15 +294,12 @@ def tile_attend_grope_kernel(tc, q1, q2, G, cs, sn, offs, poffs, out_0, out_1):
         look_up_cos(1)
         look_up_sin(1)
         products(1, "cb ca sa sb")
-        put_d2(0, 0)
-        look_up_cos(2)
-        put_d2(0, 1)
+        for u in range(2):
+            put_d2(0, u)
+            nc.scalar.activation(cos[2][:, half(u)], cos_table[2][:].indirect(entries(position_list, u)), COPY)
         put_d1(0)
 
-        late_words[3] = place("words3", BY_SIN + SLOTS, SLOTS)[:]
         turned = {block: round_and_turn(block, block - 2) for block in (2, 3)}
-        q_scales[2] = place("scales2", BY_SIN + SLOTS, 2 * P, U8)[:]
-        sin[2] = place("sin2", BY_SIN, SLOTS)[:]
         form_d2(1)
         for block in (2, 3):
             group_and_quantise(block, turned[block])
@@ -320,9 +311,8 @@ def tile_attend_grope_kernel(tc, q1, q2, G, cs, sn, offs, poffs, out_0, out_1):
         products(2, "cb sb sa ca")
         form_d2(2)
         form_d1(2)
-        put_d2(1, 0)
+        put_whole_d2(1)
         nc.scalar.activation(cos[3][:, VECTOR_SHARE:], cos_table[3][:].indirect(position_list[:, VECTOR_SHARE // BAND :]), COPY)
-        put_d2(1, 1)
         look_up_sin(3)
         put_d1(1)
         nc.vector.tensor_copy(cos[3][:, :VECTOR_SHARE], cos_table[3][:].indirect(position_list[:, : VECTOR_SHARE // BAND]))

@@ -29,7 +29,7 @@ HALF = SLOTS // 2
 QUARTER = SLOTS // 4
 ROW_WORDS = QUERIES // 2
 WORD_BYTES = 4
-VECTOR_SHARE = SLOTS // 4
+VECTOR_SHARE = SLOTS // 8
 OVERLAP = 16
 
 FLOPS = 2 * 2 * FEATURES * QUERIES * SLOTS
@@ -69,15 +69,14 @@ def tile_attend_grope_kernel(tc, q1, q2, G, cs, sn, offs, poffs, out_0, out_1):
         sin_table = [buffer("sin_table%d" % block, POSITIONS) for block in range(BLOCKS)]
         identity = keep.tile([P, P], F32, name="identity")
         one = keep.tile([P, 1], F32, name="one")
-        early_q = [buffer("early_q%d" % h, 2 * QUERIES) for h in range(2)]
-        late_q = {block: buffer("late_q%d" % block, 2 * QUERIES) for block in (2, 3)}
+        early_q = [buffer("early_q%d" % h, 2 * QUERIES)[:] for h in range(2)]
+        LATE_Q1 = SLOTS - OVERLAP
+        late_row = buffer("late_row", LATE_Q1 + 2 * QUERIES)
+        late_q = [run_of(late_row, LATE_Q1, 2 * QUERIES), buffer("late_q2", 2 * QUERIES)[:]]
 
-        def load_early_q(h):
-            nc.sync.dma_start(early_q[h][:], (q1, q2)[h][0 : 2 * P, :].rearrange("(p j) r -> p (j r)", j=2))
-
-        def load_late_q(block):
-            for h in range(2):
-                nc.sync.dma_start(run_of(late_q[block], h * QUERIES, QUERIES), rows((q1, q2)[h], block))
+        def load_q(g, h):
+            q = (q1, q2)[h][g * 2 * P : (g + 1) * 2 * P, :]
+            nc.sync.dma_start((early_q, late_q)[g][h], q.rearrange("(p j) r -> p (j r)", j=2))
 
         def load_cos(block):
             nc.sync.dma_start(cos_table[block][:], rows(cs, block))
@@ -88,19 +87,19 @@ def tile_attend_grope_kernel(tc, q1, q2, G, cs, sn, offs, poffs, out_0, out_1):
         def load_g(u):
             nc.sync.dma_start(run_of(g_row, u * 2 * SLOTS, 2 * SLOTS), run_of(G.rearrange("(p t) i -> p (t i)", t=PACK), u * 2 * SLOTS, 2 * SLOTS))
 
-        load_early_q(0)
-        load_early_q(1)
+        nc.sync.dma_start(position_list[:], poffs)
+        load_q(0, 0)
+        load_q(0, 1)
         load_g(0)
         load_g(1)
-        nc.sync.dma_start(position_list[:], poffs)
         load_cos(0)
         load_sin(0)
         load_cos(1)
         load_sin(1)
         nc.sync.dma_start(token_list[:], offs)
-        load_late_q(2)
+        load_q(1, 1)
         load_cos(2)
-        load_late_q(3)
+        load_q(1, 0)
         load_sin(2)
         load_cos(3)
         load_sin(3)
@@ -196,22 +195,22 @@ def tile_attend_grope_kernel(tc, q1, q2, G, cs, sn, offs, poffs, out_0, out_1):
 
         first_angles = place("first_angles", 0, 4 * SLOTS)
         by_cos, by_sin = run_of(second_half, SLOTS - OVERLAP, 2 * SLOTS), buffer("by_sin", 2 * SLOTS)[:]
-        around_b3 = buffer("around_b3", 2 * SLOTS + ROW_WORDS - 2 * OVERLAP)
+        around_a2 = buffer("around_a2", 2 * SLOTS + ROW_WORDS - 2 * OVERLAP)
         after_a3 = buffer("after_a3")
         tail = buffer("tail", 3 * SLOTS - 2 * OVERLAP)
         b1_terms = buffer("b1_terms", 2 * SLOTS)
-        cb = {1: run_of(b1_terms, SLOTS), 2: run_of(around_b3, 0), 3: buffer("cb3")[:]}
+        cb = {1: run_of(b1_terms, SLOTS), 2: run_of(around_a2, 0), 3: buffer("cb3")[:]}
         sa = {block: buffer("sa%d" % block)[:] for block in (1, 2, 3)}
         ca = {1: buffer("ca1")[:], 2: buffer("ca2")[:], 3: run_of(tail, 0)}
-        sb = {1: run_of(b1_terms, 0), 2: run_of(around_b3, SLOTS + ROW_WORDS - 2 * OVERLAP), 3: run_of(tail, 2 * SLOTS - 2 * OVERLAP)}
+        sb = {1: run_of(b1_terms, 0), 2: run_of(around_a2, SLOTS + ROW_WORDS - 2 * OVERLAP), 3: run_of(tail, 2 * SLOTS - 2 * OVERLAP)}
         cos = [run_of(first_angles, 0), run_of(first_angles, 2 * SLOTS), run_of(second_half, 3 * SLOTS - OVERLAP - HALF), run_of(b1_terms, SLOTS - VECTOR_SHARE)]
         sin = [run_of(first_angles, SLOTS), run_of(first_angles, 3 * SLOTS), run_of(by_sin, 0), sa[1]]
         d1 = [buffer("d1_0")[:], after_a3[:], buffer("d1_2")[:]]
-        d2 = [run_of(second_half, 3 * SLOTS - OVERLAP), run_of(late_q[3], 0), run_of(tail, SLOTS - OVERLAP), buffer("d2_3")[:]]
-        late_words = {2: run_of(by_cos, 0), 3: run_of(by_sin, SLOTS)}
+        d2 = [run_of(second_half, 3 * SLOTS - OVERLAP), run_of(late_row, 0), run_of(tail, SLOTS - OVERLAP), buffer("d2_3")[:]]
+        late_words = [run_of(by_sin, SLOTS), run_of(by_cos, 0)]
         late_grouped = {
-            2: [run_of(late_q[3], SLOTS + h * ROW_WORDS, ROW_WORDS) for h in range(2)],
-            3: [run_of(after_a3, 0, ROW_WORDS), run_of(around_b3, SLOTS - OVERLAP, ROW_WORDS)],
+            2: [run_of(around_a2, SLOTS - OVERLAP, ROW_WORDS), run_of(late_row, SLOTS, ROW_WORDS)],
+            3: [run_of(after_a3, 0, ROW_WORDS), run_of(late_row, SLOTS + ROW_WORDS, ROW_WORDS)],
         }
 
         def entries(listed, u):
@@ -251,20 +250,18 @@ def tile_attend_grope_kernel(tc, q1, q2, G, cs, sn, offs, poffs, out_0, out_1):
         def form_d1(block):
             nc.gpsimd.tensor_tensor(d1[block], ca[block], sb[block], ADD)
 
-        def round_and_turn(block, bank_number):
-            words = late_words[block]
-            turned = bank(bank_number, [2, 2, P])
-            nc.gpsimd.tensor_scalar(words.bitcast(BF16), late_q[block][:], 1.0, 0.0, MULT, ADD)
-            for h in (1, 0):
+        def round_and_turn_late(h, turned):
+            words = late_words[h]
+            nc.gpsimd.tensor_scalar(words.bitcast(BF16), late_q[h], 1.0, 0.0, MULT, ADD)
+            for j in range(2):
                 for v in range(2):
-                    nc.tensor.transpose(turned[:, h, v, :], words[:, h * ROW_WORDS + v : (h + 1) * ROW_WORDS : 2], identity[:])
-            return turned
+                    nc.tensor.transpose(turned[2 + j][h][:, v, :], words[:, j * ROW_WORDS + v : (j + 1) * ROW_WORDS : 2], identity[:])
 
-        def group_and_quantise(block, turned):
-            for h in (1, 0):
-                nc.vector.tensor_copy(late_grouped[block][h].rearrange("p (f v) -> p f v", v=2), turned[:, h].rearrange("p v f -> p f v"))
-            for h in (1, 0):
-                quantise_q(q_run(block, h), 1, late_grouped[block][h])
+        def group_late(block, h):
+            nc.vector.tensor_copy(late_grouped[block][h].rearrange("p (f v) -> p f v", v=2), turned[block][h].rearrange("p v f -> p f v"))
+
+        def quantise_late(block, h):
+            quantise_q(q_run(block, h), 1, late_grouped[block][h])
 
         scalar_windows = [windows[w] for w in (0, 2, 1, 2)]
         vector_windows = [windows[w] for w in (1, 3, 0, 3)]
@@ -299,12 +296,19 @@ def tile_attend_grope_kernel(tc, q1, q2, G, cs, sn, offs, poffs, out_0, out_1):
             nc.scalar.activation(cos[2][:, half(u)], cos_table[2][:].indirect(entries(position_list, u)), COPY)
         put_d1(0)
 
-        turned = {block: round_and_turn(block, block - 2) for block in (2, 3)}
+        turned_late_q2 = bank(0, [2, 2, P])
+        turned = {2: [bank(1, [2, P])[:], turned_late_q2[:, 0]], 3: [bank(5, [2, P])[:], turned_late_q2[:, 1]]}
+        for h in (1, 0):
+            round_and_turn_late(h, turned)
         form_d2(1)
-        for block in (2, 3):
-            group_and_quantise(block, turned[block])
+        late_rows = [(2, 1), (3, 1), (2, 0), (3, 0)]
+        group_late(*late_rows[0])
+        for ahead, row in zip(late_rows[1:], late_rows):
+            group_late(*ahead)
+            quantise_late(*row)
+        quantise_late(*late_rows[-1])
         form_d1(1)
-        sums[2] = multiply_block(2, 1, 4)
+        sums[2] = multiply_block(2, 5, 4)
         sums[3] = multiply_block(3, 6, 7)
 
         look_up_sin(2)

from contextlib import ExitStack

import concourse.mybir as mybir
from concourse.masks import make_identity

F32 = mybir.dt.float32
BF16 = mybir.dt.bfloat16
U32 = mybir.dt.uint32
I32 = mybir.dt.int32
U16 = mybir.dt.uint16
U8 = mybir.dt.uint8
E4M3 = mybir.dt.float8_e4m3fn_x4
E5M2 = mybir.dt.float8_e5m2_x4
MULT = mybir.AluOpType.mult
ADD = mybir.AluOpType.add
SUBTRACT = mybir.AluOpType.subtract
COPY = mybir.ActivationFunctionType.Copy

P = 128
PACK = 4
FEATURES = 512
QUERIES = 512
SLOTS = 512
POSITIONS = 1024
TOKENS = 2048
BLOCKS = FEATURES // P
BAND = 16
HALF = SLOTS // 2
QUARTER = SLOTS // 4
ROW_WORDS = QUERIES // 2
WORD_BYTES = 4
VECTOR_SHARE = SLOTS // 8
OVERLAP = 16

FLOPS = 2 * 2 * FEATURES * QUERIES * SLOTS


def tile_attend_grope_kernel(tc, q1, q2, G, cs, sn, offs, poffs, out_0, out_1):
    nc = tc.nc
    with ExitStack() as ctx:
        keep = ctx.enter_context(tc.tile_pool(name="keep", bufs=1))
        placed = ctx.enter_context(tc.tile_pool(name="placed", bufs=1))
        psum = ctx.enter_context(tc.psum_pool(name="psum", bufs=1))

        def rows(x, block):
            g, j = divmod(block, 2)
            return x[g * 2 * P : (g + 1) * 2 * P, :].rearrange("(p j) n -> p j n", j=2)[:, j, :]

        def buffer(tag, columns=SLOTS, dtype=F32):
            return keep.tile([P, columns], dtype, name=tag, tag=tag, align_bytes=64)

        def place(name, start, columns, dtype=F32):
            return placed.tile([P, columns], dtype, name=name, offset=start * WORD_BYTES, align_bytes=64)

        def run_of(tile, start, columns=SLOTS):
            return tile[:, start : start + columns]

        def bank(number, shape):
            return psum.tile([P] + shape, F32, name="bank", tag="bank%d" % number)

        def half(u):
            return slice(u * HALF, (u + 1) * HALF)

        token_list = keep.tile([P, SLOTS // BAND], U16, name="token_list")
        position_list = keep.tile([P, SLOTS // BAND], U16, name="position_list")
        g_row = buffer("g_row", PACK * SLOTS)
        g_raw = g_row[:].rearrange("p (t u i) -> p u t i", t=PACK, u=2)
        cos_table = [buffer("cos_table%d" % block, POSITIONS) for block in range(BLOCKS)]
        sin_table = [buffer("sin_table%d" % block, POSITIONS) for block in range(BLOCKS)]
        identity = keep.tile([P, P], F32, name="identity")
        one = keep.tile([P, 1], F32, name="one")
        early_q = [buffer("early_q%d" % h, 2 * QUERIES)[:] for h in range(2)]
        LATE_Q1 = SLOTS - OVERLAP
        late_row = buffer("late_row", LATE_Q1 + 2 * QUERIES)
        late_q = [run_of(late_row, LATE_Q1, 2 * QUERIES), buffer("late_q2", 2 * QUERIES)[:]]

        def load_q(g, h):
            q = (q1, q2)[h][g * 2 * P : (g + 1) * 2 * P, :]
            nc.sync.dma_start((early_q, late_q)[g][h], q.rearrange("(p j) r -> p (j r)", j=2))

        def load_cos(block):
            nc.sync.dma_start(cos_table[block][:], rows(cs, block))

        def load_sin(block):
            nc.sync.dma_start(sin_table[block][:], rows(sn, block))

        def load_g(u):
            nc.sync.dma_start(run_of(g_row, u * 2 * SLOTS, 2 * SLOTS), run_of(G.rearrange("(p t) i -> p (t i)", t=PACK), u * 2 * SLOTS, 2 * SLOTS))

        nc.sync.dma_start(position_list[:], poffs)
        load_q(0, 0)
        load_q(0, 1)
        load_g(0)
        load_g(1)
        load_cos(0)
        load_sin(0)
        load_cos(1)
        load_sin(1)
        nc.sync.dma_start(token_list[:], offs)
        load_q(1, 1)
        load_cos(2)
        load_q(1, 0)
        load_sin(2)
        load_cos(3)
        load_sin(3)

        make_identity(nc, identity[:])
        windows = [keep.tile([P, TOKENS], F32, name="window%d" % w) for w in range(4)]
        for window in windows:
            nc.vector.memset(window[:].bitcast(I32), 0)
        nc.vector.memset(one[:], 1.0)

        LAST_WORDS = 4 * SLOTS - OVERLAP
        GROUPED_Q1 = LAST_WORDS + ROW_WORDS
        G_CODES = GROUPED_Q1 + SLOTS - OVERLAP
        GROUPED_Q2 = G_CODES + SLOTS
        early_grouped = [place("grouped_q1", GROUPED_Q1, SLOTS), place("grouped_q2", GROUPED_Q2, SLOTS)]
        q_codes = buffer("q_codes", 2 * BLOCKS * P, U32)
        q_scales = buffer("q_scales", 2 * BLOCKS * P, U8)

        def quantise_q(run, runs, grouped):
            cols = slice(run * P, (run + runs) * P)
            nc.vector.quantize_mx(out=q_codes[:, cols].bitcast(E4M3), scales=q_scales[:, cols], in_=grouped.bitcast(BF16))

        def q_run(block, h):
            g, j = divmod(block, 2)
            return 2 * h + j if g == 0 else BLOCKS + 2 * j + h

        def round_and_turn_early(h, j, words, turned):
            nc.scalar.copy(
                words[:].bitcast(BF16).rearrange("f (v p e) -> f v p e", v=2, e=2),
                run_of(early_q[h], j * QUERIES, QUERIES).rearrange("f (p v e) -> f v p e", v=2, e=2),
            )
            for v in range(2):
                nc.tensor.transpose(turned[:, v, :], words[:, v * P : (v + 1) * P], identity[:])

        turned_q1 = bank(4, [2, 2, P])
        turned_q2 = [bank(5 + j, [2, P]) for j in range(2)]
        for j in range(2):
            round_and_turn_early(0, j, buffer("rounded0_%d" % j, ROW_WORDS), turned_q1[:, j])
        round_and_turn_early(1, 0, buffer("rounded1_0", ROW_WORDS), turned_q2[0])
        round_and_turn_early(1, 1, place("last_words", LAST_WORDS, ROW_WORDS), turned_q2[1])
        nc.scalar.copy(early_grouped[0][:].rearrange("p (n f v) -> p n f v", n=2, v=2), turned_q1[:].rearrange("p n v f -> p n f v"))
        for j, copy in enumerate((nc.scalar.copy, nc.vector.tensor_copy)):
            copy(run_of(early_grouped[1], j * ROW_WORDS, ROW_WORDS).rearrange("p (f v) -> p f v", v=2), turned_q2[j][:].rearrange("p v f -> p f v"))

        second_half = place("second_half", GROUPED_Q2, 4 * SLOTS)
        g_grouped = [buffer("first_half"), second_half]
        g_scales = buffer("g_scales", SLOTS, U8)

        def interleave_g(u, lo, hi):
            nc.vector.tensor_copy(
                g_grouped[u][:, 2 * lo : 2 * hi].bitcast(BF16).rearrange("p (c i t) -> p c t i", i=4, t=PACK),
                g_raw[:, u, :, lo:hi].rearrange("p t (c i) -> p c t i", i=4),
            )

        quantise_q(0, 2, early_grouped[0][:])
        interleave_g(0, 0, HALF)
        quantise_q(2, 2, early_grouped[1][:])
        g_codes = place("g_codes", G_CODES, SLOTS, U32)

        def quantise_g(u, lo, hi):
            cols = slice(u * HALF + lo, u * HALF + hi)
            nc.vector.quantize_mx(
                out=g_codes[:, cols].bitcast(E5M2), scales=g_scales[:, cols], in_=g_grouped[u][:, 2 * lo : 2 * hi].bitcast(BF16)
            )

        def multiply(out, block, h, slots):
            cols = slice(q_run(block, h) * P, (q_run(block, h) + 1) * P)
            nc.tensor.matmul_mx(
                out=out,
                lhsT=q_codes[:, cols].bitcast(E4M3),
                lhsT_scale=q_scales[:, cols],
                rhs=g_codes[:, slots].bitcast(E5M2),
                rhs_scale=g_scales[:, slots],
                start=True,
                stop=True,
            )

        def multiply_block(block, a_bank, b_bank):
            banks = [bank(a_bank, [SLOTS]), bank(b_bank, [SLOTS])]
            for h in (1, 0):
                multiply(banks[h][:], block, h, slice(0, SLOTS))
            return banks

        quantise_g(0, 0, HALF)
        for step in (interleave_g, quantise_g):
            step(1, QUARTER, HALF)
            step(1, 0, QUARTER)
        first_sums = [bank(u, [2, HALF]) for u in range(2)]
        for u in range(2):
            for h in range(2):
                multiply(first_sums[u][:, h, :], 0, h, half(u))
        sums = {1: multiply_block(1, 2, 3)}

        first_angles = place("first_angles", 0, 4 * SLOTS)
        by_cos, by_sin = run_of(second_half, SLOTS - OVERLAP, 2 * SLOTS), buffer("by_sin", 2 * SLOTS)[:]
        around_a2 = buffer("around_a2", 2 * SLOTS + ROW_WORDS - 2 * OVERLAP)
        after_a3 = buffer("after_a3")
        tail = buffer("tail", 3 * SLOTS - 2 * OVERLAP)
        b1_terms = buffer("b1_terms", 2 * SLOTS)
        cb = {1: run_of(b1_terms, SLOTS), 2: run_of(around_a2, 0), 3: buffer("cb3")[:]}
        sa = {block: buffer("sa%d" % block)[:] for block in (1, 2, 3)}
        ca = {1: buffer("ca1")[:], 2: buffer("ca2")[:], 3: run_of(tail, 0)}
        sb = {1: run_of(b1_terms, 0), 2: run_of(around_a2, SLOTS + ROW_WORDS - 2 * OVERLAP), 3: run_of(tail, 2 * SLOTS - 2 * OVERLAP)}
        cos = [run_of(first_angles, 0), run_of(first_angles, 2 * SLOTS), run_of(second_half, 3 * SLOTS - OVERLAP - HALF), run_of(b1_terms, SLOTS - VECTOR_SHARE)]
        sin = [run_of(first_angles, SLOTS), run_of(first_angles, 3 * SLOTS), run_of(by_sin, 0), sa[1]]
        d1 = [buffer("d1_0")[:], after_a3[:], buffer("d1_2")[:]]
        d2 = [run_of(second_half, 3 * SLOTS - OVERLAP), run_of(late_row, 0), run_of(tail, SLOTS - OVERLAP), buffer("d2_3")[:]]
        late_words = [run_of(by_sin, SLOTS), run_of(by_cos, 0)]
        late_grouped = {
            2: [run_of(around_a2, SLOTS - OVERLAP, ROW_WORDS), run_of(late_row, SLOTS, ROW_WORDS)],
            3: [run_of(after_a3, 0, ROW_WORDS), run_of(late_row, SLOTS + ROW_WORDS, ROW_WORDS)],
        }

        def entries(listed, u):
            return listed[:, u * HALF // BAND : (u + 1) * HALF // BAND]

        def look_up_cos(block):
            nc.scalar.activation(cos[block], cos_table[block][:].indirect(position_list[:]), COPY)

        def look_up_sin(block):
            nc.scalar.activation(sin[block], sin_table[block][:].indirect(position_list[:]), COPY)

        def first_products(u):
            for terms, angle in ((by_cos, cos[0]), (by_sin, sin[0])):
                nc.vector.tensor_tensor(
                    terms.rearrange("p (h u n) -> p u h n", u=2, h=2)[:, u],
                    first_sums[u][:],
                    angle[:, half(u)].unsqueeze(1).to_broadcast([P, 2, HALF]),
                    MULT,
                )

        def products(block, names):
            a_sum, b_sum = sums[block]
            steps = {"ca": (ca, a_sum, cos), "cb": (cb, b_sum, cos), "sa": (sa, a_sum, sin), "sb": (sb, b_sum, sin)}
            for name in names.split():
                term, acc, angle = steps[name]
                nc.vector.tensor_tensor(term[block], acc[:], angle[block], MULT)

        def form_first_d2(u):
            nc.gpsimd.tensor_tensor(d2[0][:, half(u)], run_of(by_cos, SLOTS + u * HALF, HALF), run_of(by_sin, u * HALF, HALF), SUBTRACT)

        def form_first_d1(u):
            nc.gpsimd.tensor_tensor(d1[0][:, half(u)], run_of(by_cos, u * HALF, HALF), run_of(by_sin, SLOTS + u * HALF, HALF), ADD)

        def form_d2(block):
            nc.gpsimd.tensor_tensor(d2[block], cb[block], sa[block], SUBTRACT)

        def form_d1(block):
            nc.gpsimd.tensor_tensor(d1[block], ca[block], sb[block], ADD)

        def round_and_turn_late(h, turned):
            words = late_words[h]
            nc.gpsimd.tensor_scalar(words.bitcast(BF16), late_q[h], 1.0, 0.0, MULT, ADD)
            for j in range(2):
                for v in range(2):
                    nc.tensor.transpose(turned[2 + j][h][:, v, :], words[:, j * ROW_WORDS + v : (j + 1) * ROW_WORDS : 2], identity[:])

        def group_late(block, h):
            nc.vector.tensor_copy(late_grouped[block][h].rearrange("p (f v) -> p f v", v=2), turned[block][h].rearrange("p v f -> p f v"))

        def quantise_late(block, h):
            quantise_q(q_run(block, h), 1, late_grouped[block][h])

        scalar_windows = [windows[w] for w in (0, 2, 1, 2)]
        vector_windows = [windows[w] for w in (1, 3, 0, 3)]

        def put_d2(block, u):
            nc.scalar.activation(scalar_windows[block][:].indirect(entries(token_list, u)), d2[block][:, half(u)], COPY)
            if u == 1:
                nc.sync.dma_start(rows(out_1, block), scalar_windows[block][:])

        def put_whole_d2(block):
            nc.scalar.activation(scalar_windows[block][:].indirect(token_list[:]), d2[block], COPY, scale=one[:])
            nc.sync.dma_start(rows(out_1, block), scalar_windows[block][:])

        def put_d1(block):
            nc.vector.tensor_copy(vector_windows[block][:].indirect(token_list[:]), d1[block])
            nc.sync.dma_start(rows(out_0, block), vector_windows[block][:])

        look_up_cos(0)
        for u in range(2):
            nc.scalar.activation(sin[0][:, half(u)], sin_table[0][:].indirect(entries(position_list, u)), COPY)
        first_products(0)
        form_first_d2(0)
        form_first_d1(0)
        first_products(1)
        form_first_d1(1)
        form_first_d2(1)
        look_up_cos(1)
        look_up_sin(1)
        products(1, "cb ca sa sb")
        for u in range(2):
            put_d2(0, u)
            nc.scalar.activation(cos[2][:, half(u)], cos_table[2][:].indirect(entries(position_list, u)), COPY)
        put_d1(0)

        turned_late_q2 = bank(0, [2, 2, P])
        turned = {2: [bank(1, [2, P])[:], turned_late_q2[:, 0]], 3: [bank(5, [2, P])[:], turned_late_q2[:, 1]]}
        for h in (1, 0):
            round_and_turn_late(h, turned)
        form_d2(1)
        late_rows = [(2, 1), (3, 1), (2, 0), (3, 0)]
        group_late(*late_rows[0])
        for ahead, row in zip(late_rows[1:], late_rows):
            group_late(*ahead)
            quantise_late(*row)
        quantise_late(*late_rows[-1])
        form_d1(1)
        sums[2] = multiply_block(2, 5, 4)
        sums[3] = multiply_block(3, 6, 7)

        look_up_sin(2)
        products(2, "cb sb sa ca")
        form_d2(2)
        form_d1(2)
        put_whole_d2(1)
        nc.scalar.activation(cos[3][:, VECTOR_SHARE:], cos_table[3][:].indirect(position_list[:, VECTOR_SHARE // BAND :]), COPY)
        look_up_sin(3)
        put_d1(1)
        nc.vector.tensor_copy(cos[3][:, :VECTOR_SHARE], cos_table[3][:].indirect(position_list[:, : VECTOR_SHARE // BAND]))
        products(3, "sa cb")
        form_d2(3)
        put_whole_d2(2)
        put_d1(2)
        products(3, "ca sb")
        put_whole_d2(3)
        nc.vector.tensor_tensor(vector_windows[3][:].indirect(token_list[:]), ca[3], sb[3], ADD)
        nc.sync.dma_start(rows(out_0, 3), vector_windows[3][:])
